import numpy as np
import ml_dtypes


def mxq(x, axis, fmt="e4m3"):
    dtype, down = {"e4m3": (ml_dtypes.float8_e4m3fn, 7), "e5m2": (ml_dtypes.float8_e5m2, 14)}[fmt]
    v = np.moveaxis(np.asarray(x, np.float32).astype(ml_dtypes.bfloat16).astype(np.float64), axis, -1)
    blocks = v.reshape(v.shape[:-1] + (-1, 32))
    amax = np.abs(blocks).max(-1, keepdims=True)
    byte = np.maximum(np.where(amax > 0, np.frexp(amax)[1] - 1 + 127, 0) - down, 1)
    scale = np.exp2(byte - 127.0)
    codes = (blocks / scale).astype(np.float32).astype(dtype).astype(np.float64)
    return np.moveaxis((codes * scale).reshape(v.shape), -1, axis)


WIDE = False


def mx_kscale(k):
    if not WIDE:
        return np.ones(k)
    levels = np.array([10, -10, 5, -5, 0])
    if k % 512:
        return np.exp2(np.random.permutation(np.resize(levels, k // 32))).repeat(32)
    a = np.empty((k // 512, 16))
    for p in range(k // 512):
        a[p, :8] = np.random.permutation(np.resize(levels, 8))
        for g in range(8):
            far = levels[np.abs(levels - a[p, g]) >= 10]
            a[p, g + 8] = far[np.random.randint(len(far))]
    return np.exp2(a.ravel()).repeat(32)


def f64(x):
    return np.asarray(x).astype(np.float64)


def striped(idx):
    return np.tile(idx.reshape(-1, 16).T, (8, 1)).astype(np.uint16)


def unstriped(offs):
    return offs[:16].T.reshape(-1).astype(np.int64)


E2M1 = np.array([0.0, 0.5, 1.0, 1.5, 2.0, 3.0, 4.0, 6.0, -0.0, -0.5, -1.0, -1.5, -2.0, -3.0, -4.0, -6.0])


def pack_weight(w, fmt):
    k, n = w.shape
    w = f64(np.asarray(w, np.float32).astype(ml_dtypes.bfloat16)).reshape(k // 32, 32, n)
    amax = np.abs(w).max(1)
    if fmt == "e4m3":
        byte = np.frexp(amax)[1] - 1 + 127 - 7
    else:
        mant, ex = np.frexp(amax / 6.0)
        byte = np.where(mant > 0.5, ex, ex - 1) + 127
    byte = np.clip(np.where(amax > 0, byte, 1), 1, 254)
    scaled = (w * np.exp2(127.0 - byte)[:, None, :]).reshape(k, n).astype(np.float32)
    by_word = np.ascontiguousarray(scaled.reshape(k // 512, 128, 4, n).transpose(0, 1, 3, 2))
    if fmt == "e4m3":
        words = by_word.astype(ml_dtypes.float8_e4m3fn).view(np.uint8)
    else:
        c = by_word.astype(ml_dtypes.float4_e2m1fn).view(np.uint8) & 0xF
        words = (c[..., 0::2] | (c[..., 1::2] << 4)).reshape(k // 512, 128, 2 * n)
    return np.ascontiguousarray(words), np.ascontiguousarray(byte.astype(np.uint8).reshape(k // 512, 16, n))


def unpack_weight(words, scales, fmt):
    g, _, n = scales.shape
    words = np.ascontiguousarray(words).reshape(g, 128, n, -1)
    if fmt == "e4m3":
        vals = words.view(ml_dtypes.float8_e4m3fn).astype(np.float64)
    else:
        nib = np.empty((g, 128, n, 4), np.uint8)
        nib[..., 0::2] = words & 0xF
        nib[..., 1::2] = words >> 4
        vals = E2M1[nib]
    vals = vals * np.repeat(np.exp2(scales.astype(np.float64) - 127.0), 8, axis=1)[..., None]
    return vals.transpose(0, 1, 3, 2).reshape(g * 512, n)


def gelu(v):
    return 0.5 * v * (1.0 + np.tanh(np.sqrt(2.0 / np.pi) * (v + 0.044715 * v**3)))


K, R, N, D, T, S, T2 = 1536, 512, 1024, 128, 4096, 1024, 2048

def setup_inputs():
    n = np.random.standard_normal
    s = mx_kscale(K)[:, None]
    u = mx_kscale(R)[:, None]
    tab_words, tab_scales = pack_weight(n((K, T)) * s, "e4m3")
    w0_words, w0_scales = pack_weight(n((K, N)) / np.sqrt(K) / s, "e2m1")
    return {
        "tab_words": tab_words, "tab_scales": tab_scales,
        "offs": striped(np.random.permutation(T)[:S]),
        "w0_words": w0_words, "w0_scales": w0_scales,
        "wa": (n((K, R)) / np.sqrt(K) / s * u.T).astype(np.float32),
        "lam": np.exp(0.3 * n(R)).astype(np.float32),
        "strength": np.exp(0.3 * n(S)).astype(np.float32),
        "wb": (n((R, N)) / np.sqrt(R) / u).astype(np.float32),
        "bk": (0.5 * n(N)).astype(np.float32),
        "wgo": np.exp(0.3 * n((D, S))).astype(np.float32),
        "offs2": striped(np.random.permutation(T2)[:S]),
    }

def reference(tab_words, tab_scales, offs, w0_words, w0_scales, wa, lam, strength, wb, bk, wgo, offs2):
    v = unpack_weight(tab_words, tab_scales, "e4m3")[:, unstriped(offs)]
    w0 = unpack_weight(w0_words, w0_scales, "e2m1")
    low = mxq(f64(wa), 0, "e4m3").T @ v
    h = mxq(low * f64(lam)[:, None] * f64(strength)[None, :], 0, "e4m3")
    y = (w0.T @ v + mxq(f64(wb), 0, "e4m3").T @ h) + f64(bk)[:, None]
    out = np.zeros((N, T2))
    out[:, unstriped(offs2)] = np.tile(f64(wgo), (N // D, 1)) * y
    return out

@@ -1,0 +1,268 @@
+from contextlib import ExitStack
+
+import concourse.mybir as mybir
+from concourse.masks import make_identity
+
+K, R, N, T, S, T2 = 1536, 512, 1024, 4096, 1024, 2048
+FLOPS = 2 * S * (K * R + K * N + R * N)
+
+F32 = mybir.dt.float32
+BF16 = mybir.dt.bfloat16
+I32 = mybir.dt.int32
+U32 = mybir.dt.uint32
+U16 = mybir.dt.uint16
+U8 = mybir.dt.uint8
+FP8X4 = mybir.dt.float8_e4m3fn_x4
+FP4X4 = mybir.dt.float4_e2m1fn_x4
+MULT = mybir.AluOpType.mult
+ADD = mybir.AluOpType.add
+
+P = 128
+PACK = 4
+PASSES = K // (P * PACK)
+HALF = S // 2
+CHUNK = 128
+HEADS = N // P
+WB_COLS = [(0, 256), (256, 512), (512, 1024)]
+OUT_BUFS = 3
+
+
+def tile_list_adapted_key_cache_kernel(
+    tc, tab_words, tab_scales, offs, w0_words, w0_scales, wa, lam, strength, wb, bk, wgo, offs2, out
+):
+    nc = tc.nc
+    with ExitStack() as ctx:
+        keep = ctx.enter_context(tc.tile_pool(name="keep", bufs=1))
+        ring = ctx.enter_context(tc.tile_pool(name="ring", bufs=3))
+        low_psum = ctx.enter_context(tc.psum_pool(name="low_psum", bufs=4))
+        y_psum = ctx.enter_context(tc.psum_pool(name="y_psum", bufs=4))
+
+        idx = keep.tile([P, S // 16], U16, name="idx")
+        idx2 = keep.tile([P, S // 16], U16, name="idx2")
+        table = [keep.tile([P, T], I32, name="table%d" % a, align_bytes=64) for a in range(PASSES)]
+        scale_rows = keep.tile([P, T // 4], I32, name="scale_rows", align_bytes=64)
+        picked_rows = keep.tile([P, S // 4], I32, name="picked_rows", align_bytes=64)
+        v_scales = keep.tile([P, PASSES, S // 4], I32, name="v_scales", align_bytes=64)
+        v_words = [keep.tile([P, S], I32, name="v_words%d" % a, align_bytes=64) for a in range(PASSES)]
+        w0_codes = keep.tile([P, PASSES, N // 2], I32, name="w0_codes", align_bytes=64)
+        w0_planes = keep.tile([P, PASSES, N // 4], I32, name="w0_planes", align_bytes=64)
+        wa_raw = [keep.tile([P, PACK, R], F32, name="wa_raw%d" % a) for a in range(PASSES)]
+        wa_bf = [keep.tile([P, PACK, P, PACK], BF16, name="wa_bf%d" % a, align_bytes=64) for a in range(PASSES)]
+        wa_codes = keep.tile([P, PASSES, R], U32, name="wa_codes", align_bytes=64)
+        wa_planes = keep.tile([P, PASSES, R], U8, name="wa_planes", align_bytes=64)
+        wb_raw = [keep.tile([P, PACK, c1 - c0], F32, name="wb_raw%d" % c0) for c0, c1 in WB_COLS]
+        wb_bf = keep.tile([P, N, PACK], BF16, name="wb_bf", align_bytes=64)
+        wb_codes = keep.tile([P, N], U32, name="wb_codes", align_bytes=64)
+        wb_plane = keep.tile([P, N], U8, name="wb_plane", align_bytes=64)
+        gain = keep.tile([P, S, PACK], F32, name="gain", align_bytes=64)
+        h_bf = keep.tile([P, S, PACK], BF16, name="h_bf", align_bytes=64)
+        h_codes = keep.tile([P, S], U32, name="h_codes", align_bytes=64)
+        h_plane = keep.tile([P, S], U8, name="h_plane", align_bytes=64)
+        wgo_sb = keep.tile([P, S], F32, name="wgo_sb", align_bytes=64)
+        lam_sb = keep.tile([P, PACK], F32, name="lam_sb")
+        strength_sb = keep.tile([P, S // P], F32, name="strength_sb")
+        bk_rows = keep.tile([P, P], F32, name="bk_rows")
+        bk_cols = keep.tile([P, HEADS], F32, name="bk_cols")
+        ident = keep.tile([P, P], F32, name="ident")
+        cache = [keep.tile([P, T2], F32, name="cache%d" % b, align_bytes=64) for b in range(OUT_BUFS)]
+
+        nc.vector.memset(scale_rows[:], 0)
+        nc.vector.memset(w0_planes[:], 0)
+        nc.vector.memset(bk_rows[:], 0.0)
+        nc.vector.memset(v_scales[:], 0)
+
+        def load_table(a):
+            nc.sync.dma_start(table[a][:], tab_words[a].rearrange("p t i -> p (t i)").bitcast(I32))
+
+        def load_wa(a, c0, c1):
+            rows = wa[a * P * PACK : (a + 1) * P * PACK, c0:c1]
+            nc.sync.dma_start(wa_raw[a][:, :, c0:c1], rows.rearrange("(p j) c -> p j c", j=PACK))
+
+        def load_wb(i):
+            c0, c1 = WB_COLS[i]
+            nc.sync.dma_start(wb_raw[i][:], wb[:, c0:c1].rearrange("(p j) c -> p j c", j=PACK))
+
+        all_scale_rows = tab_scales.rearrange("a q t -> (a q) t").bitcast(I32)
+        load_table(0)
+        nc.sync.dma_start(idx[:], offs)
+        nc.sync.dma_start(scale_rows[0:P:4, :], all_scale_rows[0:32, :])
+        nc.sync.dma_start(scale_rows[1:P:8, :], all_scale_rows[32:48, :])
+        load_wa(0, 0, R)
+        load_table(1)
+        load_wa(1, 0, R)
+        load_table(2)
+        load_wa(2, 0, R // 2)
+        load_wa(2, R // 2, R)
+        load_wb(0)
+        nc.sync.dma_start(w0_codes[:], w0_words.rearrange("a p b -> p a b").bitcast(I32))
+        nc.sync.dma_start(idx2[:], offs2)
+        nc.sync.dma_start(wgo_sb[:, 0:HALF], wgo[:, 0:HALF])
+        nc.sync.dma_start(wgo_sb[:, HALF:S], wgo[:, HALF:S])
+        load_wb(1)
+        load_wb(2)
+
+        nc.gpsimd.dma_start(strength_sb[:], strength.rearrange("(p c) -> p c", c=S // P))
+        nc.gpsimd.dma_start(lam_sb[:], lam.rearrange("(p t) -> p t", t=PACK))
+        make_identity(nc, ident[:])
+        nc.gpsimd.dma_start(bk_rows[0:HEADS, :], bk.rearrange("(c p) -> c p", p=P))
+        for q in range(4):
+            rows = w0_scales[:, 4 * q : 4 * q + 4, :].rearrange("a r n -> r a n").bitcast(I32)
+            nc.gpsimd.dma_start(w0_planes[32 * q : 32 * q + 4, :, :], rows)
+
+        for b in range(OUT_BUFS):
+            nc.vector.memset(cache[b][:], 0.0)
+
+        def gather_words(a, j0, j1):
+            nc.vector.tensor_copy(
+                v_words[a][:, j0:j1].bitcast(U32), table[a][:].bitcast(U32).indirect(idx[:, j0 // 16 : j1 // 16])
+            )
+
+        nc.vector.tensor_copy(picked_rows[:].bitcast(U8), scale_rows[:].bitcast(U8).indirect(idx[:]))
+        for a in range(PASSES):
+            for q in range(4):
+                if a < 2:
+                    first = 4 * (16 * a + 4 * q)
+                    src = picked_rows[first : first + 13 : 4, :]
+                else:
+                    first = 1 + 8 * (4 * q)
+                    src = picked_rows[first : first + 25 : 8, :]
+                nc.gpsimd.dma_start(v_scales[32 * q : 32 * q + 4, a, :], src)
+        gather_words(0, 0, S)
+
+        gain_view = gain[:].rearrange("p (q c) t -> p q c t", c=S // P)
+        for b in range(2):
+            spread = low_psum.tile([P, PACK, P], F32, name="low")
+            for c in range(4):
+                col = 4 * b + c
+                nc.tensor.transpose(spread[:, c, :], strength_sb[:, col : col + 1].to_broadcast([P, P]), ident[:])
+            nc.vector.tensor_tensor(
+                gain_view[:, :, 4 * b : 4 * b + 4, :],
+                spread[:].rearrange("p c q -> p q c").unsqueeze(3).broadcast_to([P, P, 4, PACK]),
+                lam_sb[:].unsqueeze(1).unsqueeze(1).broadcast_to([P, P, 4, PACK]),
+                MULT,
+            )
+        bk_t = low_psum.tile([P, PACK, P], F32, name="low")
+        nc.tensor.transpose(bk_t[:, 0, :], bk_rows[:], ident[:])
+        nc.scalar.copy(bk_cols[:], bk_t[:, 0, 0:HEADS])
+
+        def cast_wa(engine_copy, a, m0, m1):
+            engine_copy(
+                wa_bf[a][:, :, m0:m1, :].rearrange("p t m j -> p m t j"),
+                wa_raw[a][:, :, PACK * m0 : PACK * m1].rearrange("p j (m t) -> p m t j", t=PACK),
+            )
+
+        def quantize_wa(a):
+            nc.vector.quantize_mx(
+                out=wa_codes[:, a, :].bitcast(FP8X4),
+                scales=wa_planes[:, a, :],
+                in_=wa_bf[a][:].rearrange("p t m j -> p (t m j)"),
+            )
+
+        cast_wa(nc.scalar.copy, 0, 0, P)
+        quantize_wa(0)
+        gather_words(1, 0, S)
+        cast_wa(nc.scalar.copy, 1, 0, P)
+        quantize_wa(1)
+        gather_words(2, 0, HALF)
+        cast_wa(nc.scalar.copy, 2, 0, P // 2)
+        cast_wa(nc.vector.tensor_copy, 2, P // 2, P)
+        quantize_wa(2)
+        gather_words(2, HALF, S)
+
+        def prepare_wb(i):
+            c0, c1 = WB_COLS[i]
+            nc.scalar.copy(wb_bf[:, c0:c1, :], wb_raw[i][:].rearrange("p j c -> p c j"))
+            nc.vector.quantize_mx(
+                out=wb_codes[:, c0:c1].bitcast(FP8X4),
+                scales=wb_plane[:, c0:c1],
+                in_=wb_bf[:, c0:c1, :].rearrange("p c j -> p (c j)"),
+            )
+
+        def v_operand(a, j0, j1):
+            return v_words[a][:, j0:j1].bitcast(FP8X4), v_scales[:, a, j0 // 4 : j1 // 4].bitcast(U8)
+
+        def make_h_chunk(j0):
+            low = low_psum.tile([P, PACK, CHUNK], F32, name="low")
+            for t in range(PACK):
+                for a in range(PASSES):
+                    codes, plane = v_operand(a, j0, j0 + CHUNK)
+                    nc.tensor.matmul_mx(
+                        out=low[:, t, :],
+                        lhsT=wa_codes[:, a, t * P : (t + 1) * P].bitcast(FP8X4),
+                        lhsT_scale=wa_planes[:, a, t * P : (t + 1) * P],
+                        rhs=codes,
+                        rhs_scale=plane,
+                        start=(a == 0),
+                        stop=(a == PASSES - 1),
+                    )
+            nc.vector.tensor_tensor(
+                h_bf[:, j0 : j0 + CHUNK, :], low[:].rearrange("p t j -> p j t"), gain[:, j0 : j0 + CHUNK, :], MULT
+            )
+
+        def quantize_h(j0, j1):
+            nc.vector.quantize_mx(
+                out=h_codes[:, j0:j1].bitcast(FP8X4),
+                scales=h_plane[:, j0:j1],
+                in_=h_bf[:, j0:j1, :].rearrange("p j t -> p (j t)"),
+            )
+
+        def make_h_half(half):
+            for pair in range(2):
+                j0 = half * HALF + pair * 2 * CHUNK
+                make_h_chunk(j0)
+                make_h_chunk(j0 + CHUNK)
+                quantize_h(j0, j0 + 2 * CHUNK)
+
+        def keys(head, half, dst):
+            j0, j1 = half * HALF, (half + 1) * HALF
+            n0, n1 = head * P, (head + 1) * P
+            y = y_psum.tile([P, HALF], F32, name="y")
+            for a in range(PASSES):
+                codes, plane = v_operand(a, j0, j1)
+                nc.tensor.matmul_mx(
+                    out=y[:],
+                    lhsT=w0_codes[:, a, n0 // 2 : n1 // 2].bitcast(U8).bitcast(FP4X4),
+                    lhsT_scale=w0_planes[:, a, n0 // 4 : n1 // 4].bitcast(U8),
+                    rhs=codes,
+                    rhs_scale=plane,
+                    start=(a == 0),
+                    stop=False,
+                )
+            nc.tensor.matmul_mx(
+                out=y[:],
+                lhsT=wb_codes[:, n0:n1].bitcast(FP8X4),
+                lhsT_scale=wb_plane[:, n0:n1],
+                rhs=h_codes[:, j0:j1].bitcast(FP8X4),
+                rhs_scale=h_plane[:, j0:j1],
+                start=False,
+                stop=True,
+            )
+            nc.vector.scalar_tensor_tensor(dst, y[:], bk_cols[:, head : head + 1], wgo_sb[:, j0:j1], ADD, MULT)
+
+        def scatter(head, values, j0, j1):
+            nc.vector.tensor_copy(cache[head % OUT_BUFS][:].indirect(idx2[:, j0 // 16 : j1 // 16]), values)
+
+        def store(head):
+            nc.sync.dma_start(out[head * P : (head + 1) * P, :], cache[head % OUT_BUFS][:])
+
+        prepare_wb(0)
+        make_h_half(0)
+        early = [ring.tile([P, S], F32, name="weighted", align_bytes=64) for head in range(2)]
+        keys(0, 0, early[0][:, 0:HALF])
+        keys(1, 0, early[1][:, 0:HALF])
+        scatter(0, early[0][:, 0:HALF], 0, HALF)
+        make_h_half(1)
+        scatter(1, early[1][:, 0:HALF], 0, HALF)
+        prepare_wb(1)
+        for head in range(2):
+            keys(head, 1, early[head][:, HALF:S])
+        for head in range(2):
+            scatter(head, early[head][:, HALF:S], HALF, S)
+            store(head)
+        prepare_wb(2)
+        for head in range(2, HEADS):
+            weighted = ring.tile([P, S], F32, name="weighted", align_bytes=64)
+            keys(head, 0, weighted[:, 0:HALF])
+            keys(head, 1, weighted[:, HALF:S])
+            scatter(head, weighted[:], 0, S)
+            store(head)

@@ -15,7 +15,7 @@ U8 = mybir.dt.uint8
 FP8X4 = mybir.dt.float8_e4m3fn_x4
 FP4X4 = mybir.dt.float4_e2m1fn_x4
 MULT = mybir.AluOpType.mult
-ADD = mybir.AluOpType.add
+IDENTITY = mybir.ActivationFunctionType.Identity
 
 P = 128
 PACK = 4
@@ -51,11 +51,9 @@ def tile_list_adapted_key_cache_kernel(
         wa_codes = keep.tile([P, PASSES, R], U32, name="wa_codes", align_bytes=64)
         wa_planes = keep.tile([P, PASSES, R], U8, name="wa_planes", align_bytes=64)
         wb_raw = [keep.tile([P, PACK, c1 - c0], F32, name="wb_raw%d" % c0) for c0, c1 in WB_COLS]
-        wb_bf = keep.tile([P, N, PACK], BF16, name="wb_bf", align_bytes=64)
         wb_codes = keep.tile([P, N], U32, name="wb_codes", align_bytes=64)
         wb_plane = keep.tile([P, N], U8, name="wb_plane", align_bytes=64)
         gain = keep.tile([P, S, PACK], F32, name="gain", align_bytes=64)
-        h_bf = keep.tile([P, S, PACK], BF16, name="h_bf", align_bytes=64)
         h_codes = keep.tile([P, S], U32, name="h_codes", align_bytes=64)
         h_plane = keep.tile([P, S], U8, name="h_plane", align_bytes=64)
         wgo_sb = keep.tile([P, S], F32, name="wgo_sb", align_bytes=64)
@@ -66,10 +64,8 @@ def tile_list_adapted_key_cache_kernel(
         ident = keep.tile([P, P], F32, name="ident")
         cache = [keep.tile([P, T2], F32, name="cache%d" % b, align_bytes=64) for b in range(OUT_BUFS)]
 
-        nc.vector.memset(scale_rows[:], 0)
-        nc.vector.memset(w0_planes[:], 0)
-        nc.vector.memset(bk_rows[:], 0.0)
         nc.vector.memset(v_scales[:], 0)
+        nc.vector.memset(w0_planes[:], 0)
 
         def load_table(a):
             nc.sync.dma_start(table[a][:], tab_words[a].rearrange("p t i -> p (t i)").bitcast(I32))
@@ -83,31 +79,31 @@ def tile_list_adapted_key_cache_kernel(
             nc.sync.dma_start(wb_raw[i][:], wb[:, c0:c1].rearrange("(p j) c -> p j c", j=PACK))
 
         all_scale_rows = tab_scales.rearrange("a q t -> (a q) t").bitcast(I32)
-        load_table(0)
+        for odd in range(2):
+            rows = all_scale_rows[16 * odd : 16 * odd + 32, :].unsqueeze(1).broadcast_to([32, 2, T // 4])
+            nc.sync.dma_start(scale_rows[odd:P:2, :], rows)
         nc.sync.dma_start(idx[:], offs)
-        nc.sync.dma_start(scale_rows[0:P:4, :], all_scale_rows[0:32, :])
-        nc.sync.dma_start(scale_rows[1:P:8, :], all_scale_rows[32:48, :])
+        load_table(0)
+        nc.sync.dma_start(strength_sb[:], strength.rearrange("(p c) -> p c", c=S // P))
+        nc.sync.dma_start(lam_sb[:], lam.rearrange("(p t) -> p t", t=PACK))
         load_wa(0, 0, R)
-        load_table(1)
         load_wa(1, 0, R)
+        load_table(1)
+        bk_by_head = bk.rearrange("(c p) -> c p", p=P)
+        nc.sync.dma_start(bk_rows[:], bk_by_head.unsqueeze(0).broadcast_to([P // HEADS, HEADS, P]))
+        load_wa(2, 0, R)
         load_table(2)
-        load_wa(2, 0, R // 2)
-        load_wa(2, R // 2, R)
         load_wb(0)
+        for q in range(4):
+            rows = w0_scales[:, 4 * q : 4 * q + 4, :].rearrange("a r n -> r a n").bitcast(I32)
+            nc.sync.dma_start(w0_planes[32 * q : 32 * q + 4, :, :], rows)
         nc.sync.dma_start(w0_codes[:], w0_words.rearrange("a p b -> p a b").bitcast(I32))
         nc.sync.dma_start(idx2[:], offs2)
-        nc.sync.dma_start(wgo_sb[:, 0:HALF], wgo[:, 0:HALF])
-        nc.sync.dma_start(wgo_sb[:, HALF:S], wgo[:, HALF:S])
+        nc.sync.dma_start(wgo_sb[:], wgo)
         load_wb(1)
         load_wb(2)
 
-        nc.gpsimd.dma_start(strength_sb[:], strength.rearrange("(p c) -> p c", c=S // P))
-        nc.gpsimd.dma_start(lam_sb[:], lam.rearrange("(p t) -> p t", t=PACK))
         make_identity(nc, ident[:])
-        nc.gpsimd.dma_start(bk_rows[0:HEADS, :], bk.rearrange("(c p) -> c p", p=P))
-        for q in range(4):
-            rows = w0_scales[:, 4 * q : 4 * q + 4, :].rearrange("a r n -> r a n").bitcast(I32)
-            nc.gpsimd.dma_start(w0_planes[32 * q : 32 * q + 4, :, :], rows)
 
         for b in range(OUT_BUFS):
             nc.vector.memset(cache[b][:], 0.0)
@@ -120,12 +116,9 @@ def tile_list_adapted_key_cache_kernel(
         nc.vector.tensor_copy(picked_rows[:].bitcast(U8), scale_rows[:].bitcast(U8).indirect(idx[:]))
         for a in range(PASSES):
             for q in range(4):
-                if a < 2:
-                    first = 4 * (16 * a + 4 * q)
-                    src = picked_rows[first : first + 13 : 4, :]
-                else:
-                    first = 1 + 8 * (4 * q)
-                    src = picked_rows[first : first + 25 : 8, :]
+                row = 16 * a + 4 * q
+                first = 4 * row if row < 32 else 4 * (row - 16) + 1
+                src = picked_rows[first : first + 13 : 4, :]
                 nc.gpsimd.dma_start(v_scales[32 * q : 32 * q + 4, a, :], src)
         gather_words(0, 0, S)
 
@@ -160,28 +153,28 @@ def tile_list_adapted_key_cache_kernel(
 
         cast_wa(nc.scalar.copy, 0, 0, P)
         quantize_wa(0)
-        gather_words(1, 0, S)
         cast_wa(nc.scalar.copy, 1, 0, P)
         quantize_wa(1)
-        gather_words(2, 0, HALF)
-        cast_wa(nc.scalar.copy, 2, 0, P // 2)
-        cast_wa(nc.vector.tensor_copy, 2, P // 2, P)
+        gather_words(1, 0, S)
+        cast_wa(nc.scalar.copy, 2, 0, P)
         quantize_wa(2)
+        gather_words(2, 0, HALF)
         gather_words(2, HALF, S)
 
         def prepare_wb(i):
             c0, c1 = WB_COLS[i]
-            nc.scalar.copy(wb_bf[:, c0:c1, :], wb_raw[i][:].rearrange("p j c -> p c j"))
+            wb_bf = keep.tile([P, c1 - c0, PACK], BF16, name="wb_bf", tag="rounded%d" % i, align_bytes=64)
+            nc.scalar.copy(wb_bf[:], wb_raw[i][:].rearrange("p j c -> p c j"))
             nc.vector.quantize_mx(
                 out=wb_codes[:, c0:c1].bitcast(FP8X4),
                 scales=wb_plane[:, c0:c1],
-                in_=wb_bf[:, c0:c1, :].rearrange("p c j -> p (c j)"),
+                in_=wb_bf[:].rearrange("p c j -> p (c j)"),
             )
 
         def v_operand(a, j0, j1):
             return v_words[a][:, j0:j1].bitcast(FP8X4), v_scales[:, a, j0 // 4 : j1 // 4].bitcast(U8)
 
-        def make_h_chunk(j0):
+        def make_h_chunk(h_bf, j0):
             low = low_psum.tile([P, PACK, CHUNK], F32, name="low")
             for t in range(PACK):
                 for a in range(PASSES):
@@ -196,22 +189,23 @@ def tile_list_adapted_key_cache_kernel(
                         stop=(a == PASSES - 1),
                     )
             nc.vector.tensor_tensor(
-                h_bf[:, j0 : j0 + CHUNK, :], low[:].rearrange("p t j -> p j t"), gain[:, j0 : j0 + CHUNK, :], MULT
+                h_bf[:, j0 % HALF : j0 % HALF + CHUNK, :], low[:].rearrange("p t j -> p j t"), gain[:, j0 : j0 + CHUNK, :], MULT
             )
 
-        def quantize_h(j0, j1):
+        def quantize_h(h_bf, j0, j1):
             nc.vector.quantize_mx(
                 out=h_codes[:, j0:j1].bitcast(FP8X4),
                 scales=h_plane[:, j0:j1],
-                in_=h_bf[:, j0:j1, :].rearrange("p j t -> p (j t)"),
+                in_=h_bf[:, j0 % HALF : j0 % HALF + j1 - j0, :].rearrange("p j t -> p (j t)"),
             )
 
         def make_h_half(half):
+            h_bf = keep.tile([P, HALF, PACK], BF16, name="h_bf", tag="rounded%d" % (half + 1), align_bytes=64)
             for pair in range(2):
                 j0 = half * HALF + pair * 2 * CHUNK
-                make_h_chunk(j0)
-                make_h_chunk(j0 + CHUNK)
-                quantize_h(j0, j0 + 2 * CHUNK)
+                make_h_chunk(h_bf, j0)
+                make_h_chunk(h_bf, j0 + CHUNK)
+                quantize_h(h_bf, j0, j0 + 2 * CHUNK)
 
         def keys(head, half, dst):
             j0, j1 = half * HALF, (half + 1) * HALF
@@ -237,10 +231,11 @@ def tile_list_adapted_key_cache_kernel(
                 start=False,
                 stop=True,
             )
-            nc.vector.scalar_tensor_tensor(dst, y[:], bk_cols[:, head : head + 1], wgo_sb[:, j0:j1], ADD, MULT)
+            nc.scalar.activation(dst, y[:], IDENTITY, bias=bk_cols[:, head : head + 1])
 
         def scatter(head, values, j0, j1):
-            nc.vector.tensor_copy(cache[head % OUT_BUFS][:].indirect(idx2[:, j0 // 16 : j1 // 16]), values)
+            window = cache[head % OUT_BUFS][:].indirect(idx2[:, j0 // 16 : j1 // 16])
+            nc.vector.tensor_tensor(window, values, wgo_sb[:, j0:j1], MULT)
 
         def store(head):
             nc.sync.dma_start(out[head * P : (head + 1) * P, :], cache[head % OUT_BUFS][:])

@@ -24,6 +24,7 @@ HALF = S // 2
 CHUNK = 128
 HEADS = N // P
 WB_COLS = [(0, 256), (256, 512), (512, 1024)]
+WB_SLOTS = ["wa_raw0", "table1", "wa_raw2"]
 OUT_BUFS = 3
 
 
@@ -39,24 +40,21 @@ def tile_list_adapted_key_cache_kernel(
 
         idx = keep.tile([P, S // 16], U16, name="idx")
         idx2 = keep.tile([P, S // 16], U16, name="idx2")
-        table = [keep.tile([P, T], I32, name="table%d" % a, align_bytes=64) for a in range(PASSES)]
-        scale_rows = keep.tile([P, T // 4], I32, name="scale_rows", align_bytes=64)
+        scale_rows = keep.tile([P, T // 4], I32, name="scale_rows", tag="table2", align_bytes=64)
+        table = {}
         picked_rows = keep.tile([P, S // 4], I32, name="picked_rows", align_bytes=64)
         v_scales = keep.tile([P, PASSES, S // 4], I32, name="v_scales", align_bytes=64)
         v_words = [keep.tile([P, S], I32, name="v_words%d" % a, align_bytes=64) for a in range(PASSES)]
-        w0_codes = keep.tile([P, PASSES, N // 2], I32, name="w0_codes", align_bytes=64)
-        w0_planes = keep.tile([P, PASSES, N // 4], I32, name="w0_planes", align_bytes=64)
-        wa_raw = [keep.tile([P, PACK, R], F32, name="wa_raw%d" % a) for a in range(PASSES)]
+        wa_raw = [keep.tile([P, PACK, R], F32, name="wa_raw%d" % a, align_bytes=64) for a in range(PASSES)]
         wa_bf = [keep.tile([P, PACK, P, PACK], BF16, name="wa_bf%d" % a, align_bytes=64) for a in range(PASSES)]
         wa_codes = keep.tile([P, PASSES, R], U32, name="wa_codes", align_bytes=64)
         wa_planes = keep.tile([P, PASSES, R], U8, name="wa_planes", align_bytes=64)
-        wb_raw = [keep.tile([P, PACK, c1 - c0], F32, name="wb_raw%d" % c0) for c0, c1 in WB_COLS]
+        wb_raw = {}
         wb_codes = keep.tile([P, N], U32, name="wb_codes", align_bytes=64)
         wb_plane = keep.tile([P, N], U8, name="wb_plane", align_bytes=64)
         gain = keep.tile([P, S, PACK], F32, name="gain", align_bytes=64)
         h_codes = keep.tile([P, S], U32, name="h_codes", align_bytes=64)
         h_plane = keep.tile([P, S], U8, name="h_plane", align_bytes=64)
-        wgo_sb = keep.tile([P, S], F32, name="wgo_sb", align_bytes=64)
         lam_sb = keep.tile([P, PACK], F32, name="lam_sb")
         strength_sb = keep.tile([P, S // P], F32, name="strength_sb")
         bk_rows = keep.tile([P, P], F32, name="bk_rows")
@@ -65,9 +63,9 @@ def tile_list_adapted_key_cache_kernel(
         cache = [keep.tile([P, T2], F32, name="cache%d" % b, align_bytes=64) for b in range(OUT_BUFS)]
 
         nc.vector.memset(v_scales[:], 0)
-        nc.vector.memset(w0_planes[:], 0)
 
         def load_table(a):
+            table[a] = keep.tile([P, T], I32, name="table", tag="table%d" % a, align_bytes=64)
             nc.sync.dma_start(table[a][:], tab_words[a].rearrange("p t i -> p (t i)").bitcast(I32))
 
         def load_wa(a, c0, c1):
@@ -76,6 +74,7 @@ def tile_list_adapted_key_cache_kernel(
 
         def load_wb(i):
             c0, c1 = WB_COLS[i]
+            wb_raw[i] = keep.tile([P, PACK, c1 - c0], F32, name="wb_raw", tag=WB_SLOTS[i], align_bytes=64)
             nc.sync.dma_start(wb_raw[i][:], wb[:, c0:c1].rearrange("(p j) c -> p j c", j=PACK))
 
         all_scale_rows = tab_scales.rearrange("a q t -> (a q) t").bitcast(I32)
@@ -92,16 +91,7 @@ def tile_list_adapted_key_cache_kernel(
         bk_by_head = bk.rearrange("(c p) -> c p", p=P)
         nc.sync.dma_start(bk_rows[:], bk_by_head.unsqueeze(0).broadcast_to([P // HEADS, HEADS, P]))
         load_wa(2, 0, R)
-        load_table(2)
-        load_wb(0)
-        for q in range(4):
-            rows = w0_scales[:, 4 * q : 4 * q + 4, :].rearrange("a r n -> r a n").bitcast(I32)
-            nc.sync.dma_start(w0_planes[32 * q : 32 * q + 4, :, :], rows)
-        nc.sync.dma_start(w0_codes[:], w0_words.rearrange("a p b -> p a b").bitcast(I32))
         nc.sync.dma_start(idx2[:], offs2)
-        nc.sync.dma_start(wgo_sb[:], wgo)
-        load_wb(1)
-        load_wb(2)
 
         make_identity(nc, ident[:])
 
@@ -119,7 +109,9 @@ def tile_list_adapted_key_cache_kernel(
                 row = 16 * a + 4 * q
                 first = 4 * row if row < 32 else 4 * (row - 16) + 1
                 src = picked_rows[first : first + 13 : 4, :]
-                nc.gpsimd.dma_start(v_scales[32 * q : 32 * q + 4, a, :], src)
+                nc.sync.dma_start(v_scales[32 * q : 32 * q + 4, a, :], src)
+                if row == 16:
+                    load_table(2)
         gather_words(0, 0, S)
 
         gain_view = gain[:].rearrange("p (q c) t -> p q c t", c=S // P)
@@ -160,6 +152,19 @@ def tile_list_adapted_key_cache_kernel(
         quantize_wa(2)
         gather_words(2, 0, HALF)
         gather_words(2, HALF, S)
+
+        load_wb(0)
+        w0_planes = keep.tile([P, PASSES, N // 4], I32, name="w0_planes", tag="wa_bf0", align_bytes=64)
+        nc.vector.memset(w0_planes[:], 0)
+        for q in range(4):
+            rows = w0_scales[:, 4 * q : 4 * q + 4, :].rearrange("a r n -> r a n").bitcast(I32)
+            nc.sync.dma_start(w0_planes[32 * q : 32 * q + 4, :, :], rows)
+        w0_codes = keep.tile([P, PASSES, N // 2], I32, name="w0_codes", tag="wa_raw1", align_bytes=64)
+        nc.sync.dma_start(w0_codes[:], w0_words.rearrange("a p b -> p a b").bitcast(I32))
+        wgo_sb = keep.tile([P, S], F32, name="wgo_sb", tag="wa_bf1", align_bytes=64)
+        nc.sync.dma_start(wgo_sb[:], wgo)
+        load_wb(1)
+        load_wb(2)
 
         def prepare_wb(i):
             c0, c1 = WB_COLS[i]

@@ -26,6 +26,7 @@ HEADS = N // P
 WB_COLS = [(0, 256), (256, 512), (512, 1024)]
 WB_SLOTS = ["wa_raw0", "table1", "wa_raw2"]
 OUT_BUFS = 3
+WARM_PASSES = 4
 
 
 def tile_list_adapted_key_cache_kernel(
@@ -87,11 +88,12 @@ def tile_list_adapted_key_cache_kernel(
         nc.sync.dma_start(lam_sb[:], lam.rearrange("(p t) -> p t", t=PACK))
         load_wa(0, 0, R)
         load_wa(1, 0, R)
-        load_table(1)
-        bk_by_head = bk.rearrange("(c p) -> c p", p=P)
-        nc.sync.dma_start(bk_rows[:], bk_by_head.unsqueeze(0).broadcast_to([P // HEADS, HEADS, P]))
-        load_wa(2, 0, R)
         nc.sync.dma_start(idx2[:], offs2)
+        load_table(1)
+        load_wa(2, 0, R)
+        bk_by_head = bk.rearrange("(c p) -> c p", p=P)
+        nc.gpsimd.memset(bk_rows[:], 0.0)
+        nc.gpsimd.dma_start(bk_rows[0:HEADS, :], bk_by_head)
 
         make_identity(nc, ident[:])
 
@@ -110,7 +112,7 @@ def tile_list_adapted_key_cache_kernel(
                 first = 4 * row if row < 32 else 4 * (row - 16) + 1
                 src = picked_rows[first : first + 13 : 4, :]
                 nc.sync.dma_start(v_scales[32 * q : 32 * q + 4, a, :], src)
-                if row == 16:
+                if row == 20:
                     load_table(2)
         gather_words(0, 0, S)
 
@@ -244,6 +246,20 @@ def tile_list_adapted_key_cache_kernel(
 
         def store(head):
             nc.sync.dma_start(out[head * P : (head + 1) * P, :], cache[head % OUT_BUFS][:])
+
+        warm = y_psum.tile([P, HALF], F32, name="y")
+        for v_pass, wa_pass in [(1, 0)] * 6 + [(0, 2)] * 2:
+            codes = v_operand(v_pass, 0, HALF)[0]
+            plane = v_operand(0, 0, HALF)[1]
+            nc.tensor.matmul_mx(
+                out=warm[:],
+                lhsT=wa_codes[:, wa_pass, 0:P].bitcast(FP8X4),
+                lhsT_scale=wa_planes[:, wa_pass, 0:P],
+                rhs=codes,
+                rhs_scale=plane,
+                start=True,
+                stop=True,
+            )
 
         prepare_wb(0)
         make_h_half(0)

@@ -23,10 +23,10 @@ PASSES = K // (P * PACK)
 HALF = S // 2
 CHUNK = 128
 HEADS = N // P
-WB_COLS = [(0, 256), (256, 512), (512, 1024)]
-WB_SLOTS = ["wa_raw0", "table1", "wa_raw2"]
+WB_HEADS = [(0, 1), (1, 4), (4, 8)]
+W0_HEADS = [(0, 2), (2, 8)]
 OUT_BUFS = 3
-WARM_PASSES = 4
+FIRST_TABLE_PIECES = 4
 
 
 def tile_list_adapted_key_cache_kernel(
@@ -41,19 +41,26 @@ def tile_list_adapted_key_cache_kernel(
 
         idx = keep.tile([P, S // 16], U16, name="idx")
         idx2 = keep.tile([P, S // 16], U16, name="idx2")
-        scale_rows = keep.tile([P, T // 4], I32, name="scale_rows", tag="table2", align_bytes=64)
-        table = {}
-        picked_rows = keep.tile([P, S // 4], I32, name="picked_rows", align_bytes=64)
-        v_scales = keep.tile([P, PASSES, S // 4], I32, name="v_scales", align_bytes=64)
+        scale_rows = keep.tile([P, T // 4], I32, name="scale_rows", align_bytes=64)
+        table = [keep.tile([P, T], I32, name="table%d" % a, align_bytes=64) for a in range(PASSES)]
+        v_planes = [keep.tile([P, S // 4], I32, name="v_plane%d" % a, align_bytes=64) for a in range(PASSES)]
         v_words = [keep.tile([P, S], I32, name="v_words%d" % a, align_bytes=64) for a in range(PASSES)]
-        wa_raw = [keep.tile([P, PACK, R], F32, name="wa_raw%d" % a, align_bytes=64) for a in range(PASSES)]
+        wa_raw = [keep.tile([P, PACK * R], F32, name="wa_raw%d" % a, align_bytes=64) for a in range(PASSES)]
         wa_bf = [keep.tile([P, PACK, P, PACK], BF16, name="wa_bf%d" % a, align_bytes=64) for a in range(PASSES)]
-        wa_codes = keep.tile([P, PASSES, R], U32, name="wa_codes", align_bytes=64)
-        wa_planes = keep.tile([P, PASSES, R], U8, name="wa_planes", align_bytes=64)
-        wb_raw = {}
+        wa_codes = [keep.tile([P, R], U32, name="wa_codes%d" % a, align_bytes=64) for a in range(PASSES)]
+        wa_planes = [keep.tile([P, R], U8, name="wa_plane%d" % a, align_bytes=64) for a in range(PASSES)]
+        wb_raw = [
+            keep.tile([P, PACK, P * (n1 - n0)], F32, name="wb_raw%d" % n0, align_bytes=64) for n0, n1 in WB_HEADS
+        ]
         wb_codes = keep.tile([P, N], U32, name="wb_codes", align_bytes=64)
         wb_plane = keep.tile([P, N], U8, name="wb_plane", align_bytes=64)
+        w0_planes = keep.tile([P, PASSES, N // 4], I32, name="w0_planes", align_bytes=64)
+        w0_codes = [
+            keep.tile([P, PASSES, P * (n1 - n0) // 2], I32, name="w0_codes%d" % n0, align_bytes=64) for n0, n1 in W0_HEADS
+        ]
+        wgo_sb = keep.tile([P, S], F32, name="wgo_sb", align_bytes=64)
         gain = keep.tile([P, S, PACK], F32, name="gain", align_bytes=64)
+        h_bf = [keep.tile([P, HALF, PACK], BF16, name="h_bf%d" % half, align_bytes=64) for half in range(2)]
         h_codes = keep.tile([P, S], U32, name="h_codes", align_bytes=64)
         h_plane = keep.tile([P, S], U8, name="h_plane", align_bytes=64)
         lam_sb = keep.tile([P, PACK], F32, name="lam_sb")
@@ -63,62 +70,71 @@ def tile_list_adapted_key_cache_kernel(
         ident = keep.tile([P, P], F32, name="ident")
         cache = [keep.tile([P, T2], F32, name="cache%d" % b, align_bytes=64) for b in range(OUT_BUFS)]
 
-        nc.vector.memset(v_scales[:], 0)
+        nc.vector.memset(scale_rows[:], 0)
+        for a in range(1, PASSES):
+            nc.vector.memset(v_planes[a][:], 0)
+        nc.vector.memset(w0_planes[:], 0)
 
-        def load_table(a):
-            table[a] = keep.tile([P, T], I32, name="table", tag="table%d" % a, align_bytes=64)
-            nc.sync.dma_start(table[a][:], tab_words[a].rearrange("p t i -> p (t i)").bitcast(I32))
+        def load_table(a, pieces):
+            words = tab_words[a].rearrange("p t i -> p (t i)").bitcast(I32)
+            width = T // pieces
+            for c0 in range(0, T, width):
+                nc.sync.dma_start(table[a][:, c0 : c0 + width], words[:, c0 : c0 + width])
 
-        def load_wa(a, c0, c1):
-            rows = wa[a * P * PACK : (a + 1) * P * PACK, c0:c1]
-            nc.sync.dma_start(wa_raw[a][:, :, c0:c1], rows.rearrange("(p j) c -> p j c", j=PACK))
+        def load_wa(a):
+            rows = wa[a * P * PACK : (a + 1) * P * PACK, :]
+            nc.sync.dma_start(wa_raw[a][:], rows.rearrange("(p j) c -> p (j c)", j=PACK))
 
         def load_wb(i):
-            c0, c1 = WB_COLS[i]
-            wb_raw[i] = keep.tile([P, PACK, c1 - c0], F32, name="wb_raw", tag=WB_SLOTS[i], align_bytes=64)
-            nc.sync.dma_start(wb_raw[i][:], wb[:, c0:c1].rearrange("(p j) c -> p j c", j=PACK))
+            n0, n1 = WB_HEADS[i]
+            nc.sync.dma_start(wb_raw[i][:], wb[:, P * n0 : P * n1].rearrange("(p j) c -> p j c", j=PACK))
 
-        all_scale_rows = tab_scales.rearrange("a q t -> (a q) t").bitcast(I32)
-        for odd in range(2):
-            rows = all_scale_rows[16 * odd : 16 * odd + 32, :].unsqueeze(1).broadcast_to([32, 2, T // 4])
-            nc.sync.dma_start(scale_rows[odd:P:2, :], rows)
+        def load_w0(i):
+            n0, n1 = W0_HEADS[i]
+            words = w0_words.rearrange("a p b -> p a b").bitcast(I32)
+            nc.sync.dma_start(w0_codes[i][:], words[:, :, P * n0 // 2 : P * n1 // 2])
+
         nc.sync.dma_start(idx[:], offs)
-        load_table(0)
         nc.sync.dma_start(strength_sb[:], strength.rearrange("(p c) -> p c", c=S // P))
         nc.sync.dma_start(lam_sb[:], lam.rearrange("(p t) -> p t", t=PACK))
-        load_wa(0, 0, R)
-        load_wa(1, 0, R)
         nc.sync.dma_start(idx2[:], offs2)
-        load_table(1)
-        load_wa(2, 0, R)
-        bk_by_head = bk.rearrange("(c p) -> c p", p=P)
+        load_table(0, FIRST_TABLE_PIECES)
+        for q in range(4):
+            rows = tab_scales[:, 4 * q : 4 * q + 4, :].bitcast(I32)
+            nc.scalar.dma_start(scale_rows[32 * q : 32 * q + 4 * PASSES, :], rows)
+        load_wa(0)
+        load_table(1, 1)
+        load_wa(2)
+        load_wa(1)
+        load_table(2, 1)
+        load_wb(0)
         nc.gpsimd.memset(bk_rows[:], 0.0)
-        nc.gpsimd.dma_start(bk_rows[0:HEADS, :], bk_by_head)
-
+        nc.gpsimd.dma_start(bk_rows[0:HEADS, :], bk.rearrange("(c p) -> c p", p=P))
         make_identity(nc, ident[:])
-
-        for b in range(OUT_BUFS):
-            nc.vector.memset(cache[b][:], 0.0)
 
         def gather_words(a, j0, j1):
             nc.vector.tensor_copy(
                 v_words[a][:, j0:j1].bitcast(U32), table[a][:].bitcast(U32).indirect(idx[:, j0 // 16 : j1 // 16])
             )
 
-        nc.vector.tensor_copy(picked_rows[:].bitcast(U8), scale_rows[:].bitcast(U8).indirect(idx[:]))
-        for a in range(PASSES):
-            for q in range(4):
-                row = 16 * a + 4 * q
-                first = 4 * row if row < 32 else 4 * (row - 16) + 1
-                src = picked_rows[first : first + 13 : 4, :]
-                nc.sync.dma_start(v_scales[32 * q : 32 * q + 4, a, :], src)
-                if row == 20:
-                    load_table(2)
+        nc.vector.tensor_copy(v_planes[0][:].bitcast(U8), scale_rows[:].bitcast(U8).indirect(idx[:]))
+        for a in range(1, PASSES):
+            nc.sync.dma_start(v_planes[a][0 : P - 4 * a, :], v_planes[0][4 * a : P, :])
+        for q in range(4):
+            rows = w0_scales[:, 4 * q : 4 * q + 4, :].rearrange("a r n -> r a n").bitcast(I32)
+            nc.sync.dma_start(w0_planes[32 * q : 32 * q + 4, :, :], rows)
+        load_w0(0)
+        nc.sync.dma_start(wgo_sb[:, 0:HALF], wgo[:, 0:HALF])
+        load_wb(1)
+        nc.sync.dma_start(wgo_sb[:, HALF:S], wgo[:, HALF:S])
+        load_w0(1)
+        load_wb(2)
+
         gather_words(0, 0, S)
 
         gain_view = gain[:].rearrange("p (q c) t -> p q c t", c=S // P)
         for b in range(2):
-            spread = low_psum.tile([P, PACK, P], F32, name="low")
+            spread = y_psum.tile([P, PACK, P], F32, name="y")
             for c in range(4):
                 col = 4 * b + c
                 nc.tensor.transpose(spread[:, c, :], strength_sb[:, col : col + 1].to_broadcast([P, P]), ident[:])
@@ -128,104 +144,90 @@ def tile_list_adapted_key_cache_kernel(
                 lam_sb[:].unsqueeze(1).unsqueeze(1).broadcast_to([P, P, 4, PACK]),
                 MULT,
             )
-        bk_t = low_psum.tile([P, PACK, P], F32, name="low")
+        bk_t = y_psum.tile([P, PACK, P], F32, name="y")
         nc.tensor.transpose(bk_t[:, 0, :], bk_rows[:], ident[:])
         nc.scalar.copy(bk_cols[:], bk_t[:, 0, 0:HEADS])
 
-        def cast_wa(engine_copy, a, m0, m1):
-            engine_copy(
-                wa_bf[a][:, :, m0:m1, :].rearrange("p t m j -> p m t j"),
-                wa_raw[a][:, :, PACK * m0 : PACK * m1].rearrange("p j (m t) -> p m t j", t=PACK),
-            )
+        for b in range(OUT_BUFS):
+            nc.vector.memset(cache[b][:], 0.0)
 
-        def quantize_wa(a):
+        def prepare_wa(a):
+            nc.scalar.copy(
+                wa_bf[a][:].rearrange("p t m j -> p m j t"),
+                wa_raw[a][:].rearrange("p (j m t) -> p m j t", j=PACK, t=PACK),
+            )
             nc.vector.quantize_mx(
-                out=wa_codes[:, a, :].bitcast(FP8X4),
-                scales=wa_planes[:, a, :],
+                out=wa_codes[a][:].bitcast(FP8X4),
+                scales=wa_planes[a][:],
                 in_=wa_bf[a][:].rearrange("p t m j -> p (t m j)"),
             )
 
-        cast_wa(nc.scalar.copy, 0, 0, P)
-        quantize_wa(0)
-        cast_wa(nc.scalar.copy, 1, 0, P)
-        quantize_wa(1)
+        prepare_wa(0)
         gather_words(1, 0, S)
-        cast_wa(nc.scalar.copy, 2, 0, P)
-        quantize_wa(2)
+        prepare_wa(2)
+        prepare_wa(1)
         gather_words(2, 0, HALF)
         gather_words(2, HALF, S)
 
-        load_wb(0)
-        w0_planes = keep.tile([P, PASSES, N // 4], I32, name="w0_planes", tag="wa_bf0", align_bytes=64)
-        nc.vector.memset(w0_planes[:], 0)
-        for q in range(4):
-            rows = w0_scales[:, 4 * q : 4 * q + 4, :].rearrange("a r n -> r a n").bitcast(I32)
-            nc.sync.dma_start(w0_planes[32 * q : 32 * q + 4, :, :], rows)
-        w0_codes = keep.tile([P, PASSES, N // 2], I32, name="w0_codes", tag="wa_raw1", align_bytes=64)
-        nc.sync.dma_start(w0_codes[:], w0_words.rearrange("a p b -> p a b").bitcast(I32))
-        wgo_sb = keep.tile([P, S], F32, name="wgo_sb", tag="wa_bf1", align_bytes=64)
-        nc.sync.dma_start(wgo_sb[:], wgo)
-        load_wb(1)
-        load_wb(2)
-
-        def prepare_wb(i):
-            c0, c1 = WB_COLS[i]
-            wb_bf = keep.tile([P, c1 - c0, PACK], BF16, name="wb_bf", tag="rounded%d" % i, align_bytes=64)
-            nc.scalar.copy(wb_bf[:], wb_raw[i][:].rearrange("p j c -> p c j"))
+        def prepare_wb(head):
+            i = [n0 <= head < n1 for n0, n1 in WB_HEADS].index(True)
+            c0 = P * (head - WB_HEADS[i][0])
+            wb_bf = ring.tile([P, P, PACK], BF16, name="wb_bf", align_bytes=64)
+            nc.scalar.copy(
+                wb_bf[:].rearrange("p (c i) j -> p c j i", i=4),
+                wb_raw[i][:, :, c0 : c0 + P].rearrange("p j (c i) -> p c j i", i=4),
+            )
             nc.vector.quantize_mx(
-                out=wb_codes[:, c0:c1].bitcast(FP8X4),
-                scales=wb_plane[:, c0:c1],
+                out=wb_codes[:, head * P : (head + 1) * P].bitcast(FP8X4),
+                scales=wb_plane[:, head * P : (head + 1) * P],
                 in_=wb_bf[:].rearrange("p c j -> p (c j)"),
             )
 
-        def v_operand(a, j0, j1):
-            return v_words[a][:, j0:j1].bitcast(FP8X4), v_scales[:, a, j0 // 4 : j1 // 4].bitcast(U8)
-
-        def make_h_chunk(h_bf, j0):
+        def make_h_chunk(j0):
             low = low_psum.tile([P, PACK, CHUNK], F32, name="low")
-            for t in range(PACK):
-                for a in range(PASSES):
-                    codes, plane = v_operand(a, j0, j0 + CHUNK)
+            for a in range(PASSES):
+                for t in range(PACK):
                     nc.tensor.matmul_mx(
                         out=low[:, t, :],
-                        lhsT=wa_codes[:, a, t * P : (t + 1) * P].bitcast(FP8X4),
-                        lhsT_scale=wa_planes[:, a, t * P : (t + 1) * P],
-                        rhs=codes,
-                        rhs_scale=plane,
-                        start=(a == 0),
-                        stop=(a == PASSES - 1),
+                        lhsT=wa_codes[a][:, t * P : (t + 1) * P].bitcast(FP8X4),
+                        lhsT_scale=wa_planes[a][:, t * P : (t + 1) * P],
+                        rhs=v_words[a][:, j0 : j0 + CHUNK].bitcast(FP8X4),
+                        rhs_scale=v_planes[0][4 * a : P, j0 // 4 : (j0 + CHUNK) // 4].bitcast(U8),
+                        start=(a == 0 and t == 0),
+                        stop=(a == PASSES - 1 and t == PACK - 1),
                     )
             nc.vector.tensor_tensor(
-                h_bf[:, j0 % HALF : j0 % HALF + CHUNK, :], low[:].rearrange("p t j -> p j t"), gain[:, j0 : j0 + CHUNK, :], MULT
+                h_bf[j0 // HALF][:, j0 % HALF : j0 % HALF + CHUNK, :],
+                low[:].rearrange("p t j -> p j t"),
+                gain[:, j0 : j0 + CHUNK, :],
+                MULT,
             )
 
-        def quantize_h(h_bf, j0, j1):
+        def quantize_h(j0, j1):
             nc.vector.quantize_mx(
                 out=h_codes[:, j0:j1].bitcast(FP8X4),
                 scales=h_plane[:, j0:j1],
-                in_=h_bf[:, j0 % HALF : j0 % HALF + j1 - j0, :].rearrange("p j t -> p (j t)"),
+                in_=h_bf[j0 // HALF][:, j0 % HALF : j0 % HALF + j1 - j0, :].rearrange("p j t -> p (j t)"),
             )
 
         def make_h_half(half):
-            h_bf = keep.tile([P, HALF, PACK], BF16, name="h_bf", tag="rounded%d" % (half + 1), align_bytes=64)
-            for pair in range(2):
-                j0 = half * HALF + pair * 2 * CHUNK
-                make_h_chunk(h_bf, j0)
-                make_h_chunk(h_bf, j0 + CHUNK)
-                quantize_h(h_bf, j0, j0 + 2 * CHUNK)
+            for j0 in range(half * HALF, (half + 1) * HALF, CHUNK):
+                make_h_chunk(j0)
+            quantize_h(half * HALF, (half + 1) * HALF)
 
         def keys(head, half, dst):
             j0, j1 = half * HALF, (half + 1) * HALF
+            i = [n0 <= head < n1 for n0, n1 in W0_HEADS].index(True)
+            c0 = P * (head - W0_HEADS[i][0]) // 2
             n0, n1 = head * P, (head + 1) * P
             y = y_psum.tile([P, HALF], F32, name="y")
             for a in range(PASSES):
-                codes, plane = v_operand(a, j0, j1)
                 nc.tensor.matmul_mx(
                     out=y[:],
-                    lhsT=w0_codes[:, a, n0 // 2 : n1 // 2].bitcast(U8).bitcast(FP4X4),
+                    lhsT=w0_codes[i][:, a, c0 : c0 + P // 2].bitcast(U8).bitcast(FP4X4),
                     lhsT_scale=w0_planes[:, a, n0 // 4 : n1 // 4].bitcast(U8),
-                    rhs=codes,
-                    rhs_scale=plane,
+                    rhs=v_words[a][:, j0:j1].bitcast(FP8X4),
+                    rhs_scale=v_planes[a][:, j0 // 4 : j1 // 4].bitcast(U8),
                     start=(a == 0),
                     stop=False,
                 )
@@ -247,38 +249,21 @@ def tile_list_adapted_key_cache_kernel(
         def store(head):
             nc.sync.dma_start(out[head * P : (head + 1) * P, :], cache[head % OUT_BUFS][:])
 
-        warm = y_psum.tile([P, HALF], F32, name="y")
-        for v_pass, wa_pass in [(1, 0)] * 6 + [(0, 2)] * 2:
-            codes = v_operand(v_pass, 0, HALF)[0]
-            plane = v_operand(0, 0, HALF)[1]
-            nc.tensor.matmul_mx(
-                out=warm[:],
-                lhsT=wa_codes[:, wa_pass, 0:P].bitcast(FP8X4),
-                lhsT_scale=wa_planes[:, wa_pass, 0:P],
-                rhs=codes,
-                rhs_scale=plane,
-                start=True,
-                stop=True,
-            )
-
         prepare_wb(0)
         make_h_half(0)
-        early = [ring.tile([P, S], F32, name="weighted", align_bytes=64) for head in range(2)]
-        keys(0, 0, early[0][:, 0:HALF])
-        keys(1, 0, early[1][:, 0:HALF])
-        scatter(0, early[0][:, 0:HALF], 0, HALF)
+        first = ring.tile([P, S], F32, name="weighted", align_bytes=64)
+        keys(0, 0, first[:, 0:HALF])
         make_h_half(1)
-        scatter(1, early[1][:, 0:HALF], 0, HALF)
+        scatter(0, first[:, 0:HALF], 0, HALF)
+        keys(0, 1, first[:, HALF:S])
         prepare_wb(1)
-        for head in range(2):
-            keys(head, 1, early[head][:, HALF:S])
-        for head in range(2):
-            scatter(head, early[head][:, HALF:S], HALF, S)
-            store(head)
-        prepare_wb(2)
-        for head in range(2, HEADS):
+        scatter(0, first[:, HALF:S], HALF, S)
+        store(0)
+        for head in range(1, HEADS):
             weighted = ring.tile([P, S], F32, name="weighted", align_bytes=64)
             keys(head, 0, weighted[:, 0:HALF])
             keys(head, 1, weighted[:, HALF:S])
+            if head + 1 < HEADS:
+                prepare_wb(head + 1)
             scatter(head, weighted[:], 0, S)
             store(head)

@@ -16,6 +16,7 @@ FP8X4 = mybir.dt.float8_e4m3fn_x4
 FP4X4 = mybir.dt.float4_e2m1fn_x4
 MULT = mybir.AluOpType.mult
 IDENTITY = mybir.ActivationFunctionType.Identity
+COPY = mybir.ActivationFunctionType.Copy
 
 P = 128
 PACK = 4
@@ -24,7 +25,9 @@ HALF = S // 2
 CHUNK = 128
 HEADS = N // P
 WB_HEADS = [(0, 1), (1, 4), (4, 8)]
+WB_TAGS = ["wb_raw0", "wa_raw0", "wa_raw1"]
 W0_HEADS = [(0, 2), (2, 8)]
+W0_TAGS = ["w0_codes0", "table1"]
 OUT_BUFS = 3
 FIRST_TABLE_PIECES = 4
 
@@ -36,8 +39,7 @@ def tile_list_adapted_key_cache_kernel(
     with ExitStack() as ctx:
         keep = ctx.enter_context(tc.tile_pool(name="keep", bufs=1))
         ring = ctx.enter_context(tc.tile_pool(name="ring", bufs=3))
-        low_psum = ctx.enter_context(tc.psum_pool(name="low_psum", bufs=4))
-        y_psum = ctx.enter_context(tc.psum_pool(name="y_psum", bufs=4))
+        psum = ctx.enter_context(tc.psum_pool(name="psum", bufs=8))
 
         idx = keep.tile([P, S // 16], U16, name="idx")
         idx2 = keep.tile([P, S // 16], U16, name="idx2")
@@ -49,24 +51,19 @@ def tile_list_adapted_key_cache_kernel(
         wa_bf = [keep.tile([P, PACK, P, PACK], BF16, name="wa_bf%d" % a, align_bytes=64) for a in range(PASSES)]
         wa_codes = [keep.tile([P, R], U32, name="wa_codes%d" % a, align_bytes=64) for a in range(PASSES)]
         wa_planes = [keep.tile([P, R], U8, name="wa_plane%d" % a, align_bytes=64) for a in range(PASSES)]
-        wb_raw = [
-            keep.tile([P, PACK, P * (n1 - n0)], F32, name="wb_raw%d" % n0, align_bytes=64) for n0, n1 in WB_HEADS
-        ]
+        wb_raw = {}
         wb_codes = keep.tile([P, N], U32, name="wb_codes", align_bytes=64)
         wb_plane = keep.tile([P, N], U8, name="wb_plane", align_bytes=64)
         w0_planes = keep.tile([P, PASSES, N // 4], I32, name="w0_planes", align_bytes=64)
-        w0_codes = [
-            keep.tile([P, PASSES, P * (n1 - n0) // 2], I32, name="w0_codes%d" % n0, align_bytes=64) for n0, n1 in W0_HEADS
-        ]
-        wgo_sb = keep.tile([P, S], F32, name="wgo_sb", align_bytes=64)
-        gain = keep.tile([P, S, PACK], F32, name="gain", align_bytes=64)
+        w0_codes = {}
+        gain = keep.tile([P, HALF, PACK], F32, name="gain", align_bytes=64)
         h_bf = [keep.tile([P, HALF, PACK], BF16, name="h_bf%d" % half, align_bytes=64) for half in range(2)]
         h_codes = keep.tile([P, S], U32, name="h_codes", align_bytes=64)
         h_plane = keep.tile([P, S], U8, name="h_plane", align_bytes=64)
         lam_sb = keep.tile([P, PACK], F32, name="lam_sb")
-        strength_sb = keep.tile([P, S // P], F32, name="strength_sb")
-        bk_rows = keep.tile([P, P], F32, name="bk_rows")
-        bk_cols = keep.tile([P, HEADS], F32, name="bk_cols")
+        vector_rows = keep.tile([P, P], F32, name="vector_rows")
+        vector_cols = keep.tile([P, HEADS + S // P], F32, name="vector_cols")
+        scaled = keep.tile([P, PACK, HALF], F32, name="scaled", align_bytes=64)
         ident = keep.tile([P, P], F32, name="ident")
         cache = [keep.tile([P, T2], F32, name="cache%d" % b, align_bytes=64) for b in range(OUT_BUFS)]
 
@@ -87,15 +84,16 @@ def tile_list_adapted_key_cache_kernel(
 
         def load_wb(i):
             n0, n1 = WB_HEADS[i]
+            wb_raw[i] = keep.tile([P, PACK, P * (n1 - n0)], F32, name="wb_raw", tag=WB_TAGS[i], align_bytes=64)
             nc.sync.dma_start(wb_raw[i][:], wb[:, P * n0 : P * n1].rearrange("(p j) c -> p j c", j=PACK))
 
         def load_w0(i):
             n0, n1 = W0_HEADS[i]
+            w0_codes[i] = keep.tile([P, PASSES, P * (n1 - n0) // 2], I32, name="w0_codes", tag=W0_TAGS[i], align_bytes=64)
             words = w0_words.rearrange("a p b -> p a b").bitcast(I32)
             nc.sync.dma_start(w0_codes[i][:], words[:, :, P * n0 // 2 : P * n1 // 2])
 
         nc.sync.dma_start(idx[:], offs)
-        nc.sync.dma_start(strength_sb[:], strength.rearrange("(p c) -> p c", c=S // P))
         nc.sync.dma_start(lam_sb[:], lam.rearrange("(p t) -> p t", t=PACK))
         nc.sync.dma_start(idx2[:], offs2)
         load_table(0, FIRST_TABLE_PIECES)
@@ -104,12 +102,13 @@ def tile_list_adapted_key_cache_kernel(
             nc.scalar.dma_start(scale_rows[32 * q : 32 * q + 4 * PASSES, :], rows)
         load_wa(0)
         load_table(1, 1)
-        load_wa(2)
         load_wa(1)
+        load_wa(2)
         load_table(2, 1)
         load_wb(0)
-        nc.gpsimd.memset(bk_rows[:], 0.0)
-        nc.gpsimd.dma_start(bk_rows[0:HEADS, :], bk.rearrange("(c p) -> c p", p=P))
+        nc.gpsimd.memset(vector_rows[:], 0.0)
+        nc.gpsimd.dma_start(vector_rows[HEADS : HEADS + S // P, :], strength.rearrange("(c p) -> c p", p=P))
+        nc.gpsimd.dma_start(vector_rows[0:HEADS, :], bk.rearrange("(c p) -> c p", p=P))
         make_identity(nc, ident[:])
 
         def gather_words(a, j0, j1):
@@ -124,32 +123,27 @@ def tile_list_adapted_key_cache_kernel(
             rows = w0_scales[:, 4 * q : 4 * q + 4, :].rearrange("a r n -> r a n").bitcast(I32)
             nc.sync.dma_start(w0_planes[32 * q : 32 * q + 4, :, :], rows)
         load_w0(0)
-        nc.sync.dma_start(wgo_sb[:, 0:HALF], wgo[:, 0:HALF])
-        load_wb(1)
-        nc.sync.dma_start(wgo_sb[:, HALF:S], wgo[:, HALF:S])
-        load_w0(1)
-        load_wb(2)
+        wgo_sb = keep.tile([P, S], F32, name="wgo_sb", tag="scale_rows", align_bytes=64)
+        nc.sync.dma_start(wgo_sb[:], wgo)
 
         gather_words(0, 0, S)
 
-        gain_view = gain[:].rearrange("p (q c) t -> p q c t", c=S // P)
-        for b in range(2):
-            spread = y_psum.tile([P, PACK, P], F32, name="y")
-            for c in range(4):
-                col = 4 * b + c
-                nc.tensor.transpose(spread[:, c, :], strength_sb[:, col : col + 1].to_broadcast([P, P]), ident[:])
-            nc.vector.tensor_tensor(
-                gain_view[:, :, 4 * b : 4 * b + 4, :],
-                spread[:].rearrange("p c q -> p q c").unsqueeze(3).broadcast_to([P, P, 4, PACK]),
-                lam_sb[:].unsqueeze(1).unsqueeze(1).broadcast_to([P, P, 4, PACK]),
-                MULT,
-            )
-        bk_t = y_psum.tile([P, PACK, P], F32, name="y")
-        nc.tensor.transpose(bk_t[:, 0, :], bk_rows[:], ident[:])
-        nc.scalar.copy(bk_cols[:], bk_t[:, 0, 0:HEADS])
+        turned = psum.tile([P, P], F32, name="bank")
+        nc.tensor.transpose(turned[:], vector_rows[:], ident[:])
+        nc.scalar.copy(vector_cols[:], turned[:, 0 : HEADS + S // P])
+        spread = psum.tile([P, HALF], F32, name="bank")
+        for c in range(HALF // P):
+            column = vector_cols[:, HEADS + c : HEADS + c + 1]
+            nc.tensor.transpose(spread[:, c * P : (c + 1) * P], column.to_broadcast([P, P]), ident[:])
+        nc.vector.tensor_tensor(
+            gain[:],
+            spread[:].unsqueeze(2).broadcast_to([P, HALF, PACK]),
+            lam_sb[:].unsqueeze(1).broadcast_to([P, HALF, PACK]),
+            MULT,
+        )
 
         for b in range(OUT_BUFS):
-            nc.vector.memset(cache[b][:], 0.0)
+            nc.gpsimd.memset(cache[b][:], 0.0)
 
         def prepare_wa(a):
             nc.scalar.copy(
@@ -163,42 +157,62 @@ def tile_list_adapted_key_cache_kernel(
             )
 
         prepare_wa(0)
+        load_wb(1)
         gather_words(1, 0, S)
-        prepare_wa(2)
+        load_w0(1)
         prepare_wa(1)
+        load_wb(2)
+        prepare_wa(2)
         gather_words(2, 0, HALF)
         gather_words(2, HALF, S)
 
-        def prepare_wb(head):
-            i = [n0 <= head < n1 for n0, n1 in WB_HEADS].index(True)
-            c0 = P * (head - WB_HEADS[i][0])
-            wb_bf = ring.tile([P, P, PACK], BF16, name="wb_bf", align_bytes=64)
+        def prepare_wb(n0, n1, tag):
+            i = [lo <= n0 < hi for lo, hi in WB_HEADS].index(True)
+            c0 = P * (n0 - WB_HEADS[i][0])
+            width = P * (n1 - n0)
+            wb_bf = keep.tile([P, width, PACK], BF16, name="wb_bf", tag=tag, align_bytes=64)
             nc.scalar.copy(
                 wb_bf[:].rearrange("p (c i) j -> p c j i", i=4),
-                wb_raw[i][:, :, c0 : c0 + P].rearrange("p j (c i) -> p c j i", i=4),
+                wb_raw[i][:, :, c0 : c0 + width].rearrange("p j (c i) -> p c j i", i=4),
             )
             nc.vector.quantize_mx(
-                out=wb_codes[:, head * P : (head + 1) * P].bitcast(FP8X4),
-                scales=wb_plane[:, head * P : (head + 1) * P],
+                out=wb_codes[:, n0 * P : n1 * P].bitcast(FP8X4),
+                scales=wb_plane[:, n0 * P : n1 * P],
                 in_=wb_bf[:].rearrange("p c j -> p (c j)"),
             )
 
+        def low_product(dst, a, t, j0, j1, start, stop):
+            nc.tensor.matmul_mx(
+                out=dst,
+                lhsT=wa_codes[a][:, t * P : (t + 1) * P].bitcast(FP8X4),
+                lhsT_scale=wa_planes[a][:, t * P : (t + 1) * P],
+                rhs=v_words[a][:, j0:j1].bitcast(FP8X4),
+                rhs_scale=v_planes[0][4 * a : P, j0 // 4 : j1 // 4].bitcast(U8),
+                start=start,
+                stop=stop,
+            )
+
+        def low_pass(j0, a):
+            for t in range(PACK):
+                last = a == PASSES - 1 and t == PACK - 1
+                low_product(low[j0][:, t, :], a, t, j0, j0 + CHUNK, a == 0 and t == 0, last)
+
+        def low_slot_pass(t, a):
+            low_product(low_slot[t][:], a, t, HALF, S, a == 0, a == PASSES - 1)
+
+        low = {j0: psum.tile([P, PACK, CHUNK], F32, name="bank") for j0 in range(0, HALF, CHUNK)}
+        low_slot = [psum.tile([P, HALF], F32, name="bank") for t in range(PACK)]
+        for a in range(PASSES - 1):
+            for j0 in range(0, HALF, CHUNK):
+                low_pass(j0, a)
+            for t in range(PACK):
+                low_slot_pass(t, a)
+
         def make_h_chunk(j0):
-            low = low_psum.tile([P, PACK, CHUNK], F32, name="low")
-            for a in range(PASSES):
-                for t in range(PACK):
-                    nc.tensor.matmul_mx(
-                        out=low[:, t, :],
-                        lhsT=wa_codes[a][:, t * P : (t + 1) * P].bitcast(FP8X4),
-                        lhsT_scale=wa_planes[a][:, t * P : (t + 1) * P],
-                        rhs=v_words[a][:, j0 : j0 + CHUNK].bitcast(FP8X4),
-                        rhs_scale=v_planes[0][4 * a : P, j0 // 4 : (j0 + CHUNK) // 4].bitcast(U8),
-                        start=(a == 0 and t == 0),
-                        stop=(a == PASSES - 1 and t == PACK - 1),
-                    )
+            low_pass(j0, PASSES - 1)
             nc.vector.tensor_tensor(
                 h_bf[j0 // HALF][:, j0 % HALF : j0 % HALF + CHUNK, :],
-                low[:].rearrange("p t j -> p j t"),
+                low[j0][:].rearrange("p t j -> p j t"),
                 gain[:, j0 : j0 + CHUNK, :],
                 MULT,
             )
@@ -210,17 +224,35 @@ def tile_list_adapted_key_cache_kernel(
                 in_=h_bf[j0 // HALF][:, j0 % HALF : j0 % HALF + j1 - j0, :].rearrange("p j t -> p (j t)"),
             )
 
-        def make_h_half(half):
-            for j0 in range(half * HALF, (half + 1) * HALF, CHUNK):
-                make_h_chunk(j0)
-            quantize_h(half * HALF, (half + 1) * HALF)
+        def scale_by_lam():
+            for t in range(PACK):
+                low_slot_pass(t, PASSES - 1)
+                nc.scalar.activation(scaled[:, t, :], low_slot[t][:], COPY, scale=lam_sb[:, t : t + 1])
+
+        def scale_by_strength(c, pairs):
+            by_entry = psum.tile([P, PACK, P], F32, name="bank")
+            for t in range(PACK):
+                nc.tensor.transpose(by_entry[:, t, :], scaled[:, t, c * P : (c + 1) * P], ident[:])
+            col = HEADS + HALF // P + c
+            nc.scalar.activation(
+                pairs, by_entry[:].rearrange("p (u e) m -> p u m e", u=2), COPY, scale=vector_cols[:, col : col + 1]
+            )
+
+        def turn_back(c0, both):
+            back = psum.tile([P, 2, 2, P], F32, name="bank")
+            for i in range(2):
+                words = both[:, i].rearrange("p u m e -> p (u m e)").bitcast(F32)
+                for u in range(2):
+                    nc.tensor.transpose(back[:, i, u, :], words[:, u * P : (u + 1) * P], ident[:])
+            dst = h_bf[1][:, c0 * P : (c0 + 2) * P, :].rearrange("p j t -> p (j t)").bitcast(F32)
+            nc.scalar.copy(dst.rearrange("p (i j u) -> p i j u", i=2, u=2), back[:].rearrange("p i u j -> p i j u"))
 
         def keys(head, half, dst):
             j0, j1 = half * HALF, (half + 1) * HALF
             i = [n0 <= head < n1 for n0, n1 in W0_HEADS].index(True)
             c0 = P * (head - W0_HEADS[i][0]) // 2
             n0, n1 = head * P, (head + 1) * P
-            y = y_psum.tile([P, HALF], F32, name="y")
+            y = psum.tile([P, HALF], F32, name="bank")
             for a in range(PASSES):
                 nc.tensor.matmul_mx(
                     out=y[:],
@@ -240,7 +272,7 @@ def tile_list_adapted_key_cache_kernel(
                 start=False,
                 stop=True,
             )
-            nc.scalar.activation(dst, y[:], IDENTITY, bias=bk_cols[:, head : head + 1])
+            nc.scalar.activation(dst, y[:], IDENTITY, bias=vector_cols[:, head : head + 1])
 
         def scatter(head, values, j0, j1):
             window = cache[head % OUT_BUFS][:].indirect(idx2[:, j0 // 16 : j1 // 16])
@@ -249,21 +281,39 @@ def tile_list_adapted_key_cache_kernel(
         def store(head):
             nc.sync.dma_start(out[head * P : (head + 1) * P, :], cache[head % OUT_BUFS][:])
 
-        prepare_wb(0)
-        make_h_half(0)
-        first = ring.tile([P, S], F32, name="weighted", align_bytes=64)
-        keys(0, 0, first[:, 0:HALF])
-        make_h_half(1)
-        scatter(0, first[:, 0:HALF], 0, HALF)
-        keys(0, 1, first[:, HALF:S])
-        prepare_wb(1)
-        scatter(0, first[:, HALF:S], HALF, S)
-        store(0)
-        for head in range(1, HEADS):
+        prepare_wb(0, 1, "wb_bf0")
+        for j0 in range(0, HALF, CHUNK):
+            make_h_chunk(j0)
+        quantize_h(0, HALF)
+        scale_by_lam()
+        early = [ring.tile([P, S], F32, name="weighted", align_bytes=64) for head in range(2)]
+        keys(0, 0, early[0][:, 0:HALF])
+        prepare_wb(1, 3, "wb_bf1")
+        keys(1, 0, early[1][:, 0:HALF])
+        paired = [keep.tile([P, 2, 2, P, 2], BF16, name="pairs%d" % i, align_bytes=64) for i in range(2)]
+        for c in range(HALF // P):
+            scale_by_strength(c, paired[c // 2][:, c % 2])
+        for i in range(2):
+            turn_back(2 * i, paired[i])
+        scatter(0, early[0][:, 0:HALF], 0, HALF)
+        scatter(1, early[1][:, 0:HALF], 0, HALF)
+        quantize_h(HALF, S)
+        third = keep.tile([P, HALF], F32, name="third", tag="pairs1", align_bytes=64)
+        keys(2, 0, third[:])
+        scatter(2, third[:], 0, HALF)
+        for head in range(2):
+            keys(head, 1, early[head][:, HALF:S])
+            scatter(head, early[head][:, HALF:S], HALF, S)
+            store(head)
+        prepare_wb(3, 4, "pairs1")
+        prepare_wb(4, 8, "h_bf1")
+        rest = ring.tile([P, S], F32, name="weighted", align_bytes=64)
+        keys(2, 1, rest[:, HALF:S])
+        scatter(2, rest[:, HALF:S], HALF, S)
+        store(2)
+        for head in range(3, HEADS):
             weighted = ring.tile([P, S], F32, name="weighted", align_bytes=64)
             keys(head, 0, weighted[:, 0:HALF])
             keys(head, 1, weighted[:, HALF:S])
-            if head + 1 < HEADS:
-                prepare_wb(head + 1)
             scatter(head, weighted[:], 0, S)
             store(head)

@@ -22,9 +22,10 @@ P = 128
 PACK = 4
 PASSES = K // (P * PACK)
 HALF = S // 2
+QUARTER = S // 4
 CHUNK = 128
 HEADS = N // P
-WB_HEADS = [(0, 1), (1, 4), (4, 8)]
+WB_HEADS = [(0, 2), (2, 4), (4, 8)]
 WB_TAGS = ["wb_raw0", "wa_raw0", "wa_raw1"]
 W0_HEADS = [(0, 2), (2, 8)]
 W0_TAGS = ["w0_codes0", "table1"]
@@ -247,22 +248,23 @@ def tile_list_adapted_key_cache_kernel(
             dst = h_bf[1][:, c0 * P : (c0 + 2) * P, :].rearrange("p j t -> p (j t)").bitcast(F32)
             nc.scalar.copy(dst.rearrange("p (i j u) -> p i j u", i=2, u=2), back[:].rearrange("p i u j -> p i j u"))
 
-        def keys(head, half, dst):
-            j0, j1 = half * HALF, (half + 1) * HALF
+        def keys(head, j0, j1, dst):
             i = [n0 <= head < n1 for n0, n1 in W0_HEADS].index(True)
             c0 = P * (head - W0_HEADS[i][0]) // 2
             n0, n1 = head * P, (head + 1) * P
-            y = psum.tile([P, HALF], F32, name="bank")
+            y = psum.tile([P, j1 - j0], F32, name="bank")
+            width = HALF if j1 - j0 == HALF else CHUNK
             for a in range(PASSES):
-                nc.tensor.matmul_mx(
-                    out=y[:],
-                    lhsT=w0_codes[i][:, a, c0 : c0 + P // 2].bitcast(U8).bitcast(FP4X4),
-                    lhsT_scale=w0_planes[:, a, n0 // 4 : n1 // 4].bitcast(U8),
-                    rhs=v_words[a][:, j0:j1].bitcast(FP8X4),
-                    rhs_scale=v_planes[a][:, j0 // 4 : j1 // 4].bitcast(U8),
-                    start=(a == 0),
-                    stop=False,
-                )
+                for lo in range(j0, j1, width):
+                    nc.tensor.matmul_mx(
+                        out=y[:, lo - j0 : lo - j0 + width],
+                        lhsT=w0_codes[i][:, a, c0 : c0 + P // 2].bitcast(U8).bitcast(FP4X4),
+                        lhsT_scale=w0_planes[:, a, n0 // 4 : n1 // 4].bitcast(U8),
+                        rhs=v_words[a][:, lo : lo + width].bitcast(FP8X4),
+                        rhs_scale=v_planes[a][:, lo // 4 : (lo + width) // 4].bitcast(U8),
+                        start=(a == 0 and lo == j0),
+                        stop=False,
+                    )
             nc.tensor.matmul_mx(
                 out=y[:],
                 lhsT=wb_codes[:, n0:n1].bitcast(FP8X4),
@@ -281,39 +283,43 @@ def tile_list_adapted_key_cache_kernel(
         def store(head):
             nc.sync.dma_start(out[head * P : (head + 1) * P, :], cache[head % OUT_BUFS][:])
 
-        prepare_wb(0, 1, "wb_bf0")
-        for j0 in range(0, HALF, CHUNK):
-            make_h_chunk(j0)
-        quantize_h(0, HALF)
-        scale_by_lam()
+        prepare_wb(0, 2, "wb_bf0")
         early = [ring.tile([P, S], F32, name="weighted", align_bytes=64) for head in range(2)]
-        keys(0, 0, early[0][:, 0:HALF])
-        prepare_wb(1, 3, "wb_bf1")
-        keys(1, 0, early[1][:, 0:HALF])
+        for j0 in range(0, HALF, QUARTER):
+            make_h_chunk(j0)
+            make_h_chunk(j0 + CHUNK)
+            quantize_h(j0, j0 + QUARTER)
+            if j0 == 0:
+                keys(0, 0, QUARTER, early[0][:, 0:QUARTER])
+        scale_by_lam()
+        keys(1, 0, HALF, early[1][:, 0:HALF])
+        keys(0, QUARTER, HALF, early[0][:, QUARTER:HALF])
+        prepare_wb(2, 3, "wb_bf1")
         paired = [keep.tile([P, 2, 2, P, 2], BF16, name="pairs%d" % i, align_bytes=64) for i in range(2)]
         for c in range(HALF // P):
             scale_by_strength(c, paired[c // 2][:, c % 2])
         for i in range(2):
             turn_back(2 * i, paired[i])
-        scatter(0, early[0][:, 0:HALF], 0, HALF)
+        scatter(0, early[0][:, 0:QUARTER], 0, QUARTER)
         scatter(1, early[1][:, 0:HALF], 0, HALF)
+        scatter(0, early[0][:, QUARTER:HALF], QUARTER, HALF)
         quantize_h(HALF, S)
         third = keep.tile([P, HALF], F32, name="third", tag="pairs1", align_bytes=64)
-        keys(2, 0, third[:])
+        keys(2, 0, HALF, third[:])
         scatter(2, third[:], 0, HALF)
         for head in range(2):
-            keys(head, 1, early[head][:, HALF:S])
+            keys(head, HALF, S, early[head][:, HALF:S])
             scatter(head, early[head][:, HALF:S], HALF, S)
             store(head)
         prepare_wb(3, 4, "pairs1")
         prepare_wb(4, 8, "h_bf1")
         rest = ring.tile([P, S], F32, name="weighted", align_bytes=64)
-        keys(2, 1, rest[:, HALF:S])
+        keys(2, HALF, S, rest[:, HALF:S])
         scatter(2, rest[:, HALF:S], HALF, S)
         store(2)
         for head in range(3, HEADS):
             weighted = ring.tile([P, S], F32, name="weighted", align_bytes=64)
-            keys(head, 0, weighted[:, 0:HALF])
-            keys(head, 1, weighted[:, HALF:S])
+            keys(head, 0, HALF, weighted[:, 0:HALF])
+            keys(head, HALF, S, weighted[:, HALF:S])
             scatter(head, weighted[:], 0, S)
             store(head)

@@ -30,6 +30,7 @@ WB_TAGS = ["wb_raw0", "wa_raw0", "wa_raw1"]
 W0_HEADS = [(0, 2), (2, 8)]
 W0_TAGS = ["w0_codes0", "table1"]
 OUT_BUFS = 3
+SHIFT_ROWS = 112
 FIRST_TABLE_PIECES = 4
 
 
@@ -100,7 +101,7 @@ def tile_list_adapted_key_cache_kernel(
         load_table(0, FIRST_TABLE_PIECES)
         for q in range(4):
             rows = tab_scales[:, 4 * q : 4 * q + 4, :].bitcast(I32)
-            nc.scalar.dma_start(scale_rows[32 * q : 32 * q + 4 * PASSES, :], rows)
+            nc.gpsimd.dma_start(scale_rows[32 * q : 32 * q + 4 * PASSES, :], rows)
         load_wa(0)
         load_table(1, 1)
         load_wa(1)
@@ -119,10 +120,10 @@ def tile_list_adapted_key_cache_kernel(
 
         nc.vector.tensor_copy(v_planes[0][:].bitcast(U8), scale_rows[:].bitcast(U8).indirect(idx[:]))
         for a in range(1, PASSES):
-            nc.sync.dma_start(v_planes[a][0 : P - 4 * a, :], v_planes[0][4 * a : P, :])
-        for q in range(4):
-            rows = w0_scales[:, 4 * q : 4 * q + 4, :].rearrange("a r n -> r a n").bitcast(I32)
-            nc.sync.dma_start(w0_planes[32 * q : 32 * q + 4, :, :], rows)
+            nc.sync.dma_start(v_planes[a][0:SHIFT_ROWS, :], v_planes[0][4 * a : 4 * a + SHIFT_ROWS, :])
+        for r in range(4):
+            rows = w0_scales[:, r:16:4, :].rearrange("a q n -> q a n").bitcast(I32)
+            nc.sync.dma_start(w0_planes[r:P:32, :, :], rows)
         load_w0(0)
         wgo_sb = keep.tile([P, S], F32, name="wgo_sb", tag="scale_rows", align_bytes=64)
         nc.sync.dma_start(wgo_sb[:], wgo)

@@ -101,7 +101,7 @@ def tile_list_adapted_key_cache_kernel(
         load_table(0, FIRST_TABLE_PIECES)
         for q in range(4):
             rows = tab_scales[:, 4 * q : 4 * q + 4, :].bitcast(I32)
-            nc.gpsimd.dma_start(scale_rows[32 * q : 32 * q + 4 * PASSES, :], rows)
+            nc.scalar.dma_start(scale_rows[32 * q : 32 * q + 4 * PASSES, :], rows)
         load_wa(0)
         load_table(1, 1)
         load_wa(1)
@@ -145,7 +145,7 @@ def tile_list_adapted_key_cache_kernel(
         )
 
         for b in range(OUT_BUFS):
-            nc.gpsimd.memset(cache[b][:], 0.0)
+            nc.vector.memset(cache[b][:], 0.0)
 
         def prepare_wa(a):
             nc.scalar.copy(

@@ -47,7 +47,7 @@ def tile_list_adapted_key_cache_kernel(
         idx2 = keep.tile([P, S // 16], U16, name="idx2")
         scale_rows = keep.tile([P, T // 4], I32, name="scale_rows", align_bytes=64)
         table = [keep.tile([P, T], I32, name="table%d" % a, align_bytes=64) for a in range(PASSES)]
-        v_planes = [keep.tile([P, S // 4], I32, name="v_plane%d" % a, align_bytes=64) for a in range(PASSES)]
+        v_planes = {a: keep.tile([P, S // 4], I32, name="v_plane%d" % a, align_bytes=64) for a in range(1, PASSES)}
         v_words = [keep.tile([P, S], I32, name="v_words%d" % a, align_bytes=64) for a in range(PASSES)]
         wa_raw = [keep.tile([P, PACK * R], F32, name="wa_raw%d" % a, align_bytes=64) for a in range(PASSES)]
         wa_bf = [keep.tile([P, PACK, P, PACK], BF16, name="wa_bf%d" % a, align_bytes=64) for a in range(PASSES)]
@@ -69,7 +69,8 @@ def tile_list_adapted_key_cache_kernel(
         ident = keep.tile([P, P], F32, name="ident")
         cache = [keep.tile([P, T2], F32, name="cache%d" % b, align_bytes=64) for b in range(OUT_BUFS)]
 
-        nc.vector.memset(scale_rows[:], 0)
+        nc.gpsimd.memset(vector_rows[:], 0.0)
+        nc.gpsimd.memset(scale_rows[:], 0)
         for a in range(1, PASSES):
             nc.vector.memset(v_planes[a][:], 0)
         nc.vector.memset(w0_planes[:], 0)
@@ -95,6 +96,8 @@ def tile_list_adapted_key_cache_kernel(
             words = w0_words.rearrange("a p b -> p a b").bitcast(I32)
             nc.sync.dma_start(w0_codes[i][:], words[:, :, P * n0 // 2 : P * n1 // 2])
 
+        nc.scalar.dma_start(vector_rows[HEADS : HEADS + S // P, :], strength.rearrange("(c p) -> c p", p=P))
+        nc.scalar.dma_start(vector_rows[0:HEADS, :], bk.rearrange("(c p) -> c p", p=P))
         nc.sync.dma_start(idx[:], offs)
         nc.sync.dma_start(lam_sb[:], lam.rearrange("(p t) -> p t", t=PACK))
         nc.sync.dma_start(idx2[:], offs2)
@@ -108,9 +111,6 @@ def tile_list_adapted_key_cache_kernel(
         load_wa(2)
         load_table(2, 1)
         load_wb(0)
-        nc.gpsimd.memset(vector_rows[:], 0.0)
-        nc.gpsimd.dma_start(vector_rows[HEADS : HEADS + S // P, :], strength.rearrange("(c p) -> c p", p=P))
-        nc.gpsimd.dma_start(vector_rows[0:HEADS, :], bk.rearrange("(c p) -> c p", p=P))
         make_identity(nc, ident[:])
 
         def gather_words(a, j0, j1):
@@ -118,6 +118,8 @@ def tile_list_adapted_key_cache_kernel(
                 v_words[a][:, j0:j1].bitcast(U32), table[a][:].bitcast(U32).indirect(idx[:, j0 // 16 : j1 // 16])
             )
 
+        gather_words(0, 0, S)
+        v_planes[0] = keep.tile([P, S // 4], I32, name="v_plane0", tag="table0", align_bytes=64)
         nc.vector.tensor_copy(v_planes[0][:].bitcast(U8), scale_rows[:].bitcast(U8).indirect(idx[:]))
         for a in range(1, PASSES):
             nc.sync.dma_start(v_planes[a][0:SHIFT_ROWS, :], v_planes[0][4 * a : 4 * a + SHIFT_ROWS, :])
@@ -127,8 +129,6 @@ def tile_list_adapted_key_cache_kernel(
         load_w0(0)
         wgo_sb = keep.tile([P, S], F32, name="wgo_sb", tag="scale_rows", align_bytes=64)
         nc.sync.dma_start(wgo_sb[:], wgo)
-
-        gather_words(0, 0, S)
 
         turned = psum.tile([P, P], F32, name="bank")
         nc.tensor.transpose(turned[:], vector_rows[:], ident[:])

@@ -30,7 +30,7 @@ WB_TAGS = ["wb_raw0", "wa_raw0", "wa_raw1"]
 W0_HEADS = [(0, 2), (2, 8)]
 W0_TAGS = ["w0_codes0", "table1"]
 OUT_BUFS = 3
-SHIFT_ROWS = 112
+SHIFT_ROWS = 100
 FIRST_TABLE_PIECES = 4
 
 

@@ -132,7 +132,7 @@ def tile_list_adapted_key_cache_kernel(
 
         turned = psum.tile([P, P], F32, name="bank")
         nc.tensor.transpose(turned[:], vector_rows[:], ident[:])
-        nc.scalar.copy(vector_cols[:], turned[:, 0 : HEADS + S // P])
+        nc.scalar.activation(vector_cols[:], turned[:, 0 : HEADS + S // P], COPY)
         spread = psum.tile([P, HALF], F32, name="bank")
         for c in range(HALF // P):
             column = vector_cols[:, HEADS + c : HEADS + c + 1]

@@ -25,9 +25,9 @@ HALF = S // 2
 QUARTER = S // 4
 CHUNK = 128
 HEADS = N // P
-WB_HEADS = [(0, 2), (2, 4), (4, 8)]
-WB_TAGS = ["wb_raw0", "wa_raw0", "wa_raw1"]
-W0_HEADS = [(0, 2), (2, 8)]
+WB_HEADS = [(0, 3), (3, 8)]
+WB_TAGS = ["wb_raw0", "wa_raw0"]
+W0_HEADS = [(0, 3), (3, 8)]
 W0_TAGS = ["w0_codes0", "table1"]
 OUT_BUFS = 3
 SHIFT_ROWS = 100
@@ -104,7 +104,7 @@ def tile_list_adapted_key_cache_kernel(
         load_table(0, FIRST_TABLE_PIECES)
         for q in range(4):
             rows = tab_scales[:, 4 * q : 4 * q + 4, :].bitcast(I32)
-            nc.scalar.dma_start(scale_rows[32 * q : 32 * q + 4 * PASSES, :], rows)
+            nc.sync.dma_start(scale_rows[32 * q : 32 * q + 4 * PASSES, :], rows)
         load_wa(0)
         load_table(1, 1)
         load_wa(1)
@@ -163,7 +163,6 @@ def tile_list_adapted_key_cache_kernel(
         gather_words(1, 0, S)
         load_w0(1)
         prepare_wa(1)
-        load_wb(2)
         prepare_wa(2)
         gather_words(2, 0, HALF)
         gather_words(2, HALF, S)
@@ -285,6 +284,7 @@ def tile_list_adapted_key_cache_kernel(
             nc.sync.dma_start(out[head * P : (head + 1) * P, :], cache[head % OUT_BUFS][:])
 
         prepare_wb(0, 2, "wb_bf0")
+        prepare_wb(2, 3, "wb_bf1")
         early = [ring.tile([P, S], F32, name="weighted", align_bytes=64) for head in range(2)]
         for j0 in range(0, HALF, QUARTER):
             make_h_chunk(j0)
@@ -295,7 +295,6 @@ def tile_list_adapted_key_cache_kernel(
         scale_by_lam()
         keys(1, 0, HALF, early[1][:, 0:HALF])
         keys(0, QUARTER, HALF, early[0][:, QUARTER:HALF])
-        prepare_wb(2, 3, "wb_bf1")
         paired = [keep.tile([P, 2, 2, P, 2], BF16, name="pairs%d" % i, align_bytes=64) for i in range(2)]
         for c in range(HALF // P):
             scale_by_strength(c, paired[c // 2][:, c % 2])

@@ -104,7 +104,7 @@ def tile_list_adapted_key_cache_kernel(
         load_table(0, FIRST_TABLE_PIECES)
         for q in range(4):
             rows = tab_scales[:, 4 * q : 4 * q + 4, :].bitcast(I32)
-            nc.sync.dma_start(scale_rows[32 * q : 32 * q + 4 * PASSES, :], rows)
+            nc.scalar.dma_start(scale_rows[32 * q : 32 * q + 4 * PASSES, :], rows)
         load_wa(0)
         load_table(1, 1)
         load_wa(1)

@@ -25,9 +25,9 @@ HALF = S // 2
 QUARTER = S // 4
 CHUNK = 128
 HEADS = N // P
-WB_HEADS = [(0, 3), (3, 8)]
-WB_TAGS = ["wb_raw0", "wa_raw0"]
-W0_HEADS = [(0, 3), (3, 8)]
+WB_HEADS = [(0, 2), (2, 3), (3, 8)]
+WB_TAGS = ["wb_raw0", "wa_raw0", "wa_raw1"]
+W0_HEADS = [(0, 2), (2, 8)]
 W0_TAGS = ["w0_codes0", "table1"]
 OUT_BUFS = 3
 SHIFT_ROWS = 100
@@ -163,6 +163,7 @@ def tile_list_adapted_key_cache_kernel(
         gather_words(1, 0, S)
         load_w0(1)
         prepare_wa(1)
+        load_wb(2)
         prepare_wa(2)
         gather_words(2, 0, HALF)
         gather_words(2, HALF, S)

@@ -49,7 +49,8 @@ def tile_list_adapted_key_cache_kernel(
         table = [keep.tile([P, T], I32, name="table%d" % a, align_bytes=64) for a in range(PASSES)]
         v_planes = {a: keep.tile([P, S // 4], I32, name="v_plane%d" % a, align_bytes=64) for a in range(1, PASSES)}
         v_words = [keep.tile([P, S], I32, name="v_words%d" % a, align_bytes=64) for a in range(PASSES)]
-        wa_raw = [keep.tile([P, PACK * R], F32, name="wa_raw%d" % a, align_bytes=64) for a in range(PASSES)]
+        wa_raw = [keep.tile([P, PACK * R], F32, name="wa_raw%d" % a, align_bytes=64) for a in range(PASSES - 1)]
+        wa_last = [keep.tile([P, PACK, R // 2], F32, name="wa_last%d" % i, align_bytes=64) for i in range(2)]
         wa_bf = [keep.tile([P, PACK, P, PACK], BF16, name="wa_bf%d" % a, align_bytes=64) for a in range(PASSES)]
         wa_codes = [keep.tile([P, R], U32, name="wa_codes%d" % a, align_bytes=64) for a in range(PASSES)]
         wa_planes = [keep.tile([P, R], U8, name="wa_plane%d" % a, align_bytes=64) for a in range(PASSES)]
@@ -85,6 +86,10 @@ def tile_list_adapted_key_cache_kernel(
             rows = wa[a * P * PACK : (a + 1) * P * PACK, :]
             nc.sync.dma_start(wa_raw[a][:], rows.rearrange("(p j) c -> p (j c)", j=PACK))
 
+        def load_wa_last(i):
+            rows = wa[(PASSES - 1) * P * PACK :, i * R // 2 : (i + 1) * R // 2]
+            nc.sync.dma_start(wa_last[i][:], rows.rearrange("(p j) c -> p j c", j=PACK))
+
         def load_wb(i):
             n0, n1 = WB_HEADS[i]
             wb_raw[i] = keep.tile([P, PACK, P * (n1 - n0)], F32, name="wb_raw", tag=WB_TAGS[i], align_bytes=64)
@@ -108,8 +113,9 @@ def tile_list_adapted_key_cache_kernel(
         load_wa(0)
         load_table(1, 1)
         load_wa(1)
-        load_wa(2)
         load_table(2, 1)
+        load_wa_last(0)
+        load_wa_last(1)
         load_wb(0)
         make_identity(nc, ident[:])
 
@@ -164,9 +170,24 @@ def tile_list_adapted_key_cache_kernel(
         load_w0(1)
         prepare_wa(1)
         load_wb(2)
-        prepare_wa(2)
-        gather_words(2, 0, HALF)
-        gather_words(2, HALF, S)
+        gather_words(2, 0, S)
+        last_bf = wa_bf[PASSES - 1]
+
+        def round_last(copy, i, t0, t1):
+            copy(
+                last_bf[:, t0:t1, i * P // 2 : (i + 1) * P // 2, :].rearrange("p t m j -> p m j t"),
+                wa_last[i][:].rearrange("p j (m t) -> p m j t", t=PACK)[:, :, :, t0:t1],
+            )
+
+        round_last(nc.scalar.copy, 0, 0, PACK)
+        round_last(nc.vector.tensor_copy, 1, 0, 2)
+        round_last(nc.scalar.copy, 1, 2, PACK)
+        for t0 in range(0, PACK, 2):
+            nc.vector.quantize_mx(
+                out=wa_codes[PASSES - 1][:, t0 * P : (t0 + 2) * P].bitcast(FP8X4),
+                scales=wa_planes[PASSES - 1][:, t0 * P : (t0 + 2) * P],
+                in_=last_bf[:, t0 : t0 + 2].rearrange("p t m j -> p (t m j)"),
+            )
 
         def prepare_wb(n0, n1, tag):
             i = [lo <= n0 < hi for lo, hi in WB_HEADS].index(True)

@@ -26,12 +26,13 @@ QUARTER = S // 4
 CHUNK = 128
 HEADS = N // P
 WB_HEADS = [(0, 2), (2, 3), (3, 8)]
-WB_TAGS = ["wb_raw0", "wa_raw0", "wa_raw1"]
+WB_TAGS = [None, "wa_raw0", "wa_raw1"]
 W0_HEADS = [(0, 2), (2, 8)]
-W0_TAGS = ["w0_codes0", "table1"]
+W0_TAGS = [None, "table1"]
 OUT_BUFS = 3
-SHIFT_ROWS = 100
-FIRST_TABLE_PIECES = 4
+TABLE_BYTES = 4 * T
+WINDOW_AT = TABLE_BYTES - 64
+FIRST_TABLE_AT = TABLE_BYTES + 4096
 
 
 def tile_list_adapted_key_cache_kernel(
@@ -40,24 +41,33 @@ def tile_list_adapted_key_cache_kernel(
     nc = tc.nc
     with ExitStack() as ctx:
         keep = ctx.enter_context(tc.tile_pool(name="keep", bufs=1))
+        stage = ctx.enter_context(tc.tile_pool(name="stage", bufs=1))
         ring = ctx.enter_context(tc.tile_pool(name="ring", bufs=3))
         psum = ctx.enter_context(tc.psum_pool(name="psum", bufs=8))
 
         idx = keep.tile([P, S // 16], U16, name="idx")
         idx2 = keep.tile([P, S // 16], U16, name="idx2")
-        scale_rows = keep.tile([P, T // 4], I32, name="scale_rows", align_bytes=64)
-        table = [keep.tile([P, T], I32, name="table%d" % a, align_bytes=64) for a in range(PASSES)]
-        v_planes = {a: keep.tile([P, S // 4], I32, name="v_plane%d" % a, align_bytes=64) for a in range(1, PASSES)}
+        scale_rows = stage.tile([P, T // 4], I32, name="scale_rows", align_bytes=64, offset=WINDOW_AT)
+        table = [
+            stage.tile([P, T], I32, name="table0", align_bytes=64, offset=FIRST_TABLE_AT),
+            keep.tile([P, T], I32, name="table1", align_bytes=64),
+            stage.tile([P, T], I32, name="table2", align_bytes=64, offset=0),
+        ]
+        picked_rows = keep.tile([P, S // 4], I32, name="picked_rows", align_bytes=64)
+        v_planes = [keep.tile([P, S // 4], I32, name="v_plane%d" % a, align_bytes=64) for a in range(PASSES)]
         v_words = [keep.tile([P, S], I32, name="v_words%d" % a, align_bytes=64) for a in range(PASSES)]
         wa_raw = [keep.tile([P, PACK * R], F32, name="wa_raw%d" % a, align_bytes=64) for a in range(PASSES - 1)]
-        wa_last = [keep.tile([P, PACK, R // 2], F32, name="wa_last%d" % i, align_bytes=64) for i in range(2)]
+        wa_last = [
+            stage.tile([P, PACK, R // 2], F32, name="wa_last%d" % i, align_bytes=64, offset=TABLE_BYTES + 4096 * i)
+            for i in range(2)
+        ]
         wa_bf = [keep.tile([P, PACK, P, PACK], BF16, name="wa_bf%d" % a, align_bytes=64) for a in range(PASSES)]
         wa_codes = [keep.tile([P, R], U32, name="wa_codes%d" % a, align_bytes=64) for a in range(PASSES)]
         wa_planes = [keep.tile([P, R], U8, name="wa_plane%d" % a, align_bytes=64) for a in range(PASSES)]
         wb_raw = {}
         wb_codes = keep.tile([P, N], U32, name="wb_codes", align_bytes=64)
         wb_plane = keep.tile([P, N], U8, name="wb_plane", align_bytes=64)
-        w0_planes = keep.tile([P, PASSES, N // 4], I32, name="w0_planes", align_bytes=64)
+        w0_planes = stage.tile([P, PASSES, N // 4], I32, name="w0_planes", align_bytes=64, offset=FIRST_TABLE_AT + 13824)
         w0_codes = {}
         gain = keep.tile([P, HALF, PACK], F32, name="gain", align_bytes=64)
         h_bf = [keep.tile([P, HALF, PACK], BF16, name="h_bf%d" % half, align_bytes=64) for half in range(2)]
@@ -72,9 +82,8 @@ def tile_list_adapted_key_cache_kernel(
 
         nc.gpsimd.memset(vector_rows[:], 0.0)
         nc.gpsimd.memset(scale_rows[:], 0)
-        for a in range(1, PASSES):
+        for a in range(PASSES):
             nc.vector.memset(v_planes[a][:], 0)
-        nc.vector.memset(w0_planes[:], 0)
 
         def load_table(a, pieces):
             words = tab_words[a].rearrange("p t i -> p (t i)").bitcast(I32)
@@ -92,31 +101,34 @@ def tile_list_adapted_key_cache_kernel(
 
         def load_wb(i):
             n0, n1 = WB_HEADS[i]
-            wb_raw[i] = keep.tile([P, PACK, P * (n1 - n0)], F32, name="wb_raw", tag=WB_TAGS[i], align_bytes=64)
+            if i == 0:
+                wb_raw[i] = stage.tile([P, PACK, P * (n1 - n0)], F32, name="wb_raw0", align_bytes=64, offset=FIRST_TABLE_AT + 4096)
+            else:
+                wb_raw[i] = keep.tile([P, PACK, P * (n1 - n0)], F32, name="wb_raw", tag=WB_TAGS[i], align_bytes=64)
             nc.sync.dma_start(wb_raw[i][:], wb[:, P * n0 : P * n1].rearrange("(p j) c -> p j c", j=PACK))
 
         def load_w0(i):
             n0, n1 = W0_HEADS[i]
-            w0_codes[i] = keep.tile([P, PASSES, P * (n1 - n0) // 2], I32, name="w0_codes", tag=W0_TAGS[i], align_bytes=64)
+            shape = [P, PASSES, P * (n1 - n0) // 2]
+            if i == 0:
+                w0_codes[i] = stage.tile(shape, I32, name="w0_codes0", align_bytes=64, offset=FIRST_TABLE_AT + 12288)
+            else:
+                w0_codes[i] = keep.tile(shape, I32, name="w0_codes", tag=W0_TAGS[i], align_bytes=64)
             words = w0_words.rearrange("a p b -> p a b").bitcast(I32)
             nc.sync.dma_start(w0_codes[i][:], words[:, :, P * n0 // 2 : P * n1 // 2])
 
-        nc.scalar.dma_start(vector_rows[HEADS : HEADS + S // P, :], strength.rearrange("(c p) -> c p", p=P))
-        nc.scalar.dma_start(vector_rows[0:HEADS, :], bk.rearrange("(c p) -> c p", p=P))
         nc.sync.dma_start(idx[:], offs)
         nc.sync.dma_start(lam_sb[:], lam.rearrange("(p t) -> p t", t=PACK))
         nc.sync.dma_start(idx2[:], offs2)
-        load_table(0, FIRST_TABLE_PIECES)
-        for q in range(4):
-            rows = tab_scales[:, 4 * q : 4 * q + 4, :].bitcast(I32)
-            nc.scalar.dma_start(scale_rows[32 * q : 32 * q + 4 * PASSES, :], rows)
+        all_rows = tab_scales.rearrange("a q n -> (a q) n").bitcast(I32)
+        nc.sync.dma_start(scale_rows[0:P:4, :], all_rows[0:32, :])
+        nc.sync.dma_start(scale_rows[2:P:8, :], all_rows[32:48, :])
+        load_table(0, 1)
+        nc.scalar.dma_start(vector_rows[HEADS : HEADS + S // P, :], strength.rearrange("(c p) -> c p", p=P))
+        nc.scalar.dma_start(vector_rows[0:HEADS, :], bk.rearrange("(c p) -> c p", p=P))
         load_wa(0)
-        load_table(1, 1)
         load_wa(1)
-        load_table(2, 1)
-        load_wa_last(0)
-        load_wa_last(1)
-        load_wb(0)
+        load_table(1, 1)
         make_identity(nc, ident[:])
 
         def gather_words(a, j0, j1):
@@ -124,16 +136,32 @@ def tile_list_adapted_key_cache_kernel(
                 v_words[a][:, j0:j1].bitcast(U32), table[a][:].bitcast(U32).indirect(idx[:, j0 // 16 : j1 // 16])
             )
 
+        def move_rows(a, q):
+            if a < 2:
+                rows = picked_rows[64 * a + 16 * q : 64 * a + 16 * q + 16 : 4, :]
+            else:
+                rows = picked_rows[32 * q + 2 : 32 * q + 32 : 8, :]
+            nc.sync.dma_start(v_planes[a][32 * q : 32 * q + 4, :], rows)
+
+        nc.vector.tensor_copy(picked_rows[:].bitcast(U8), scale_rows[:].bitcast(U8).indirect(idx[:]))
         gather_words(0, 0, S)
-        v_planes[0] = keep.tile([P, S // 4], I32, name="v_plane0", tag="table0", align_bytes=64)
-        nc.vector.tensor_copy(v_planes[0][:].bitcast(U8), scale_rows[:].bitcast(U8).indirect(idx[:]))
-        for a in range(1, PASSES):
-            nc.sync.dma_start(v_planes[a][0:SHIFT_ROWS, :], v_planes[0][4 * a : 4 * a + SHIFT_ROWS, :])
+        moves = [(a, q) for a in range(PASSES) for q in range(4)]
+        for a, q in moves[:6]:
+            move_rows(a, q)
+        load_table(2, 1)
+        for a, q in moves[6:8]:
+            move_rows(a, q)
+        load_wa_last(0)
+        load_wa_last(1)
+        for a, q in moves[8:]:
+            move_rows(a, q)
+        load_wb(0)
+        nc.vector.memset(w0_planes[:], 0)
         for r in range(4):
             rows = w0_scales[:, r:16:4, :].rearrange("a q n -> q a n").bitcast(I32)
             nc.sync.dma_start(w0_planes[r:P:32, :, :], rows)
         load_w0(0)
-        wgo_sb = keep.tile([P, S], F32, name="wgo_sb", tag="scale_rows", align_bytes=64)
+        wgo_sb = stage.tile([P, S], F32, name="wgo_sb", align_bytes=64, offset=FIRST_TABLE_AT + 8192)
         nc.sync.dma_start(wgo_sb[:], wgo)
 
         turned = psum.tile([P, P], F32, name="bank")
@@ -166,9 +194,9 @@ def tile_list_adapted_key_cache_kernel(
 
         prepare_wa(0)
         load_wb(1)
+        prepare_wa(1)
         gather_words(1, 0, S)
         load_w0(1)
-        prepare_wa(1)
         load_wb(2)
         gather_words(2, 0, S)
         last_bf = wa_bf[PASSES - 1]
@@ -210,7 +238,7 @@ def tile_list_adapted_key_cache_kernel(
                 lhsT=wa_codes[a][:, t * P : (t + 1) * P].bitcast(FP8X4),
                 lhsT_scale=wa_planes[a][:, t * P : (t + 1) * P],
                 rhs=v_words[a][:, j0:j1].bitcast(FP8X4),
-                rhs_scale=v_planes[0][4 * a : P, j0 // 4 : j1 // 4].bitcast(U8),
+                rhs_scale=v_planes[a][:, j0 // 4 : j1 // 4].bitcast(U8),
                 start=start,
                 stop=stop,
             )

@@ -57,10 +57,7 @@ def tile_list_adapted_key_cache_kernel(
         v_planes = [keep.tile([P, S // 4], I32, name="v_plane%d" % a, align_bytes=64) for a in range(PASSES)]
         v_words = [keep.tile([P, S], I32, name="v_words%d" % a, align_bytes=64) for a in range(PASSES)]
         wa_raw = [keep.tile([P, PACK * R], F32, name="wa_raw%d" % a, align_bytes=64) for a in range(PASSES - 1)]
-        wa_last = [
-            stage.tile([P, PACK, R // 2], F32, name="wa_last%d" % i, align_bytes=64, offset=TABLE_BYTES + 4096 * i)
-            for i in range(2)
-        ]
+        wa_raw.append(stage.tile([P, PACK * R], F32, name="wa_last", align_bytes=64, offset=TABLE_BYTES))
         wa_bf = [keep.tile([P, PACK, P, PACK], BF16, name="wa_bf%d" % a, align_bytes=64) for a in range(PASSES)]
         wa_codes = [keep.tile([P, R], U32, name="wa_codes%d" % a, align_bytes=64) for a in range(PASSES)]
         wa_planes = [keep.tile([P, R], U8, name="wa_plane%d" % a, align_bytes=64) for a in range(PASSES)]
@@ -70,13 +67,18 @@ def tile_list_adapted_key_cache_kernel(
         w0_planes = stage.tile([P, PASSES, N // 4], I32, name="w0_planes", align_bytes=64, offset=FIRST_TABLE_AT + 13824)
         w0_codes = {}
         gain = keep.tile([P, HALF, PACK], F32, name="gain", align_bytes=64)
-        h_bf = [keep.tile([P, HALF, PACK], BF16, name="h_bf%d" % half, align_bytes=64) for half in range(2)]
-        h_codes = keep.tile([P, S], U32, name="h_codes", align_bytes=64)
+        h_early = {0: keep.tile([P, QUARTER, PACK], BF16, name="h_early", align_bytes=64)}
+        h_bf = {1: keep.tile([P, HALF, PACK], BF16, name="h_bf1", align_bytes=64)}
         h_plane = keep.tile([P, S], U8, name="h_plane", align_bytes=64)
         lam_sb = keep.tile([P, PACK], F32, name="lam_sb")
         vector_rows = keep.tile([P, P], F32, name="vector_rows")
         vector_cols = keep.tile([P, HEADS + S // P], F32, name="vector_cols")
-        scaled = keep.tile([P, PACK, HALF], F32, name="scaled", align_bytes=64)
+        scaled = {
+            t: stage.tile([P, HALF], F32, name="scaled%d" % t, align_bytes=64, offset=FIRST_TABLE_AT + 4096 + 2048 * t)
+            for t in range(2)
+        }
+        first_bias = keep.tile([P, 1], F32, name="first_bias", align_bytes=64)
+        second_bias = keep.tile([P, 1], F32, name="second_bias", align_bytes=64)
         ident = keep.tile([P, P], F32, name="ident")
         cache = [keep.tile([P, T2], F32, name="cache%d" % b, align_bytes=64) for b in range(OUT_BUFS)]
 
@@ -85,19 +87,13 @@ def tile_list_adapted_key_cache_kernel(
         for a in range(PASSES):
             nc.vector.memset(v_planes[a][:], 0)
 
-        def load_table(a, pieces):
+        def load_table(a, c0, c1):
             words = tab_words[a].rearrange("p t i -> p (t i)").bitcast(I32)
-            width = T // pieces
-            for c0 in range(0, T, width):
-                nc.sync.dma_start(table[a][:, c0 : c0 + width], words[:, c0 : c0 + width])
+            nc.sync.dma_start(table[a][:, c0:c1], words[:, c0:c1])
 
         def load_wa(a):
             rows = wa[a * P * PACK : (a + 1) * P * PACK, :]
             nc.sync.dma_start(wa_raw[a][:], rows.rearrange("(p j) c -> p (j c)", j=PACK))
-
-        def load_wa_last(i):
-            rows = wa[(PASSES - 1) * P * PACK :, i * R // 2 : (i + 1) * R // 2]
-            nc.sync.dma_start(wa_last[i][:], rows.rearrange("(p j) c -> p j c", j=PACK))
 
         def load_wb(i):
             n0, n1 = WB_HEADS[i]
@@ -117,18 +113,19 @@ def tile_list_adapted_key_cache_kernel(
             words = w0_words.rearrange("a p b -> p a b").bitcast(I32)
             nc.sync.dma_start(w0_codes[i][:], words[:, :, P * n0 // 2 : P * n1 // 2])
 
+        load_table(0, 0, T // 4)
         nc.sync.dma_start(idx[:], offs)
         nc.sync.dma_start(lam_sb[:], lam.rearrange("(p t) -> p t", t=PACK))
-        nc.sync.dma_start(idx2[:], offs2)
+        load_table(0, T // 4, T)
         all_rows = tab_scales.rearrange("a q n -> (a q) n").bitcast(I32)
         nc.sync.dma_start(scale_rows[0:P:4, :], all_rows[0:32, :])
         nc.sync.dma_start(scale_rows[2:P:8, :], all_rows[32:48, :])
-        load_table(0, 1)
         nc.scalar.dma_start(vector_rows[HEADS : HEADS + S // P, :], strength.rearrange("(c p) -> c p", p=P))
         nc.scalar.dma_start(vector_rows[0:HEADS, :], bk.rearrange("(c p) -> c p", p=P))
         load_wa(0)
         load_wa(1)
-        load_table(1, 1)
+        load_table(1, 0, T)
+        nc.sync.dma_start(idx2[:], offs2)
         make_identity(nc, ident[:])
 
         def gather_words(a, j0, j1):
@@ -146,13 +143,12 @@ def tile_list_adapted_key_cache_kernel(
         nc.vector.tensor_copy(picked_rows[:].bitcast(U8), scale_rows[:].bitcast(U8).indirect(idx[:]))
         gather_words(0, 0, S)
         moves = [(a, q) for a in range(PASSES) for q in range(4)]
-        for a, q in moves[:6]:
+        for a, q in moves[:5]:
             move_rows(a, q)
-        load_table(2, 1)
-        for a, q in moves[6:8]:
+        load_table(2, 0, T)
+        for a, q in moves[5:8]:
             move_rows(a, q)
-        load_wa_last(0)
-        load_wa_last(1)
+        load_wa(2)
         for a, q in moves[8:]:
             move_rows(a, q)
         load_wb(0)
@@ -167,6 +163,8 @@ def tile_list_adapted_key_cache_kernel(
         turned = psum.tile([P, P], F32, name="bank")
         nc.tensor.transpose(turned[:], vector_rows[:], ident[:])
         nc.scalar.activation(vector_cols[:], turned[:, 0 : HEADS + S // P], COPY)
+        nc.scalar.activation(first_bias[:], turned[:, 0:1], COPY)
+        nc.scalar.activation(second_bias[:], turned[:, 1:2], COPY)
         spread = psum.tile([P, HALF], F32, name="bank")
         for c in range(HALF // P):
             column = vector_cols[:, HEADS + c : HEADS + c + 1]
@@ -201,15 +199,14 @@ def tile_list_adapted_key_cache_kernel(
         gather_words(2, 0, S)
         last_bf = wa_bf[PASSES - 1]
 
-        def round_last(copy, i, t0, t1):
+        def round_last(copy, t0, t1):
             copy(
-                last_bf[:, t0:t1, i * P // 2 : (i + 1) * P // 2, :].rearrange("p t m j -> p m j t"),
-                wa_last[i][:].rearrange("p j (m t) -> p m j t", t=PACK)[:, :, :, t0:t1],
+                last_bf[:, t0:t1].rearrange("p t m j -> p m j t"),
+                wa_raw[PASSES - 1][:].rearrange("p (j m t) -> p m j t", j=PACK, t=PACK)[:, :, :, t0:t1],
             )
 
-        round_last(nc.scalar.copy, 0, 0, PACK)
-        round_last(nc.vector.tensor_copy, 1, 0, 2)
-        round_last(nc.scalar.copy, 1, 2, PACK)
+        round_last(nc.vector.tensor_copy, 0, 2)
+        round_last(nc.scalar.copy, 2, PACK)
         for t0 in range(0, PACK, 2):
             nc.vector.quantize_mx(
                 out=wa_codes[PASSES - 1][:, t0 * P : (t0 + 2) * P].bitcast(FP8X4),
@@ -259,31 +256,30 @@ def tile_list_adapted_key_cache_kernel(
             for t in range(PACK):
                 low_slot_pass(t, a)
 
-        def make_h_chunk(j0):
+        def make_h_chunk(j0, dst):
             low_pass(j0, PASSES - 1)
             nc.vector.tensor_tensor(
-                h_bf[j0 // HALF][:, j0 % HALF : j0 % HALF + CHUNK, :],
+                dst,
                 low[j0][:].rearrange("p t j -> p j t"),
                 gain[:, j0 : j0 + CHUNK, :],
                 MULT,
             )
 
-        def quantize_h(j0, j1):
+        def quantize_h(j0, j1, rounded):
             nc.vector.quantize_mx(
                 out=h_codes[:, j0:j1].bitcast(FP8X4),
                 scales=h_plane[:, j0:j1],
-                in_=h_bf[j0 // HALF][:, j0 % HALF : j0 % HALF + j1 - j0, :].rearrange("p j t -> p (j t)"),
+                in_=rounded[:].rearrange("p j t -> p (j t)"),
             )
 
-        def scale_by_lam():
-            for t in range(PACK):
-                low_slot_pass(t, PASSES - 1)
-                nc.scalar.activation(scaled[:, t, :], low_slot[t][:], COPY, scale=lam_sb[:, t : t + 1])
+        def scale_by_lam(t):
+            low_slot_pass(t, PASSES - 1)
+            nc.scalar.activation(scaled[t][:, 0:HALF], low_slot[t][:], COPY, scale=lam_sb[:, t : t + 1])
 
         def scale_by_strength(c, pairs):
             by_entry = psum.tile([P, PACK, P], F32, name="bank")
             for t in range(PACK):
-                nc.tensor.transpose(by_entry[:, t, :], scaled[:, t, c * P : (c + 1) * P], ident[:])
+                nc.tensor.transpose(by_entry[:, t, :], scaled[t][:, c * P : (c + 1) * P], ident[:])
             col = HEADS + HALF // P + c
             nc.scalar.activation(
                 pairs, by_entry[:].rearrange("p (u e) m -> p u m e", u=2), COPY, scale=vector_cols[:, col : col + 1]
@@ -298,7 +294,7 @@ def tile_list_adapted_key_cache_kernel(
             dst = h_bf[1][:, c0 * P : (c0 + 2) * P, :].rearrange("p j t -> p (j t)").bitcast(F32)
             nc.scalar.copy(dst.rearrange("p (i j u) -> p i j u", i=2, u=2), back[:].rearrange("p i u j -> p i j u"))
 
-        def keys(head, j0, j1, dst):
+        def keys(head, j0, j1, dst, bias=None):
             i = [n0 <= head < n1 for n0, n1 in W0_HEADS].index(True)
             c0 = P * (head - W0_HEADS[i][0]) // 2
             n0, n1 = head * P, (head + 1) * P
@@ -324,7 +320,7 @@ def tile_list_adapted_key_cache_kernel(
                 start=False,
                 stop=True,
             )
-            nc.scalar.activation(dst, y[:], IDENTITY, bias=vector_cols[:, head : head + 1])
+            nc.scalar.activation(dst, y[:], IDENTITY, bias=vector_cols[:, head : head + 1] if bias is None else bias)
 
         def scatter(head, values, j0, j1):
             window = cache[head % OUT_BUFS][:].indirect(idx2[:, j0 // 16 : j1 // 16])
@@ -334,26 +330,39 @@ def tile_list_adapted_key_cache_kernel(
             nc.sync.dma_start(out[head * P : (head + 1) * P, :], cache[head % OUT_BUFS][:])
 
         prepare_wb(0, 2, "wb_bf0")
-        prepare_wb(2, 3, "wb_bf1")
+        h_codes = keep.tile([P, S], U32, name="h_codes", tag="wb_bf0", align_bytes=64)
         early = [ring.tile([P, S], F32, name="weighted", align_bytes=64) for head in range(2)]
-        for j0 in range(0, HALF, QUARTER):
-            make_h_chunk(j0)
-            make_h_chunk(j0 + CHUNK)
-            quantize_h(j0, j0 + QUARTER)
-            if j0 == 0:
-                keys(0, 0, QUARTER, early[0][:, 0:QUARTER])
-        scale_by_lam()
-        keys(1, 0, HALF, early[1][:, 0:HALF])
-        keys(0, QUARTER, HALF, early[0][:, QUARTER:HALF])
-        paired = [keep.tile([P, 2, 2, P, 2], BF16, name="pairs%d" % i, align_bytes=64) for i in range(2)]
+        make_h_chunk(0, h_early[0][:, 0:CHUNK, :])
+        make_h_chunk(CHUNK, h_early[0][:, CHUNK:QUARTER, :])
+        h_third = keep.tile([P, CHUNK, PACK], BF16, name="h_third", align_bytes=64)
+        make_h_chunk(QUARTER, h_third[:])
+        quantize_h(0, QUARTER, h_early[0])
+        keys(0, 0, QUARTER, early[0][:, 0:QUARTER], first_bias[:])
+        h_fourth = keep.tile([P, CHUNK, PACK], BF16, name="h_fourth", tag="h_early", align_bytes=64)
+        make_h_chunk(QUARTER + CHUNK, h_fourth[:])
+        quantize_h(QUARTER, QUARTER + CHUNK, h_third)
+        quantize_h(QUARTER + CHUNK, HALF, h_fourth)
+        scale_by_lam(0)
+        scale_by_lam(1)
+        late_scaled = keep.tile([P, 2, HALF], F32, name="late_scaled", tag="first_bias", align_bytes=64)
+        for t in range(2, PACK):
+            scaled[t] = late_scaled[:, t - 2, :]
+            scale_by_lam(t)
+        keys(1, 0, HALF, early[1][:, 0:HALF], second_bias[:])
+        prepare_wb(2, 3, "wb_bf1")
+        second = keep.tile([P, QUARTER], F32, name="second", tag=WB_TAGS[1], align_bytes=64)
+        keys(0, QUARTER, HALF, second[:])
+        paired = [
+            keep.tile([P, 2, 2, P, 2], BF16, name="pairs", tag=tag, align_bytes=64) for tag in ("second_bias", "pairs1")
+        ]
         for c in range(HALF // P):
             scale_by_strength(c, paired[c // 2][:, c % 2])
         for i in range(2):
             turn_back(2 * i, paired[i])
         scatter(0, early[0][:, 0:QUARTER], 0, QUARTER)
         scatter(1, early[1][:, 0:HALF], 0, HALF)
-        scatter(0, early[0][:, QUARTER:HALF], QUARTER, HALF)
-        quantize_h(HALF, S)
+        scatter(0, second[:], QUARTER, HALF)
+        quantize_h(HALF, S, h_bf[1])
         third = keep.tile([P, HALF], F32, name="third", tag="pairs1", align_bytes=64)
         keys(2, 0, HALF, third[:])
         scatter(2, third[:], 0, HALF)

@@ -73,10 +73,8 @@ def tile_list_adapted_key_cache_kernel(
         lam_sb = keep.tile([P, PACK], F32, name="lam_sb")
         vector_rows = keep.tile([P, P], F32, name="vector_rows")
         vector_cols = keep.tile([P, HEADS + S // P], F32, name="vector_cols")
-        scaled = {
-            t: stage.tile([P, HALF], F32, name="scaled%d" % t, align_bytes=64, offset=FIRST_TABLE_AT + 4096 + 2048 * t)
-            for t in range(2)
-        }
+        early_scaled = stage.tile([P, PACK - 1, HALF], F32, name="scaled", align_bytes=64, offset=FIRST_TABLE_AT + 2048)
+        scaled = {t: early_scaled[:, t, :] for t in range(PACK - 1)}
         first_bias = keep.tile([P, 1], F32, name="first_bias", align_bytes=64)
         second_bias = keep.tile([P, 1], F32, name="second_bias", align_bytes=64)
         ident = keep.tile([P, P], F32, name="ident")
@@ -344,10 +342,9 @@ def tile_list_adapted_key_cache_kernel(
         quantize_h(QUARTER + CHUNK, HALF, h_fourth)
         scale_by_lam(0)
         scale_by_lam(1)
-        late_scaled = keep.tile([P, 2, HALF], F32, name="late_scaled", tag="first_bias", align_bytes=64)
-        for t in range(2, PACK):
-            scaled[t] = late_scaled[:, t - 2, :]
-            scale_by_lam(t)
+        scale_by_lam(2)
+        scaled[3] = keep.tile([P, HALF], F32, name="late_scaled", tag="first_bias", align_bytes=64)
+        scale_by_lam(3)
         keys(1, 0, HALF, early[1][:, 0:HALF], second_bias[:])
         prepare_wb(2, 3, "wb_bf1")
         second = keep.tile([P, QUARTER], F32, name="second", tag=WB_TAGS[1], align_bytes=64)

@@ -147,9 +147,9 @@ def tile_list_adapted_key_cache_kernel(
         for a, q in moves[5:8]:
             move_rows(a, q)
         load_wa(2)
+        load_wb(0)
         for a, q in moves[8:]:
             move_rows(a, q)
-        load_wb(0)
         nc.vector.memset(w0_planes[:], 0)
         for r in range(4):
             rows = w0_scales[:, r:16:4, :].rearrange("a q n -> q a n").bitcast(I32)

@@ -26,7 +26,7 @@ QUARTER = S // 4
 CHUNK = 128
 HEADS = N // P
 WB_HEADS = [(0, 2), (2, 3), (3, 8)]
-WB_TAGS = [None, "wa_raw0", "wa_raw1"]
+WB_TAGS = [None, "wa_pair", "wa_bf0"]
 W0_HEADS = [(0, 2), (2, 8)]
 W0_TAGS = [None, "table1"]
 OUT_BUFS = 3
@@ -56,8 +56,9 @@ def tile_list_adapted_key_cache_kernel(
         picked_rows = keep.tile([P, S // 4], I32, name="picked_rows", align_bytes=64)
         v_planes = [keep.tile([P, S // 4], I32, name="v_plane%d" % a, align_bytes=64) for a in range(PASSES)]
         v_words = [keep.tile([P, S], I32, name="v_words%d" % a, align_bytes=64) for a in range(PASSES)]
-        wa_raw = [keep.tile([P, PACK * R], F32, name="wa_raw%d" % a, align_bytes=64) for a in range(PASSES - 1)]
-        wa_raw.append(stage.tile([P, PACK * R], F32, name="wa_last", align_bytes=64, offset=TABLE_BYTES))
+        wa_pair = keep.tile([P, PASSES - 1, PACK * R], F32, name="wa_pair", align_bytes=64)
+        wa_last = stage.tile([P, PACK * R], F32, name="wa_last", align_bytes=64, offset=TABLE_BYTES)
+        wa_raw = [wa_pair[:, 0, :], wa_pair[:, 1, :], wa_last[:]]
         wa_bf = [keep.tile([P, PACK, P, PACK], BF16, name="wa_bf%d" % a, align_bytes=64) for a in range(PASSES)]
         wa_codes = [keep.tile([P, R], U32, name="wa_codes%d" % a, align_bytes=64) for a in range(PASSES)]
         wa_planes = [keep.tile([P, R], U8, name="wa_plane%d" % a, align_bytes=64) for a in range(PASSES)]
@@ -89,9 +90,7 @@ def tile_list_adapted_key_cache_kernel(
             words = tab_words[a].rearrange("p t i -> p (t i)").bitcast(I32)
             nc.sync.dma_start(table[a][:, c0:c1], words[:, c0:c1])
 
-        def load_wa(a):
-            rows = wa[a * P * PACK : (a + 1) * P * PACK, :]
-            nc.sync.dma_start(wa_raw[a][:], rows.rearrange("(p j) c -> p (j c)", j=PACK))
+        wa_rows = wa.rearrange("(a p j) c -> p a (j c)", p=P, j=PACK)
 
         def load_wb(i):
             n0, n1 = WB_HEADS[i]
@@ -120,10 +119,9 @@ def tile_list_adapted_key_cache_kernel(
         nc.sync.dma_start(scale_rows[2:P:8, :], all_rows[32:48, :])
         nc.scalar.dma_start(vector_rows[HEADS : HEADS + S // P, :], strength.rearrange("(c p) -> c p", p=P))
         nc.scalar.dma_start(vector_rows[0:HEADS, :], bk.rearrange("(c p) -> c p", p=P))
-        load_wa(0)
-        load_wa(1)
-        load_table(1, 0, T)
+        nc.sync.dma_start(wa_pair[:], wa_rows[:, 0 : PASSES - 1, :])
         nc.sync.dma_start(idx2[:], offs2)
+        load_table(1, 0, T)
         make_identity(nc, ident[:])
 
         def gather_words(a, j0, j1):
@@ -141,15 +139,13 @@ def tile_list_adapted_key_cache_kernel(
         nc.vector.tensor_copy(picked_rows[:].bitcast(U8), scale_rows[:].bitcast(U8).indirect(idx[:]))
         gather_words(0, 0, S)
         moves = [(a, q) for a in range(PASSES) for q in range(4)]
-        for a, q in moves[:5]:
+        for a, q in moves[:6]:
             move_rows(a, q)
         load_table(2, 0, T)
-        for a, q in moves[5:8]:
+        for a, q in moves[6:]:
             move_rows(a, q)
-        load_wa(2)
+        nc.sync.dma_start(wa_last[:], wa_rows[:, PASSES - 1, :])
         load_wb(0)
-        for a, q in moves[8:]:
-            move_rows(a, q)
         nc.vector.memset(w0_planes[:], 0)
         for r in range(4):
             rows = w0_scales[:, r:16:4, :].rearrange("a q n -> q a n").bitcast(I32)
@@ -180,7 +176,7 @@ def tile_list_adapted_key_cache_kernel(
         def prepare_wa(a):
             nc.scalar.copy(
                 wa_bf[a][:].rearrange("p t m j -> p m j t"),
-                wa_raw[a][:].rearrange("p (j m t) -> p m j t", j=PACK, t=PACK),
+                wa_raw[a].rearrange("p (j m t) -> p m j t", j=PACK, t=PACK),
             )
             nc.vector.quantize_mx(
                 out=wa_codes[a][:].bitcast(FP8X4),
@@ -189,8 +185,8 @@ def tile_list_adapted_key_cache_kernel(
             )
 
         prepare_wa(0)
-        load_wb(1)
         prepare_wa(1)
+        load_wb(1)
         gather_words(1, 0, S)
         load_w0(1)
         load_wb(2)
@@ -200,7 +196,7 @@ def tile_list_adapted_key_cache_kernel(
         def round_last(copy, t0, t1):
             copy(
                 last_bf[:, t0:t1].rearrange("p t m j -> p m j t"),
-                wa_raw[PASSES - 1][:].rearrange("p (j m t) -> p m j t", j=PACK, t=PACK)[:, :, :, t0:t1],
+                wa_raw[PASSES - 1].rearrange("p (j m t) -> p m j t", j=PACK, t=PACK)[:, :, :, t0:t1],
             )
 
         round_last(nc.vector.tensor_copy, 0, 2)

@@ -25,8 +25,8 @@ HALF = S // 2
 QUARTER = S // 4
 CHUNK = 128
 HEADS = N // P
-WB_HEADS = [(0, 2), (2, 3), (3, 8)]
-WB_TAGS = [None, "wa_pair", "wa_bf0"]
+WB_HEADS = [(0, 1), (1, 2), (2, 8)]
+WB_TAGS = [None, None, "wa_pair"]
 W0_HEADS = [(0, 2), (2, 8)]
 W0_TAGS = [None, "table1"]
 OUT_BUFS = 3
@@ -78,6 +78,7 @@ def tile_list_adapted_key_cache_kernel(
         scaled = {t: early_scaled[:, t, :] for t in range(PACK - 1)}
         first_bias = keep.tile([P, 1], F32, name="first_bias", align_bytes=64)
         second_bias = keep.tile([P, 1], F32, name="second_bias", align_bytes=64)
+        late_bias = keep.tile([P, 1], F32, name="late_bias", align_bytes=64)
         ident = keep.tile([P, P], F32, name="ident")
         cache = [keep.tile([P, T2], F32, name="cache%d" % b, align_bytes=64) for b in range(OUT_BUFS)]
 
@@ -94,8 +95,8 @@ def tile_list_adapted_key_cache_kernel(
 
         def load_wb(i):
             n0, n1 = WB_HEADS[i]
-            if i == 0:
-                wb_raw[i] = stage.tile([P, PACK, P * (n1 - n0)], F32, name="wb_raw0", align_bytes=64, offset=FIRST_TABLE_AT + 4096)
+            if i < 2:
+                wb_raw[i] = stage.tile([P, PACK, P], F32, name="wb_raw%d" % i, align_bytes=64, offset=FIRST_TABLE_AT + 4096 + 2048 * i)
             else:
                 wb_raw[i] = keep.tile([P, PACK, P * (n1 - n0)], F32, name="wb_raw", tag=WB_TAGS[i], align_bytes=64)
             nc.sync.dma_start(wb_raw[i][:], wb[:, P * n0 : P * n1].rearrange("(p j) c -> p j c", j=PACK))
@@ -116,7 +117,7 @@ def tile_list_adapted_key_cache_kernel(
         load_table(0, T // 4, T)
         all_rows = tab_scales.rearrange("a q n -> (a q) n").bitcast(I32)
         nc.sync.dma_start(scale_rows[0:P:4, :], all_rows[0:32, :])
-        nc.sync.dma_start(scale_rows[2:P:8, :], all_rows[32:48, :])
+        nc.sync.dma_start(scale_rows[6:P:8, :], all_rows[32:48, :])
         nc.scalar.dma_start(vector_rows[HEADS : HEADS + S // P, :], strength.rearrange("(c p) -> c p", p=P))
         nc.scalar.dma_start(vector_rows[0:HEADS, :], bk.rearrange("(c p) -> c p", p=P))
         nc.sync.dma_start(wa_pair[:], wa_rows[:, 0 : PASSES - 1, :])
@@ -133,7 +134,7 @@ def tile_list_adapted_key_cache_kernel(
             if a < 2:
                 rows = picked_rows[64 * a + 16 * q : 64 * a + 16 * q + 16 : 4, :]
             else:
-                rows = picked_rows[32 * q + 2 : 32 * q + 32 : 8, :]
+                rows = picked_rows[32 * q + 6 : 32 * q + 32 : 8, :]
             nc.sync.dma_start(v_planes[a][32 * q : 32 * q + 4, :], rows)
 
         nc.vector.tensor_copy(picked_rows[:].bitcast(U8), scale_rows[:].bitcast(U8).indirect(idx[:]))
@@ -146,6 +147,7 @@ def tile_list_adapted_key_cache_kernel(
             move_rows(a, q)
         nc.sync.dma_start(wa_last[:], wa_rows[:, PASSES - 1, :])
         load_wb(0)
+        load_wb(1)
         nc.vector.memset(w0_planes[:], 0)
         for r in range(4):
             rows = w0_scales[:, r:16:4, :].rearrange("a q n -> q a n").bitcast(I32)
@@ -158,7 +160,8 @@ def tile_list_adapted_key_cache_kernel(
         nc.tensor.transpose(turned[:], vector_rows[:], ident[:])
         nc.scalar.activation(vector_cols[:], turned[:, 0 : HEADS + S // P], COPY)
         nc.scalar.activation(first_bias[:], turned[:, 0:1], COPY)
-        nc.scalar.activation(second_bias[:], turned[:, 1:2], COPY)
+        nc.scalar.activation(second_bias[:], turned[:, 0:1], COPY)
+        nc.scalar.activation(late_bias[:], turned[:, 0:1], COPY)
         spread = psum.tile([P, HALF], F32, name="bank")
         for c in range(HALF // P):
             column = vector_cols[:, HEADS + c : HEADS + c + 1]
@@ -186,21 +189,21 @@ def tile_list_adapted_key_cache_kernel(
 
         prepare_wa(0)
         prepare_wa(1)
-        load_wb(1)
+        load_wb(2)
         gather_words(1, 0, S)
         load_w0(1)
-        load_wb(2)
         gather_words(2, 0, S)
         last_bf = wa_bf[PASSES - 1]
 
-        def round_last(copy, t0, t1):
+        def round_last(copy, t0, t1, m0, m1):
             copy(
-                last_bf[:, t0:t1].rearrange("p t m j -> p m j t"),
-                wa_raw[PASSES - 1].rearrange("p (j m t) -> p m j t", j=PACK, t=PACK)[:, :, :, t0:t1],
+                last_bf[:, t0:t1, m0:m1].rearrange("p t m j -> p m j t"),
+                wa_raw[PASSES - 1].rearrange("p (j m t) -> p m j t", j=PACK, t=PACK)[:, m0:m1, :, t0:t1],
             )
 
-        round_last(nc.vector.tensor_copy, 0, 2)
-        round_last(nc.scalar.copy, 2, PACK)
+        round_last(nc.vector.tensor_copy, 0, 2, 0, P)
+        round_last(nc.vector.tensor_copy, 2, PACK, 0, P // 2)
+        round_last(nc.scalar.copy, 2, PACK, P // 2, P)
         for t0 in range(0, PACK, 2):
             nc.vector.quantize_mx(
                 out=wa_codes[PASSES - 1][:, t0 * P : (t0 + 2) * P].bitcast(FP8X4),
@@ -251,7 +254,6 @@ def tile_list_adapted_key_cache_kernel(
                 low_slot_pass(t, a)
 
         def make_h_chunk(j0, dst):
-            low_pass(j0, PASSES - 1)
             nc.vector.tensor_tensor(
                 dst,
                 low[j0][:].rearrange("p t j -> p j t"),
@@ -267,7 +269,6 @@ def tile_list_adapted_key_cache_kernel(
             )
 
         def scale_by_lam(t):
-            low_slot_pass(t, PASSES - 1)
             nc.scalar.activation(scaled[t][:, 0:HALF], low_slot[t][:], COPY, scale=lam_sb[:, t : t + 1])
 
         def scale_by_strength(c, pairs):
@@ -279,14 +280,14 @@ def tile_list_adapted_key_cache_kernel(
                 pairs, by_entry[:].rearrange("p (u e) m -> p u m e", u=2), COPY, scale=vector_cols[:, col : col + 1]
             )
 
-        def turn_back(c0, both):
-            back = psum.tile([P, 2, 2, P], F32, name="bank")
-            for i in range(2):
-                words = both[:, i].rearrange("p u m e -> p (u m e)").bitcast(F32)
+        def turn_back(c0, c1, pairs):
+            back = psum.tile([P, c1 - c0, 2, P], F32, name="bank")
+            for i in range(c1 - c0):
+                words = pairs[:, i].rearrange("p u m e -> p (u m e)").bitcast(F32)
                 for u in range(2):
                     nc.tensor.transpose(back[:, i, u, :], words[:, u * P : (u + 1) * P], ident[:])
-            dst = h_bf[1][:, c0 * P : (c0 + 2) * P, :].rearrange("p j t -> p (j t)").bitcast(F32)
-            nc.scalar.copy(dst.rearrange("p (i j u) -> p i j u", i=2, u=2), back[:].rearrange("p i u j -> p i j u"))
+            dst = h_bf[1][:, c0 * P : c1 * P, :].rearrange("p j t -> p (j t)").bitcast(F32)
+            nc.scalar.copy(dst.rearrange("p (i j u) -> p i j u", i=c1 - c0, u=2), back[:].rearrange("p i u j -> p i j u"))
 
         def keys(head, j0, j1, dst, bias=None):
             i = [n0 <= head < n1 for n0, n1 in W0_HEADS].index(True)
@@ -323,55 +324,56 @@ def tile_list_adapted_key_cache_kernel(
         def store(head):
             nc.sync.dma_start(out[head * P : (head + 1) * P, :], cache[head % OUT_BUFS][:])
 
-        prepare_wb(0, 2, "wb_bf0")
+        prepare_wb(0, 1, "wb_bf0")
         h_codes = keep.tile([P, S], U32, name="h_codes", tag="wb_bf0", align_bytes=64)
         early = [ring.tile([P, S], F32, name="weighted", align_bytes=64) for head in range(2)]
-        make_h_chunk(0, h_early[0][:, 0:CHUNK, :])
-        make_h_chunk(CHUNK, h_early[0][:, CHUNK:QUARTER, :])
-        h_third = keep.tile([P, CHUNK, PACK], BF16, name="h_third", align_bytes=64)
-        make_h_chunk(QUARTER, h_third[:])
+        for j0 in (0, CHUNK):
+            low_pass(j0, PASSES - 1)
+            make_h_chunk(j0, h_early[0][:, j0 : j0 + CHUNK, :])
+        for t in range(2):
+            low_slot_pass(t, PASSES - 1)
+        low_slot_pass(2, PASSES - 1)
+        low_pass(QUARTER, PASSES - 1)
+        low_slot_pass(3, PASSES - 1)
+        prepare_wb(1, 2, "wb_head1")
         quantize_h(0, QUARTER, h_early[0])
         keys(0, 0, QUARTER, early[0][:, 0:QUARTER], first_bias[:])
-        h_fourth = keep.tile([P, CHUNK, PACK], BF16, name="h_fourth", tag="h_early", align_bytes=64)
+        h_third = keep.tile([P, CHUNK, PACK], BF16, name="h_third", tag="wb_head1", align_bytes=64)
+        make_h_chunk(QUARTER, h_third[:])
+        h_fourth = keep.tile([P, CHUNK, PACK], BF16, name="h_fourth", align_bytes=64)
+        low_pass(QUARTER + CHUNK, PASSES - 1)
         make_h_chunk(QUARTER + CHUNK, h_fourth[:])
         quantize_h(QUARTER, QUARTER + CHUNK, h_third)
         quantize_h(QUARTER + CHUNK, HALF, h_fourth)
-        scale_by_lam(0)
-        scale_by_lam(1)
-        scale_by_lam(2)
+        for t in range(PACK - 1):
+            scale_by_lam(t)
         scaled[3] = keep.tile([P, HALF], F32, name="late_scaled", tag="first_bias", align_bytes=64)
         scale_by_lam(3)
-        keys(1, 0, HALF, early[1][:, 0:HALF], second_bias[:])
-        prepare_wb(2, 3, "wb_bf1")
-        second = keep.tile([P, QUARTER], F32, name="second", tag=WB_TAGS[1], align_bytes=64)
-        keys(0, QUARTER, HALF, second[:])
-        paired = [
-            keep.tile([P, 2, 2, P, 2], BF16, name="pairs", tag=tag, align_bytes=64) for tag in ("second_bias", "pairs1")
-        ]
-        for c in range(HALF // P):
-            scale_by_strength(c, paired[c // 2][:, c % 2])
-        for i in range(2):
-            turn_back(2 * i, paired[i])
+        keys(1, 0, HALF, early[1][:, 0:HALF])
+        first_pairs = keep.tile([P, 3, 2, P, 2], BF16, name="pairs0", align_bytes=64)
+        last_pairs = keep.tile([P, 1, 2, P, 2], BF16, name="pairs1", align_bytes=64)
+        for c in range(3):
+            scale_by_strength(c, first_pairs[:, c])
+        scale_by_strength(3, last_pairs[:, 0])
+        turn_back(0, 2, first_pairs[:, 0:2])
+        turn_back(2, 3, first_pairs[:, 2:3])
+        turn_back(3, 4, last_pairs[:])
+        second = keep.tile([P, QUARTER], F32, name="second", tag="pairs1", align_bytes=64)
+        keys(0, QUARTER, HALF, second[:], second_bias[:])
         scatter(0, early[0][:, 0:QUARTER], 0, QUARTER)
         scatter(1, early[1][:, 0:HALF], 0, HALF)
-        scatter(0, second[:], QUARTER, HALF)
         quantize_h(HALF, S, h_bf[1])
-        third = keep.tile([P, HALF], F32, name="third", tag="pairs1", align_bytes=64)
-        keys(2, 0, HALF, third[:])
-        scatter(2, third[:], 0, HALF)
-        for head in range(2):
-            keys(head, HALF, S, early[head][:, HALF:S])
+        scatter(0, second[:], QUARTER, HALF)
+        prepare_wb(2, 4, "second_bias")
+        for head in (1, 0):
+            keys(head, HALF, S, early[head][:, HALF:S], late_bias[:] if head == 0 else None)
             scatter(head, early[head][:, HALF:S], HALF, S)
             store(head)
-        prepare_wb(3, 4, "pairs1")
-        prepare_wb(4, 8, "h_bf1")
-        rest = ring.tile([P, S], F32, name="weighted", align_bytes=64)
-        keys(2, HALF, S, rest[:, HALF:S])
-        scatter(2, rest[:, HALF:S], HALF, S)
-        store(2)
-        for head in range(3, HEADS):
+        for head in range(2, HEADS):
             weighted = ring.tile([P, S], F32, name="weighted", align_bytes=64)
             keys(head, 0, HALF, weighted[:, 0:HALF])
             keys(head, HALF, S, weighted[:, HALF:S])
             scatter(head, weighted[:], 0, S)
             store(head)
+            if head == 2:
+                prepare_wb(4, 8, "late_bias")

@@ -21,18 +21,28 @@ COPY = mybir.ActivationFunctionType.Copy
 P = 128
 PACK = 4
 PASSES = K // (P * PACK)
+LAST = PASSES - 1
 HALF = S // 2
 QUARTER = S // 4
-CHUNK = 128
 HEADS = N // P
-WB_HEADS = [(0, 1), (1, 2), (2, 8)]
-WB_TAGS = [None, None, "wa_pair"]
-W0_HEADS = [(0, 2), (2, 8)]
-W0_TAGS = [None, "table1"]
-OUT_BUFS = 3
-TABLE_BYTES = 4 * T
-WINDOW_AT = TABLE_BYTES - 64
-FIRST_TABLE_AT = TABLE_BYTES + 4096
+CACHES = 5
+KB = 1024
+
+CACHE3_AT = 0
+TABLE1_AT = 8 * KB
+WINDOW_AT = 24 * KB - 128
+WA2_AT = 24 * KB
+TABLE2_AT = 32 * KB
+TABLE0_AT = 48 * KB
+CACHE2_AT = 64 * KB - 128
+WA01_AT = 72 * KB
+GAIN1_AT = 88 * KB
+BIAS0_AT = 122 * KB
+PAIRS3_AT = 99 * KB
+PAIRS7_AT = 103 * KB
+CACHE4_AT = 107 * KB
+GAIN0_AT = 115 * KB
+WA2_BF_AT = 117 * KB
 
 
 def tile_list_adapted_key_cache_kernel(
@@ -42,138 +52,130 @@ def tile_list_adapted_key_cache_kernel(
     with ExitStack() as ctx:
         keep = ctx.enter_context(tc.tile_pool(name="keep", bufs=1))
         stage = ctx.enter_context(tc.tile_pool(name="stage", bufs=1))
-        ring = ctx.enter_context(tc.tile_pool(name="ring", bufs=3))
-        psum = ctx.enter_context(tc.psum_pool(name="psum", bufs=8))
+        psum = ctx.enter_context(tc.psum_pool(name="psum", bufs=1))
+
+        def kept(shape, dtype, name):
+            return keep.tile(shape, dtype, name=name, align_bytes=64)
+
+        def placed(shape, dtype, name, at):
+            return stage.tile(shape, dtype, name=name, align_bytes=64, offset=at)
+
+        def bank(shape, b):
+            return psum.tile(shape, F32, name="bank%d" % b)
 
         idx = keep.tile([P, S // 16], U16, name="idx")
         idx2 = keep.tile([P, S // 16], U16, name="idx2")
-        scale_rows = stage.tile([P, T // 4], I32, name="scale_rows", align_bytes=64, offset=WINDOW_AT)
-        table = [
-            stage.tile([P, T], I32, name="table0", align_bytes=64, offset=FIRST_TABLE_AT),
-            keep.tile([P, T], I32, name="table1", align_bytes=64),
-            stage.tile([P, T], I32, name="table2", align_bytes=64, offset=0),
-        ]
-        picked_rows = keep.tile([P, S // 4], I32, name="picked_rows", align_bytes=64)
-        v_planes = [keep.tile([P, S // 4], I32, name="v_plane%d" % a, align_bytes=64) for a in range(PASSES)]
-        v_words = [keep.tile([P, S], I32, name="v_words%d" % a, align_bytes=64) for a in range(PASSES)]
-        wa_pair = keep.tile([P, PASSES - 1, PACK * R], F32, name="wa_pair", align_bytes=64)
-        wa_last = stage.tile([P, PACK * R], F32, name="wa_last", align_bytes=64, offset=TABLE_BYTES)
+        scale_rows = placed([P, T // 4], I32, "scale_rows", WINDOW_AT)
+        table = [placed([P, T], I32, "table%d" % a, at) for a, at in enumerate((TABLE0_AT - 64, TABLE1_AT - 64, TABLE2_AT))]
+        picked_rows = kept([P, S // 4], I32, "picked_rows")
+        v_planes = {(a, 0): kept([P, (S if a < LAST else HALF) // 4], I32, "v_plane%d" % a) for a in range(PASSES)}
+        v_words = {(a, 0): kept([P, S], I32, "v_words%d" % a) for a in range(LAST)}
+        wa_pair = placed([P, LAST, PACK * R], F32, "wa_pair", WA01_AT)
+        wa_last = placed([P, PACK * R], F32, "wa_last", WA2_AT)
         wa_raw = [wa_pair[:, 0, :], wa_pair[:, 1, :], wa_last[:]]
-        wa_bf = [keep.tile([P, PACK, P, PACK], BF16, name="wa_bf%d" % a, align_bytes=64) for a in range(PASSES)]
-        wa_codes = [keep.tile([P, R], U32, name="wa_codes%d" % a, align_bytes=64) for a in range(PASSES)]
-        wa_planes = [keep.tile([P, R], U8, name="wa_plane%d" % a, align_bytes=64) for a in range(PASSES)]
-        wb_raw = {}
-        wb_codes = keep.tile([P, N], U32, name="wb_codes", align_bytes=64)
-        wb_plane = keep.tile([P, N], U8, name="wb_plane", align_bytes=64)
-        w0_planes = stage.tile([P, PASSES, N // 4], I32, name="w0_planes", align_bytes=64, offset=FIRST_TABLE_AT + 13824)
-        w0_codes = {}
-        gain = keep.tile([P, HALF, PACK], F32, name="gain", align_bytes=64)
-        h_early = {0: keep.tile([P, QUARTER, PACK], BF16, name="h_early", align_bytes=64)}
-        h_bf = {1: keep.tile([P, HALF, PACK], BF16, name="h_bf1", align_bytes=64)}
-        h_plane = keep.tile([P, S], U8, name="h_plane", align_bytes=64)
+        wa_bf = [kept([P, PACK, P, PACK], BF16, "wa_bf%d" % a) for a in range(LAST)]
+        wa_bf += [placed([P, PACK, P, PACK], BF16, "wa_bf2", WA2_BF_AT)]
+        wa_codes = [kept([P, R], U32, "wa_codes%d" % a) for a in range(PASSES)]
+        wa_planes = [kept([P, R], U8, "wa_plane%d" % a) for a in range(PASSES)]
+        wb_codes = kept([P, N], U32, "wb_codes")
+        gain = [placed([P, P, PACK], F32, "gain0", GAIN0_AT), placed([P, P, PACK], F32, "gain1", GAIN1_AT)]
+        h_codes = kept([P, S], U32, "h_codes")
+        h_plane = kept([P, S], U8, "h_plane")
         lam_sb = keep.tile([P, PACK], F32, name="lam_sb")
         vector_rows = keep.tile([P, P], F32, name="vector_rows")
         vector_cols = keep.tile([P, HEADS + S // P], F32, name="vector_cols")
-        early_scaled = stage.tile([P, PACK - 1, HALF], F32, name="scaled", align_bytes=64, offset=FIRST_TABLE_AT + 2048)
-        scaled = {t: early_scaled[:, t, :] for t in range(PACK - 1)}
-        first_bias = keep.tile([P, 1], F32, name="first_bias", align_bytes=64)
-        second_bias = keep.tile([P, 1], F32, name="second_bias", align_bytes=64)
-        late_bias = keep.tile([P, 1], F32, name="late_bias", align_bytes=64)
+        first_bias = placed([P, 32], F32, "first_bias", BIAS0_AT)
         ident = keep.tile([P, P], F32, name="ident")
-        cache = [keep.tile([P, T2], F32, name="cache%d" % b, align_bytes=64) for b in range(OUT_BUFS)]
+        cache = [kept([P, T2], F32, "cache%d" % b) for b in range(2)]
+        cache += [placed([P, T2], F32, "cache%d" % b, at) for b, at in ((2, CACHE2_AT), (3, CACHE3_AT), (4, CACHE4_AT))]
 
-        nc.gpsimd.memset(vector_rows[:], 0.0)
         nc.gpsimd.memset(scale_rows[:], 0)
+        nc.gpsimd.memset(vector_rows[:], 0.0)
         for a in range(PASSES):
-            nc.vector.memset(v_planes[a][:], 0)
+            nc.vector.memset(v_planes[a, 0][:], 0)
 
         def load_table(a, c0, c1):
             words = tab_words[a].rearrange("p t i -> p (t i)").bitcast(I32)
             nc.sync.dma_start(table[a][:, c0:c1], words[:, c0:c1])
 
         wa_rows = wa.rearrange("(a p j) c -> p a (j c)", p=P, j=PACK)
-
-        def load_wb(i):
-            n0, n1 = WB_HEADS[i]
-            if i < 2:
-                wb_raw[i] = stage.tile([P, PACK, P], F32, name="wb_raw%d" % i, align_bytes=64, offset=FIRST_TABLE_AT + 4096 + 2048 * i)
-            else:
-                wb_raw[i] = keep.tile([P, PACK, P * (n1 - n0)], F32, name="wb_raw", tag=WB_TAGS[i], align_bytes=64)
-            nc.sync.dma_start(wb_raw[i][:], wb[:, P * n0 : P * n1].rearrange("(p j) c -> p j c", j=PACK))
-
-        def load_w0(i):
-            n0, n1 = W0_HEADS[i]
-            shape = [P, PASSES, P * (n1 - n0) // 2]
-            if i == 0:
-                w0_codes[i] = stage.tile(shape, I32, name="w0_codes0", align_bytes=64, offset=FIRST_TABLE_AT + 12288)
-            else:
-                w0_codes[i] = keep.tile(shape, I32, name="w0_codes", tag=W0_TAGS[i], align_bytes=64)
-            words = w0_words.rearrange("a p b -> p a b").bitcast(I32)
-            nc.sync.dma_start(w0_codes[i][:], words[:, :, P * n0 // 2 : P * n1 // 2])
-
         load_table(0, 0, T // 4)
         nc.sync.dma_start(idx[:], offs)
         nc.sync.dma_start(lam_sb[:], lam.rearrange("(p t) -> p t", t=PACK))
-        load_table(0, T // 4, T)
+        nc.sync.dma_start(idx2[:], offs2)
+        load_table(0, T // 4, T // 2)
         all_rows = tab_scales.rearrange("a q n -> (a q) n").bitcast(I32)
         nc.sync.dma_start(scale_rows[0:P:4, :], all_rows[0:32, :])
         nc.sync.dma_start(scale_rows[6:P:8, :], all_rows[32:48, :])
+        load_table(0, T // 2, T)
         nc.scalar.dma_start(vector_rows[HEADS : HEADS + S // P, :], strength.rearrange("(c p) -> c p", p=P))
         nc.scalar.dma_start(vector_rows[0:HEADS, :], bk.rearrange("(c p) -> c p", p=P))
-        nc.sync.dma_start(wa_pair[:], wa_rows[:, 0 : PASSES - 1, :])
-        nc.sync.dma_start(idx2[:], offs2)
-        load_table(1, 0, T)
+        nc.sync.dma_start(wa_pair[:], wa_rows[:, 0:LAST, :])
         make_identity(nc, ident[:])
+        nc.gpsimd.memset(cache[4][:], 0.0)
 
-        def gather_words(a, j0, j1):
-            nc.vector.tensor_copy(
-                v_words[a][:, j0:j1].bitcast(U32), table[a][:].bitcast(U32).indirect(idx[:, j0 // 16 : j1 // 16])
-            )
+        def gather_words(a, j0, j1, dst):
+            nc.vector.tensor_copy(dst.bitcast(U32), table[a][:].bitcast(U32).indirect(idx[:, j0 // 16 : j1 // 16]))
 
-        def move_rows(a, q):
-            if a < 2:
+        def move_rows(a, q, j0=0):
+            if a < LAST:
                 rows = picked_rows[64 * a + 16 * q : 64 * a + 16 * q + 16 : 4, :]
             else:
-                rows = picked_rows[32 * q + 6 : 32 * q + 32 : 8, :]
-            nc.sync.dma_start(v_planes[a][32 * q : 32 * q + 4, :], rows)
+                rows = picked_rows[32 * q + 6 : 32 * q + 32 : 8, j0 // 4 : (j0 + HALF) // 4]
+            nc.sync.dma_start(v_planes[a, j0][32 * q : 32 * q + 4, :], rows)
 
         nc.vector.tensor_copy(picked_rows[:].bitcast(U8), scale_rows[:].bitcast(U8).indirect(idx[:]))
-        gather_words(0, 0, S)
+        gather_words(0, 0, S, v_words[0, 0][:])
         moves = [(a, q) for a in range(PASSES) for q in range(4)]
-        for a, q in moves[:6]:
+        for a, q in moves[:5]:
             move_rows(a, q)
-        load_table(2, 0, T)
-        for a, q in moves[6:]:
+        load_table(1, 0, T)
+        for a, q in moves[5:8]:
             move_rows(a, q)
-        nc.sync.dma_start(wa_last[:], wa_rows[:, PASSES - 1, :])
-        load_wb(0)
-        load_wb(1)
+        nc.sync.dma_start(wa_last[:], wa_rows[:, LAST, :])
+        load_table(LAST, 0, T)
+        for a, q in moves[8:]:
+            move_rows(a, q)
+
+        wb_raw, w0_codes = {}, {}
+
+        def load_wb(n0, n1, at):
+            raw = placed([P, PACK, P * (n1 - n0)], F32, "wb_raw%d" % n0, at)
+            nc.sync.dma_start(raw[:], wb[:, P * n0 : P * n1].rearrange("(p j) c -> p j c", j=PACK))
+            wb_raw[n0] = raw
+
+        def load_w0(n0, n1, at):
+            codes = placed([P, PASSES, P * (n1 - n0) // 2], I32, "w0_codes%d" % n0, at)
+            words = w0_words.rearrange("a p b -> p a b").bitcast(I32)
+            nc.sync.dma_start(codes[:], words[:, :, P * n0 // 2 : P * n1 // 2])
+            for head in range(n0, n1):
+                w0_codes[head] = (codes, P * (head - n0) // 2)
+
+        load_wb(0, 1, TABLE0_AT + 10 * KB)
+        w0_planes = placed([P, PASSES, N // 4], I32, "w0_planes", TABLE0_AT + 6 * KB)
         nc.vector.memset(w0_planes[:], 0)
         for r in range(4):
             rows = w0_scales[:, r:16:4, :].rearrange("a q n -> q a n").bitcast(I32)
             nc.sync.dma_start(w0_planes[r:P:32, :, :], rows)
-        load_w0(0)
-        wgo_sb = stage.tile([P, S], F32, name="wgo_sb", align_bytes=64, offset=FIRST_TABLE_AT + 8192)
-        nc.sync.dma_start(wgo_sb[:], wgo)
+        load_w0(0, 2, TABLE0_AT + 4 * KB)
+        load_wb(1, 2, TABLE0_AT)
 
-        turned = psum.tile([P, P], F32, name="bank")
+        turned = bank([P, P], 0)
         nc.tensor.transpose(turned[:], vector_rows[:], ident[:])
         nc.scalar.activation(vector_cols[:], turned[:, 0 : HEADS + S // P], COPY)
-        nc.scalar.activation(first_bias[:], turned[:, 0:1], COPY)
-        nc.scalar.activation(second_bias[:], turned[:, 0:1], COPY)
-        nc.scalar.activation(late_bias[:], turned[:, 0:1], COPY)
-        spread = psum.tile([P, HALF], F32, name="bank")
-        for c in range(HALF // P):
+        nc.scalar.activation(first_bias[:, 0:1], turned[:, 0:1], COPY)
+        spread = bank([P, QUARTER], 1)
+        for c in range(2):
             column = vector_cols[:, HEADS + c : HEADS + c + 1]
             nc.tensor.transpose(spread[:, c * P : (c + 1) * P], column.to_broadcast([P, P]), ident[:])
-        nc.vector.tensor_tensor(
-            gain[:],
-            spread[:].unsqueeze(2).broadcast_to([P, HALF, PACK]),
-            lam_sb[:].unsqueeze(1).broadcast_to([P, HALF, PACK]),
-            MULT,
-        )
-
-        for b in range(OUT_BUFS):
+        for c in range(2):
+            nc.vector.tensor_tensor(
+                gain[c][:],
+                spread[:, c * P : (c + 1) * P].unsqueeze(2).broadcast_to([P, P, PACK]),
+                lam_sb[:].unsqueeze(1).broadcast_to([P, P, PACK]),
+                MULT,
+            )
+        for b in range(3):
             nc.vector.memset(cache[b][:], 0.0)
 
         def prepare_wa(a):
@@ -189,76 +191,70 @@ def tile_list_adapted_key_cache_kernel(
 
         prepare_wa(0)
         prepare_wa(1)
-        load_wb(2)
-        gather_words(1, 0, S)
-        load_w0(1)
-        gather_words(2, 0, S)
-        last_bf = wa_bf[PASSES - 1]
+        v_planes[LAST, HALF] = placed([P, HALF // 4], I32, "v_plane_late", WA01_AT + 11 * KB // 2)
+        nc.vector.memset(v_planes[LAST, HALF][:], 0)
+        wgo_sb = placed([P, S], F32, "wgo_sb", WA01_AT)
+        nc.sync.dma_start(wgo_sb[:, 0:QUARTER], wgo[:, 0:QUARTER])
+        load_wb(2, 3, WA01_AT + 10 * KB)
+        load_w0(2, 4, WA01_AT + 4 * KB)
+        load_wb(3, 4, WA01_AT + 6 * KB)
+        nc.sync.dma_start(wgo_sb[:, QUARTER:S], wgo[:, QUARTER:S])
+        load_wb(4, 5, WA01_AT + 8 * KB)
+        for q in range(4):
+            move_rows(LAST, q, HALF)
+        gather_words(1, 0, S, v_words[1, 0][:])
+        load_w0(4, HEADS, TABLE1_AT)
+        prepare_wa(LAST)
+        load_wb(5, HEADS, WA2_AT + 2 * KB)
+        nc.vector.memset(cache[3][:], 0.0)
 
-        def round_last(copy, t0, t1, m0, m1):
-            copy(
-                last_bf[:, t0:t1, m0:m1].rearrange("p t m j -> p m j t"),
-                wa_raw[PASSES - 1].rearrange("p (j m t) -> p m j t", j=PACK, t=PACK)[:, m0:m1, :, t0:t1],
-            )
-
-        round_last(nc.vector.tensor_copy, 0, 2, 0, P)
-        round_last(nc.vector.tensor_copy, 2, PACK, 0, P // 2)
-        round_last(nc.scalar.copy, 2, PACK, P // 2, P)
-        for t0 in range(0, PACK, 2):
-            nc.vector.quantize_mx(
-                out=wa_codes[PASSES - 1][:, t0 * P : (t0 + 2) * P].bitcast(FP8X4),
-                scales=wa_planes[PASSES - 1][:, t0 * P : (t0 + 2) * P],
-                in_=last_bf[:, t0 : t0 + 2].rearrange("p t m j -> p (t m j)"),
-            )
-
-        def prepare_wb(n0, n1, tag):
-            i = [lo <= n0 < hi for lo, hi in WB_HEADS].index(True)
-            c0 = P * (n0 - WB_HEADS[i][0])
-            width = P * (n1 - n0)
-            wb_bf = keep.tile([P, width, PACK], BF16, name="wb_bf", tag=tag, align_bytes=64)
-            nc.scalar.copy(
-                wb_bf[:].rearrange("p (c i) j -> p c j i", i=4),
-                wb_raw[i][:, :, c0 : c0 + width].rearrange("p j (c i) -> p c j i", i=4),
-            )
-            nc.vector.quantize_mx(
-                out=wb_codes[:, n0 * P : n1 * P].bitcast(FP8X4),
-                scales=wb_plane[:, n0 * P : n1 * P],
-                in_=wb_bf[:].rearrange("p c j -> p (c j)"),
-            )
+        def picked(a, j0, j1):
+            lo = HALF if a == LAST and j0 >= HALF else 0
+            words = v_words[a, lo][:, j0 - lo : j1 - lo].bitcast(FP8X4)
+            return words, v_planes[a, lo][:, (j0 - lo) // 4 : (j1 - lo) // 4].bitcast(U8)
 
         def low_product(dst, a, t, j0, j1, start, stop):
+            words, plane = picked(a, j0, j1)
             nc.tensor.matmul_mx(
                 out=dst,
                 lhsT=wa_codes[a][:, t * P : (t + 1) * P].bitcast(FP8X4),
                 lhsT_scale=wa_planes[a][:, t * P : (t + 1) * P],
-                rhs=v_words[a][:, j0:j1].bitcast(FP8X4),
-                rhs_scale=v_planes[a][:, j0 // 4 : j1 // 4].bitcast(U8),
+                rhs=words,
+                rhs_scale=plane,
                 start=start,
                 stop=stop,
             )
 
-        def low_pass(j0, a):
+        low_chunk = [bank([P, PACK, P], c) for c in range(2)]
+        low_second = [bank([P, 2, QUARTER], 2 + u) for u in range(2)]
+        low_half = [bank([P, HALF], 4 + t) for t in range(PACK)]
+
+        def first_half_pass(a):
+            for c in range(2):
+                for t in range(PACK):
+                    low_product(low_chunk[c][:, t, :], a, t, c * P, (c + 1) * P, a == 0 and t == 0, a == LAST and t == PACK - 1)
             for t in range(PACK):
-                last = a == PASSES - 1 and t == PACK - 1
-                low_product(low[j0][:, t, :], a, t, j0, j0 + CHUNK, a == 0 and t == 0, last)
+                low_product(low_second[t // 2][:, t % 2, :], a, t, QUARTER, HALF, a == 0 and t % 2 == 0, a == LAST and t % 2 == 1)
 
-        def low_slot_pass(t, a):
-            low_product(low_slot[t][:], a, t, HALF, S, a == 0, a == PASSES - 1)
-
-        low = {j0: psum.tile([P, PACK, CHUNK], F32, name="bank") for j0 in range(0, HALF, CHUNK)}
-        low_slot = [psum.tile([P, HALF], F32, name="bank") for t in range(PACK)]
-        for a in range(PASSES - 1):
-            for j0 in range(0, HALF, CHUNK):
-                low_pass(j0, a)
+        def second_half_pass(a):
             for t in range(PACK):
-                low_slot_pass(t, a)
+                low_product(low_half[t][:], a, t, HALF, S, a == 0, a == LAST)
 
-        def make_h_chunk(j0, dst):
-            nc.vector.tensor_tensor(
-                dst,
-                low[j0][:].rearrange("p t j -> p j t"),
-                gain[:, j0 : j0 + CHUNK, :],
-                MULT,
+        for a in range(LAST):
+            first_half_pass(a)
+            second_half_pass(a)
+
+        def round_wb(n0, n1, wb_bf):
+            nc.scalar.copy(
+                wb_bf[:].rearrange("p (c i) j -> p c j i", i=4),
+                wb_raw[n0][:].rearrange("p j (c i) -> p c j i", i=4),
+            )
+
+        def quantize_wb(n0, n1, wb_bf):
+            nc.vector.quantize_mx(
+                out=wb_codes[:, n0 * P : n1 * P].bitcast(FP8X4),
+                scales=wb_plane[:, n0 * P : n1 * P],
+                in_=wb_bf[:].rearrange("p c j -> p (c j)"),
             )
 
         def quantize_h(j0, j1, rounded):
@@ -268,44 +264,39 @@ def tile_list_adapted_key_cache_kernel(
                 in_=rounded[:].rearrange("p j t -> p (j t)"),
             )
 
-        def scale_by_lam(t):
-            nc.scalar.activation(scaled[t][:, 0:HALF], low_slot[t][:], COPY, scale=lam_sb[:, t : t + 1])
-
-        def scale_by_strength(c, pairs):
-            by_entry = psum.tile([P, PACK, P], F32, name="bank")
-            for t in range(PACK):
-                nc.tensor.transpose(by_entry[:, t, :], scaled[t][:, c * P : (c + 1) * P], ident[:])
-            col = HEADS + HALF // P + c
+        def scale_by_strength(c, slots, pairs, b):
+            by_entry = bank([P, PACK, P], b)
+            for t in reversed(range(PACK)):
+                nc.tensor.transpose(by_entry[:, t, :], slots[t], ident[:])
+            col = HEADS + c
             nc.scalar.activation(
                 pairs, by_entry[:].rearrange("p (u e) m -> p u m e", u=2), COPY, scale=vector_cols[:, col : col + 1]
             )
 
-        def turn_back(c0, c1, pairs):
-            back = psum.tile([P, c1 - c0, 2, P], F32, name="bank")
-            for i in range(c1 - c0):
-                words = pairs[:, i].rearrange("p u m e -> p (u m e)").bitcast(F32)
+        def turn_back(pairs, dst, b):
+            back = bank([P, len(pairs), 2, P], b)
+            for i in range(len(pairs)):
+                words = pairs[i].rearrange("p u m e -> p (u m e)").bitcast(F32)
                 for u in range(2):
                     nc.tensor.transpose(back[:, i, u, :], words[:, u * P : (u + 1) * P], ident[:])
-            dst = h_bf[1][:, c0 * P : c1 * P, :].rearrange("p j t -> p (j t)").bitcast(F32)
-            nc.scalar.copy(dst.rearrange("p (i j u) -> p i j u", i=c1 - c0, u=2), back[:].rearrange("p i u j -> p i j u"))
+            words = dst.rearrange("p j t -> p (j t)").bitcast(F32)
+            nc.scalar.copy(words.rearrange("p (i j u) -> p i j u", i=len(pairs), u=2), back[:].rearrange("p i u j -> p i j u"))
 
-        def keys(head, j0, j1, dst, bias=None):
-            i = [n0 <= head < n1 for n0, n1 in W0_HEADS].index(True)
-            c0 = P * (head - W0_HEADS[i][0]) // 2
+        def keys(head, j0, j1, dst, b, bias=None):
+            codes, c0 = w0_codes[head]
             n0, n1 = head * P, (head + 1) * P
-            y = psum.tile([P, j1 - j0], F32, name="bank")
-            width = HALF if j1 - j0 == HALF else CHUNK
+            y = bank([P, j1 - j0], b)
             for a in range(PASSES):
-                for lo in range(j0, j1, width):
-                    nc.tensor.matmul_mx(
-                        out=y[:, lo - j0 : lo - j0 + width],
-                        lhsT=w0_codes[i][:, a, c0 : c0 + P // 2].bitcast(U8).bitcast(FP4X4),
-                        lhsT_scale=w0_planes[:, a, n0 // 4 : n1 // 4].bitcast(U8),
-                        rhs=v_words[a][:, lo : lo + width].bitcast(FP8X4),
-                        rhs_scale=v_planes[a][:, lo // 4 : (lo + width) // 4].bitcast(U8),
-                        start=(a == 0 and lo == j0),
-                        stop=False,
-                    )
+                words, plane = picked(a, j0, j1)
+                nc.tensor.matmul_mx(
+                    out=y[:],
+                    lhsT=codes[:, a, c0 : c0 + P // 2].bitcast(U8).bitcast(FP4X4),
+                    lhsT_scale=w0_planes[:, a, n0 // 4 : n1 // 4].bitcast(U8),
+                    rhs=words,
+                    rhs_scale=plane,
+                    start=(a == 0),
+                    stop=False,
+                )
             nc.tensor.matmul_mx(
                 out=y[:],
                 lhsT=wb_codes[:, n0:n1].bitcast(FP8X4),
@@ -318,62 +309,120 @@ def tile_list_adapted_key_cache_kernel(
             nc.scalar.activation(dst, y[:], IDENTITY, bias=vector_cols[:, head : head + 1] if bias is None else bias)
 
         def scatter(head, values, j0, j1):
-            window = cache[head % OUT_BUFS][:].indirect(idx2[:, j0 // 16 : j1 // 16])
+            window = cache[head % CACHES][:].indirect(idx2[:, j0 // 16 : j1 // 16])
             nc.vector.tensor_tensor(window, values, wgo_sb[:, j0:j1], MULT)
 
         def store(head):
-            nc.sync.dma_start(out[head * P : (head + 1) * P, :], cache[head % OUT_BUFS][:])
+            nc.sync.dma_start(out[head * P : (head + 1) * P, :], cache[head % CACHES][:])
 
-        prepare_wb(0, 1, "wb_bf0")
-        h_codes = keep.tile([P, S], U32, name="h_codes", tag="wb_bf0", align_bytes=64)
-        early = [ring.tile([P, S], F32, name="weighted", align_bytes=64) for head in range(2)]
-        for j0 in (0, CHUNK):
-            low_pass(j0, PASSES - 1)
-            make_h_chunk(j0, h_early[0][:, j0 : j0 + CHUNK, :])
-        for t in range(2):
-            low_slot_pass(t, PASSES - 1)
-        low_slot_pass(2, PASSES - 1)
-        low_pass(QUARTER, PASSES - 1)
-        low_slot_pass(3, PASSES - 1)
-        prepare_wb(1, 2, "wb_head1")
-        quantize_h(0, QUARTER, h_early[0])
-        keys(0, 0, QUARTER, early[0][:, 0:QUARTER], first_bias[:])
-        h_third = keep.tile([P, CHUNK, PACK], BF16, name="h_third", tag="wb_head1", align_bytes=64)
-        make_h_chunk(QUARTER, h_third[:])
-        h_fourth = keep.tile([P, CHUNK, PACK], BF16, name="h_fourth", align_bytes=64)
-        low_pass(QUARTER + CHUNK, PASSES - 1)
-        make_h_chunk(QUARTER + CHUNK, h_fourth[:])
-        quantize_h(QUARTER, QUARTER + CHUNK, h_third)
-        quantize_h(QUARTER + CHUNK, HALF, h_fourth)
+        def values_at(width, name, at):
+            return placed([P, width], F32, name, at)
+
+        v_words[LAST, 0] = placed([P, HALF], I32, "v_first", WA2_BF_AT)
+        wb_plane = placed([P, N], U8, "wb_plane", GAIN0_AT)
+        gather_words(LAST, 0, QUARTER, v_words[LAST, 0][:, 0:QUARTER])
+        gather_words(LAST, QUARTER, HALF, v_words[LAST, 0][:, QUARTER:HALF])
+        first_half_pass(LAST)
+        wb_bf = {head: placed([P, P, PACK], BF16, "wb_bf%d" % head, WA2_AT + head * KB) for head in range(2)}
+        round_wb(0, 1, wb_bf[0])
+        h_first = kept([P, QUARTER, PACK], BF16, "h_first")
+        for c in range(2):
+            nc.vector.tensor_tensor(
+                h_first[:, c * P : (c + 1) * P, :], low_chunk[c][:].rearrange("p t j -> p j t"), gain[c][:], MULT
+            )
+        quantize_wb(0, 1, wb_bf[0])
+        quantize_h(0, QUARTER, h_first)
+        v_words[LAST, HALF] = placed([P, HALF], I32, "v_late", GAIN1_AT)
+        gather_words(LAST, HALF, S, v_words[LAST, HALF][:])
+        scaled_second = placed([P, PACK, QUARTER], F32, "scaled_second", TABLE0_AT + 10 * KB)
+
+        def scale_second(t, c0, c1, dst):
+            nc.scalar.activation(dst, low_second[t // 2][:, t % 2, c0:c1], COPY, scale=lam_sb[:, t : t + 1])
+
         for t in range(PACK - 1):
-            scale_by_lam(t)
-        scaled[3] = keep.tile([P, HALF], F32, name="late_scaled", tag="first_bias", align_bytes=64)
+            scale_second(t, 0, QUARTER, scaled_second[:, t, :])
+        scale_second(PACK - 1, 0, P, scaled_second[:, PACK - 1, 0:P])
+        round_wb(1, 2, wb_bf[1])
+        quantize_wb(1, 2, wb_bf[1])
+        values = values_at(QUARTER, "values00", TABLE0_AT)
+        keys(0, 0, QUARTER, values[:], 0, first_bias[:, 0:1])
+        scatter(0, values[:], 0, QUARTER)
+        scaled_last = placed([P, P], F32, "scaled_last", BIAS0_AT - 448)
+        scale_second(PACK - 1, P, QUARTER, scaled_last[:])
+
+        pairs = {c: kept([P, 2, P, 2], BF16, "pairs%d" % c)[:] for c in (2, 4, 5, 6)}
+        pairs[3] = placed([P, 2, P, 2], BF16, "pairs3", PAIRS3_AT)[:]
+        pairs[7] = placed([P, 2, P, 2], BF16, "pairs7", PAIRS7_AT)[:]
+        wb_bf[2] = placed([P, P, PACK], BF16, "wb_bf2", BIAS0_AT + 64)
+        round_wb(2, 3, wb_bf[2])
+        quantize_wb(2, 3, wb_bf[2])
+        scale_by_strength(2, [scaled_second[:, t, 0:P] for t in range(PACK)], pairs[2], 0)
+        values = values_at(QUARTER, "values10", WA01_AT + 10 * KB)
+        keys(1, 0, QUARTER, values[:], 1)
+        scatter(1, values[:], 0, QUARTER)
+        scale_by_strength(3, [scaled_second[:, t, P:QUARTER] for t in range(PACK - 1)] + [scaled_last[:]], pairs[3], 2)
+        h_second = kept([P, QUARTER, PACK], BF16, "h_second")
+        turn_back([pairs[2]], h_second[:, 0:P, :], 0)
+        turn_back([pairs[3]], h_second[:, P:QUARTER, :], 2)
+        quantize_h(QUARTER, HALF, h_second)
+        values = values_at(QUARTER, "values20", PAIRS3_AT + KB // 2)
+        keys(2, 0, QUARTER, values[:], 1)
+        scatter(2, values[:], 0, QUARTER)
+        wb_bf[3] = placed([P, P, PACK], BF16, "wb_bf3", TABLE0_AT + 10 * KB)
+        round_wb(3, 4, wb_bf[3])
+        quantize_wb(3, 4, wb_bf[3])
+        second_half_pass(LAST)
+
+        scaled_half = placed([P, PACK, HALF], F32, "scaled_half", PAIRS3_AT - 15 * KB // 2)
+
+        def scale_by_lam(t):
+            nc.scalar.activation(scaled_half[:, t, :], low_half[t][:], COPY, scale=lam_sb[:, t : t + 1])
+
+        def late_slots(c):
+            return [scaled_half[:, t, (c - 4) * P : (c - 3) * P] for t in range(PACK)]
+
+        def second_quarter(head, b):
+            values = values_at(QUARTER, "values%d1" % head, TABLE1_AT + (4 + head) * KB)
+            keys(head, QUARTER, HALF, values[:], b)
+            scatter(head, values[:], QUARTER, HALF)
+
+        scale_by_lam(0)
+        scale_by_lam(1)
+        second_quarter(0, 3)
+        scale_by_lam(2)
         scale_by_lam(3)
-        keys(1, 0, HALF, early[1][:, 0:HALF])
-        first_pairs = keep.tile([P, 3, 2, P, 2], BF16, name="pairs0", align_bytes=64)
-        last_pairs = keep.tile([P, 1, 2, P, 2], BF16, name="pairs1", align_bytes=64)
-        for c in range(3):
-            scale_by_strength(c, first_pairs[:, c])
-        scale_by_strength(3, last_pairs[:, 0])
-        turn_back(0, 2, first_pairs[:, 0:2])
-        turn_back(2, 3, first_pairs[:, 2:3])
-        turn_back(3, 4, last_pairs[:])
-        second = keep.tile([P, QUARTER], F32, name="second", tag="pairs1", align_bytes=64)
-        keys(0, QUARTER, HALF, second[:], second_bias[:])
-        scatter(0, early[0][:, 0:QUARTER], 0, QUARTER)
-        scatter(1, early[1][:, 0:HALF], 0, HALF)
-        quantize_h(HALF, S, h_bf[1])
-        scatter(0, second[:], QUARTER, HALF)
-        prepare_wb(2, 4, "second_bias")
-        for head in (1, 0):
-            keys(head, HALF, S, early[head][:, HALF:S], late_bias[:] if head == 0 else None)
-            scatter(head, early[head][:, HALF:S], HALF, S)
+        second_quarter(1, 0)
+        wb_bf[4] = placed([P, P, PACK], BF16, "wb_bf4", TABLE0_AT + 10 * KB)
+        round_wb(4, 5, wb_bf[4])
+        quantize_wb(4, 5, wb_bf[4])
+        scale_by_strength(4, late_slots(4), pairs[4], 4)
+        second_quarter(2, 1)
+        scale_by_strength(5, late_slots(5), pairs[5], 5)
+        values = values_at(HALF, "values3", WA01_AT + 8 * KB)
+        keys(3, 0, HALF, values[:], 2)
+        scatter(3, values[:], 0, HALF)
+        for c in (6, 7):
+            scale_by_strength(c, late_slots(c), pairs[c], c)
+        h_late = kept([P, HALF, PACK], BF16, "h_late")
+        turn_back([pairs[4], pairs[5]], h_late[:, 0:QUARTER, :], 3)
+        turn_back([pairs[6], pairs[7]], h_late[:, QUARTER:HALF, :], 0)
+        quantize_h(HALF, S, h_late)
+        values = values_at(HALF, "values4", PAIRS7_AT - 3 * KB // 2)
+        keys(4, 0, HALF, values[:], 1)
+        scatter(4, values[:], 0, HALF)
+        late_bf = placed([P, 3 * P, PACK], BF16, "wb_bf_late", PAIRS7_AT + KB // 2)
+        round_wb(5, HEADS, late_bf)
+        quantize_wb(5, HEADS, late_bf)
+        late_at = [TABLE1_AT + (7 + 2 * head) * KB for head in range(4)] + [TABLE0_AT]
+        for head, b in enumerate((4, 5, 6, 7, 3)):
+            values = values_at(HALF, "values%d2" % head, late_at[head])
+            keys(head, HALF, S, values[:], b)
+            scatter(head, values[:], HALF, S)
             store(head)
-        for head in range(2, HEADS):
-            weighted = ring.tile([P, S], F32, name="weighted", align_bytes=64)
-            keys(head, 0, HALF, weighted[:, 0:HALF])
-            keys(head, HALF, S, weighted[:, HALF:S])
-            scatter(head, weighted[:], 0, S)
+        banks = (2, 0, 1, 4, 5, 6)
+        for head in range(CACHES, HEADS):
+            values = values_at(S, "values%d" % head, TABLE2_AT + 4 * (head - CACHES) * KB)
+            keys(head, 0, HALF, values[:, 0:HALF], banks[2 * (head - CACHES)])
+            keys(head, HALF, S, values[:, HALF:S], banks[2 * (head - CACHES) + 1])
+            scatter(head, values[:], 0, S)
             store(head)
-            if head == 2:
-                prepare_wb(4, 8, "late_bias")

@@ -73,7 +73,7 @@ def tile_list_adapted_key_cache_kernel(
         wa_pair = placed([P, LAST, PACK * R], F32, "wa_pair", WA01_AT)
         wa_last = placed([P, PACK * R], F32, "wa_last", WA2_AT)
         wa_raw = [wa_pair[:, 0, :], wa_pair[:, 1, :], wa_last[:]]
-        wa_bf = [kept([P, PACK, P, PACK], BF16, "wa_bf%d" % a) for a in range(LAST)]
+        wa_bf = [placed([P, PACK, P, PACK], BF16, "wa_bf0", CACHE4_AT), kept([P, PACK, P, PACK], BF16, "wa_bf1")]
         wa_bf += [placed([P, PACK, P, PACK], BF16, "wa_bf2", WA2_BF_AT)]
         wa_codes = [kept([P, R], U32, "wa_codes%d" % a) for a in range(PASSES)]
         wa_planes = [kept([P, R], U8, "wa_plane%d" % a) for a in range(PASSES)]
@@ -112,7 +112,6 @@ def tile_list_adapted_key_cache_kernel(
         nc.scalar.dma_start(vector_rows[0:HEADS, :], bk.rearrange("(c p) -> c p", p=P))
         nc.sync.dma_start(wa_pair[:], wa_rows[:, 0:LAST, :])
         make_identity(nc, ident[:])
-        nc.gpsimd.memset(cache[4][:], 0.0)
 
         def gather_words(a, j0, j1, dst):
             nc.vector.tensor_copy(dst.bitcast(U32), table[a][:].bitcast(U32).indirect(idx[:, j0 // 16 : j1 // 16]))
@@ -190,6 +189,7 @@ def tile_list_adapted_key_cache_kernel(
             )
 
         prepare_wa(0)
+        nc.vector.memset(cache[4][:], 0.0)
         prepare_wa(1)
         v_planes[LAST, HALF] = placed([P, HALF // 4], I32, "v_plane_late", WA01_AT + 11 * KB // 2)
         nc.vector.memset(v_planes[LAST, HALF][:], 0)

@@ -30,11 +30,11 @@ KB = 1024
 
 CACHE3_AT = 0
 TABLE1_AT = 8 * KB
-WINDOW_AT = 24 * KB - 128
+WINDOW_AT = 24 * KB - 512
 WA2_AT = 24 * KB
 TABLE2_AT = 32 * KB
 TABLE0_AT = 48 * KB
-CACHE2_AT = 64 * KB - 128
+CACHE2_AT = 64 * KB - 512
 WA01_AT = 72 * KB
 GAIN1_AT = 88 * KB
 BIAS0_AT = 122 * KB
@@ -55,10 +55,10 @@ def tile_list_adapted_key_cache_kernel(
         psum = ctx.enter_context(tc.psum_pool(name="psum", bufs=1))
 
         def kept(shape, dtype, name):
-            return keep.tile(shape, dtype, name=name, align_bytes=64)
+            return keep.tile(shape, dtype, name=name, align_bytes=256)
 
         def placed(shape, dtype, name, at):
-            return stage.tile(shape, dtype, name=name, align_bytes=64, offset=at)
+            return stage.tile(shape, dtype, name=name, align_bytes=256 if at % 256 == 0 else 64, offset=at)
 
         def bank(shape, b):
             return psum.tile(shape, F32, name="bank%d" % b)
@@ -66,7 +66,7 @@ def tile_list_adapted_key_cache_kernel(
         idx = keep.tile([P, S // 16], U16, name="idx")
         idx2 = keep.tile([P, S // 16], U16, name="idx2")
         scale_rows = placed([P, T // 4], I32, "scale_rows", WINDOW_AT)
-        table = [placed([P, T], I32, "table%d" % a, at) for a, at in enumerate((TABLE0_AT - 64, TABLE1_AT - 64, TABLE2_AT))]
+        table = [placed([P, T], I32, "table%d" % a, at) for a, at in enumerate((TABLE0_AT - 256, TABLE1_AT - 256, TABLE2_AT))]
         picked_rows = kept([P, S // 4], I32, "picked_rows")
         v_planes = {(a, 0): kept([P, (S if a < LAST else HALF) // 4], I32, "v_plane%d" % a) for a in range(PASSES)}
         v_words = {(a, 0): kept([P, S], I32, "v_words%d" % a) for a in range(LAST)}

@@ -28,7 +28,6 @@ HEADS = N // P
 CACHES = 5
 KB = 1024
 
-CACHE3_AT = 0
 TABLE1_AT = 8 * KB
 WINDOW_AT = 24 * KB - 512
 WA2_AT = 24 * KB
@@ -40,7 +39,9 @@ GAIN1_AT = 88 * KB
 BIAS0_AT = 122 * KB
 PAIRS3_AT = 99 * KB
 PAIRS7_AT = 103 * KB
-CACHE4_AT = 107 * KB
+WA0_BF_AT = 107 * KB
+CACHE3_AT = TABLE0_AT + 512 - 8 * KB
+CACHE4_AT = TABLE0_AT + KB
 GAIN0_AT = 115 * KB
 WA2_BF_AT = 117 * KB
 
@@ -73,7 +74,7 @@ def tile_list_adapted_key_cache_kernel(
         wa_pair = placed([P, LAST, PACK * R], F32, "wa_pair", WA01_AT)
         wa_last = placed([P, PACK * R], F32, "wa_last", WA2_AT)
         wa_raw = [wa_pair[:, 0, :], wa_pair[:, 1, :], wa_last[:]]
-        wa_bf = [placed([P, PACK, P, PACK], BF16, "wa_bf0", CACHE4_AT), kept([P, PACK, P, PACK], BF16, "wa_bf1")]
+        wa_bf = [placed([P, PACK, P, PACK], BF16, "wa_bf0", WA0_BF_AT), kept([P, PACK, P, PACK], BF16, "wa_bf1")]
         wa_bf += [placed([P, PACK, P, PACK], BF16, "wa_bf2", WA2_BF_AT)]
         wa_codes = [kept([P, R], U32, "wa_codes%d" % a) for a in range(PASSES)]
         wa_planes = [kept([P, R], U8, "wa_plane%d" % a) for a in range(PASSES)]
@@ -87,7 +88,7 @@ def tile_list_adapted_key_cache_kernel(
         first_bias = placed([P, 32], F32, "first_bias", BIAS0_AT)
         ident = keep.tile([P, P], F32, name="ident")
         cache = [kept([P, T2], F32, "cache%d" % b) for b in range(2)]
-        cache += [placed([P, T2], F32, "cache%d" % b, at) for b, at in ((2, CACHE2_AT), (3, CACHE3_AT), (4, CACHE4_AT))]
+        cache += [placed([P, T2], F32, "cache2", CACHE2_AT)]
 
         nc.gpsimd.memset(scale_rows[:], 0)
         nc.gpsimd.memset(vector_rows[:], 0.0)
@@ -150,14 +151,14 @@ def tile_list_adapted_key_cache_kernel(
             for head in range(n0, n1):
                 w0_codes[head] = (codes, P * (head - n0) // 2)
 
-        load_wb(0, 1, TABLE0_AT + 10 * KB)
-        w0_planes = placed([P, PASSES, N // 4], I32, "w0_planes", TABLE0_AT + 6 * KB)
+        load_wb(0, 1, TABLE0_AT)
+        w0_planes = placed([P, PASSES, N // 4], I32, "w0_planes", TABLE0_AT + 21 * KB // 2)
         nc.vector.memset(w0_planes[:], 0)
         for r in range(4):
             rows = w0_scales[:, r:16:4, :].rearrange("a q n -> q a n").bitcast(I32)
             nc.sync.dma_start(w0_planes[r:P:32, :, :], rows)
-        load_w0(0, 2, TABLE0_AT + 4 * KB)
-        load_wb(1, 2, TABLE0_AT)
+        load_w0(0, 2, TABLE0_AT + 9 * KB)
+        load_wb(1, 2, TABLE0_AT + 4 * KB)
 
         turned = bank([P, P], 0)
         nc.tensor.transpose(turned[:], vector_rows[:], ident[:])
@@ -189,7 +190,6 @@ def tile_list_adapted_key_cache_kernel(
             )
 
         prepare_wa(0)
-        nc.vector.memset(cache[4][:], 0.0)
         prepare_wa(1)
         v_planes[LAST, HALF] = placed([P, HALF // 4], I32, "v_plane_late", WA01_AT + 11 * KB // 2)
         nc.vector.memset(v_planes[LAST, HALF][:], 0)
@@ -206,7 +206,6 @@ def tile_list_adapted_key_cache_kernel(
         load_w0(4, HEADS, TABLE1_AT)
         prepare_wa(LAST)
         load_wb(5, HEADS, WA2_AT + 2 * KB)
-        nc.vector.memset(cache[3][:], 0.0)
 
         def picked(a, j0, j1):
             lo = HALF if a == LAST and j0 >= HALF else 0
@@ -334,7 +333,7 @@ def tile_list_adapted_key_cache_kernel(
         quantize_h(0, QUARTER, h_first)
         v_words[LAST, HALF] = placed([P, HALF], I32, "v_late", GAIN1_AT)
         gather_words(LAST, HALF, S, v_words[LAST, HALF][:])
-        scaled_second = placed([P, PACK, QUARTER], F32, "scaled_second", TABLE0_AT + 10 * KB)
+        scaled_second = placed([P, PACK, QUARTER], F32, "scaled_second", TABLE0_AT)
 
         def scale_second(t, c0, c1, dst):
             nc.scalar.activation(dst, low_second[t // 2][:, t % 2, c0:c1], COPY, scale=lam_sb[:, t : t + 1])
@@ -344,7 +343,7 @@ def tile_list_adapted_key_cache_kernel(
         scale_second(PACK - 1, 0, P, scaled_second[:, PACK - 1, 0:P])
         round_wb(1, 2, wb_bf[1])
         quantize_wb(1, 2, wb_bf[1])
-        values = values_at(QUARTER, "values00", TABLE0_AT)
+        values = values_at(QUARTER, "values00", TABLE0_AT + 4 * KB)
         keys(0, 0, QUARTER, values[:], 0, first_bias[:, 0:1])
         scatter(0, values[:], 0, QUARTER)
         scaled_last = placed([P, P], F32, "scaled_last", BIAS0_AT - 448)
@@ -368,7 +367,7 @@ def tile_list_adapted_key_cache_kernel(
         values = values_at(QUARTER, "values20", PAIRS3_AT + KB // 2)
         keys(2, 0, QUARTER, values[:], 1)
         scatter(2, values[:], 0, QUARTER)
-        wb_bf[3] = placed([P, P, PACK], BF16, "wb_bf3", TABLE0_AT + 10 * KB)
+        wb_bf[3] = placed([P, P, PACK], BF16, "wb_bf3", TABLE0_AT)
         round_wb(3, 4, wb_bf[3])
         quantize_wb(3, 4, wb_bf[3])
         second_half_pass(LAST)
@@ -392,9 +391,12 @@ def tile_list_adapted_key_cache_kernel(
         scale_by_lam(2)
         scale_by_lam(3)
         second_quarter(1, 0)
-        wb_bf[4] = placed([P, P, PACK], BF16, "wb_bf4", TABLE0_AT + 10 * KB)
+        wb_bf[4] = placed([P, P, PACK], BF16, "wb_bf4", TABLE0_AT + 256)
         round_wb(4, 5, wb_bf[4])
         quantize_wb(4, 5, wb_bf[4])
+        for b, at in ((3, CACHE3_AT), (4, CACHE4_AT)):
+            cache.append(placed([P, T2], F32, "cache%d" % b, at))
+            nc.gpsimd.memset(cache[b][:], 0.0)
         scale_by_strength(4, late_slots(4), pairs[4], 4)
         second_quarter(2, 1)
         scale_by_strength(5, late_slots(5), pairs[5], 5)
@@ -413,7 +415,7 @@ def tile_list_adapted_key_cache_kernel(
         late_bf = placed([P, 3 * P, PACK], BF16, "wb_bf_late", PAIRS7_AT + KB // 2)
         round_wb(5, HEADS, late_bf)
         quantize_wb(5, HEADS, late_bf)
-        late_at = [TABLE1_AT + (7 + 2 * head) * KB for head in range(4)] + [TABLE0_AT]
+        late_at = [TABLE1_AT + (7 + 2 * head) * KB for head in range(4)] + [TABLE0_AT + 27 * KB // 2]
         for head, b in enumerate((4, 5, 6, 7, 3)):
             values = values_at(HALF, "values%d2" % head, late_at[head])
             keys(head, HALF, S, values[:], b)
@@ -421,7 +423,7 @@ def tile_list_adapted_key_cache_kernel(
             store(head)
         banks = (2, 0, 1, 4, 5, 6)
         for head in range(CACHES, HEADS):
-            values = values_at(S, "values%d" % head, TABLE2_AT + 4 * (head - CACHES) * KB)
+            values = values_at(S, "values%d" % head, (0, 4 * KB, TABLE2_AT)[head - CACHES])
             keys(head, 0, HALF, values[:, 0:HALF], banks[2 * (head - CACHES)])
             keys(head, HALF, S, values[:, HALF:S], banks[2 * (head - CACHES) + 1])
             scatter(head, values[:], 0, S)

@@ -76,8 +76,8 @@ def tile_list_adapted_key_cache_kernel(
         wa_raw = [wa_pair[:, 0, :], wa_pair[:, 1, :], wa_last[:]]
         wa_bf = [placed([P, PACK, P, PACK], BF16, "wa_bf0", WA0_BF_AT), kept([P, PACK, P, PACK], BF16, "wa_bf1")]
         wa_bf += [placed([P, PACK, P, PACK], BF16, "wa_bf2", WA2_BF_AT)]
-        wa_codes = [kept([P, R], U32, "wa_codes%d" % a) for a in range(PASSES)]
-        wa_planes = [kept([P, R], U8, "wa_plane%d" % a) for a in range(PASSES)]
+        wa_codes = [kept([P, R // 2 if a == 1 else R], U32, "wa_codes%d" % a) for a in range(PASSES)]
+        wa_planes = [kept([P, R // 2 if a == 1 else R], U8, "wa_plane%d" % a) for a in range(PASSES)]
         wb_codes = kept([P, N], U32, "wb_codes")
         gain = [placed([P, P, PACK], F32, "gain0", GAIN0_AT), placed([P, P, PACK], F32, "gain1", GAIN1_AT)]
         h_codes = kept([P, S], U32, "h_codes")
@@ -178,19 +178,28 @@ def tile_list_adapted_key_cache_kernel(
         for b in range(3):
             nc.vector.memset(cache[b][:], 0.0)
 
-        def prepare_wa(a):
+        wa_slot = {}
+
+        def round_wa(a):
             nc.scalar.copy(
                 wa_bf[a][:].rearrange("p t m j -> p m j t"),
                 wa_raw[a].rearrange("p (j m t) -> p m j t", j=PACK, t=PACK),
             )
-            nc.vector.quantize_mx(
-                out=wa_codes[a][:].bitcast(FP8X4),
-                scales=wa_planes[a][:],
-                in_=wa_bf[a][:].rearrange("p t m j -> p (t m j)"),
-            )
 
-        prepare_wa(0)
-        prepare_wa(1)
+        def quantize_wa(a, t0, t1, codes, plane):
+            nc.vector.quantize_mx(
+                out=codes.bitcast(FP8X4),
+                scales=plane,
+                in_=wa_bf[a][:, t0:t1, :, :].rearrange("p t m j -> p (t m j)"),
+            )
+            for t in range(t0, t1):
+                cols = slice((t - t0) * P, (t - t0 + 1) * P)
+                wa_slot[a, t] = (codes[:, cols], plane[:, cols])
+
+        round_wa(0)
+        quantize_wa(0, 0, PACK, wa_codes[0][:], wa_planes[0][:])
+        round_wa(1)
+        quantize_wa(1, 0, PACK // 2, wa_codes[1][:], wa_planes[1][:])
         v_planes[LAST, HALF] = placed([P, HALF // 4], I32, "v_plane_late", WA01_AT + 11 * KB // 2)
         nc.vector.memset(v_planes[LAST, HALF][:], 0)
         wgo_sb = placed([P, S], F32, "wgo_sb", WA01_AT)
@@ -204,8 +213,11 @@ def tile_list_adapted_key_cache_kernel(
             move_rows(LAST, q, HALF)
         gather_words(1, 0, S, v_words[1, 0][:])
         load_w0(4, HEADS, TABLE1_AT)
-        prepare_wa(LAST)
-        load_wb(5, HEADS, WA2_AT + 2 * KB)
+        round_wa(LAST)
+        held_codes = placed([P, R // 2], U32, "held_codes", WA2_AT + 2 * KB)
+        held_plane = placed([P, R // 2], U8, "held_plane", WA2_AT + 3 * KB)
+        quantize_wa(1, PACK // 2, PACK, held_codes[:], held_plane[:])
+        quantize_wa(LAST, 0, PACK, wa_codes[LAST][:], wa_planes[LAST][:])
 
         def picked(a, j0, j1):
             lo = HALF if a == LAST and j0 >= HALF else 0
@@ -216,8 +228,8 @@ def tile_list_adapted_key_cache_kernel(
             words, plane = picked(a, j0, j1)
             nc.tensor.matmul_mx(
                 out=dst,
-                lhsT=wa_codes[a][:, t * P : (t + 1) * P].bitcast(FP8X4),
-                lhsT_scale=wa_planes[a][:, t * P : (t + 1) * P],
+                lhsT=wa_slot[a, t][0].bitcast(FP8X4),
+                lhsT_scale=wa_slot[a, t][1],
                 rhs=words,
                 rhs_scale=plane,
                 start=start,
@@ -242,6 +254,7 @@ def tile_list_adapted_key_cache_kernel(
         for a in range(LAST):
             first_half_pass(a)
             second_half_pass(a)
+        load_wb(5, HEADS, WA2_AT + 2 * KB)
 
         def round_wb(n0, n1, wb_bf):
             nc.scalar.copy(

from contextlib import ExitStack

import concourse.mybir as mybir
from concourse.masks import make_identity

K, R, N, T, S, T2 = 1536, 512, 1024, 4096, 1024, 2048
FLOPS = 2 * S * (K * R + K * N + R * N)

F32 = mybir.dt.float32
BF16 = mybir.dt.bfloat16
I32 = mybir.dt.int32
U32 = mybir.dt.uint32
U16 = mybir.dt.uint16
U8 = mybir.dt.uint8
FP8X4 = mybir.dt.float8_e4m3fn_x4
FP4X4 = mybir.dt.float4_e2m1fn_x4
MULT = mybir.AluOpType.mult
IDENTITY = mybir.ActivationFunctionType.Identity
COPY = mybir.ActivationFunctionType.Copy

P = 128
PACK = 4
PASSES = K // (P * PACK)
LAST = PASSES - 1
HALF = S // 2
QUARTER = S // 4
HEADS = N // P
CACHES = 5
KB = 1024

TABLE1_AT = 8 * KB
WINDOW_AT = 24 * KB - 512
WA2_AT = 24 * KB
TABLE2_AT = 32 * KB
TABLE0_AT = 48 * KB
CACHE2_AT = 64 * KB - 512
WA01_AT = 72 * KB
GAIN1_AT = 88 * KB
BIAS0_AT = 122 * KB
PAIRS3_AT = 99 * KB
PAIRS7_AT = 103 * KB
WA0_BF_AT = 107 * KB
CACHE3_AT = TABLE0_AT + 512 - 8 * KB
CACHE4_AT = TABLE0_AT + KB
GAIN0_AT = 115 * KB
WA2_BF_AT = 117 * KB


def tile_list_adapted_key_cache_kernel(
    tc, tab_words, tab_scales, offs, w0_words, w0_scales, wa, lam, strength, wb, bk, wgo, offs2, out
):
    nc = tc.nc
    with ExitStack() as ctx:
        keep = ctx.enter_context(tc.tile_pool(name="keep", bufs=1))
        stage = ctx.enter_context(tc.tile_pool(name="stage", bufs=1))
        psum = ctx.enter_context(tc.psum_pool(name="psum", bufs=1))

        def kept(shape, dtype, name):
            return keep.tile(shape, dtype, name=name, align_bytes=256)

        def placed(shape, dtype, name, at):
            return stage.tile(shape, dtype, name=name, align_bytes=256 if at % 256 == 0 else 64, offset=at)

        def bank(shape, b):
            return psum.tile(shape, F32, name="bank%d" % b)

        idx = keep.tile([P, S // 16], U16, name="idx")
        idx2 = keep.tile([P, S // 16], U16, name="idx2")
        scale_rows = placed([P, T // 4], I32, "scale_rows", WINDOW_AT)
        table = [placed([P, T], I32, "table%d" % a, at) for a, at in enumerate((TABLE0_AT - 256, TABLE1_AT - 256, TABLE2_AT))]
        picked_rows = kept([P, S // 4], I32, "picked_rows")
        v_planes = {(a, 0): kept([P, (S if a < LAST else HALF) // 4], I32, "v_plane%d" % a) for a in range(PASSES)}
        v_words = {(a, 0): kept([P, S], I32, "v_words%d" % a) for a in range(LAST)}
        wa_pair = placed([P, LAST, PACK * R], F32, "wa_pair", WA01_AT)
        wa_last = placed([P, PACK * R], F32, "wa_last", WA2_AT)
        wa_raw = [wa_pair[:, 0, :], wa_pair[:, 1, :], wa_last[:]]
        wa_bf = [placed([P, PACK, P, PACK], BF16, "wa_bf0", WA0_BF_AT), kept([P, PACK, P, PACK], BF16, "wa_bf1")]
        wa_bf += [placed([P, PACK, P, PACK], BF16, "wa_bf2", WA2_BF_AT)]
        wa_codes = [kept([P, R // 2 if a == 1 else R], U32, "wa_codes%d" % a) for a in range(PASSES)]
        wa_planes = [kept([P, R // 2 if a == 1 else R], U8, "wa_plane%d" % a) for a in range(PASSES)]
        wb_codes = kept([P, N], U32, "wb_codes")
        gain = [placed([P, P, PACK], F32, "gain0", GAIN0_AT), placed([P, P, PACK], F32, "gain1", GAIN1_AT)]
        h_codes = kept([P, S], U32, "h_codes")
        h_plane = kept([P, S], U8, "h_plane")
        lam_sb = keep.tile([P, PACK], F32, name="lam_sb")
        vector_rows = keep.tile([P, P], F32, name="vector_rows")
        vector_cols = keep.tile([P, HEADS + S // P], F32, name="vector_cols")
        first_bias = placed([P, 32], F32, "first_bias", BIAS0_AT)
        ident = keep.tile([P, P], F32, name="ident")
        cache = [kept([P, T2], F32, "cache%d" % b) for b in range(2)]
        cache += [placed([P, T2], F32, "cache2", CACHE2_AT)]

        nc.gpsimd.memset(scale_rows[:], 0)
        nc.gpsimd.memset(vector_rows[:], 0.0)
        for a in range(PASSES):
            nc.vector.memset(v_planes[a, 0][:], 0)

        def load_table(a, c0, c1):
            words = tab_words[a].rearrange("p t i -> p (t i)").bitcast(I32)
            nc.sync.dma_start(table[a][:, c0:c1], words[:, c0:c1])

        wa_rows = wa.rearrange("(a p j) c -> p a (j c)", p=P, j=PACK)
        load_table(0, 0, T // 4)
        nc.sync.dma_start(idx[:], offs)
        nc.sync.dma_start(lam_sb[:], lam.rearrange("(p t) -> p t", t=PACK))
        nc.sync.dma_start(idx2[:], offs2)
        load_table(0, T // 4, T // 2)
        all_rows = tab_scales.rearrange("a q n -> (a q) n").bitcast(I32)
        nc.sync.dma_start(scale_rows[0:P:4, :], all_rows[0:32, :])
        nc.sync.dma_start(scale_rows[6:P:8, :], all_rows[32:48, :])
        load_table(0, T // 2, T)
        nc.scalar.dma_start(vector_rows[HEADS : HEADS + S // P, :], strength.rearrange("(c p) -> c p", p=P))
        nc.scalar.dma_start(vector_rows[0:HEADS, :], bk.rearrange("(c p) -> c p", p=P))
        nc.sync.dma_start(wa_pair[:], wa_rows[:, 0:LAST, :])
        make_identity(nc, ident[:])

        def gather_words(a, j0, j1, dst):
            nc.vector.tensor_copy(dst.bitcast(U32), table[a][:].bitcast(U32).indirect(idx[:, j0 // 16 : j1 // 16]))

        def move_rows(a, q, j0=0):
            if a < LAST:
                rows = picked_rows[64 * a + 16 * q : 64 * a + 16 * q + 16 : 4, :]
            else:
                rows = picked_rows[32 * q + 6 : 32 * q + 32 : 8, j0 // 4 : (j0 + HALF) // 4]
            nc.sync.dma_start(v_planes[a, j0][32 * q : 32 * q + 4, :], rows)

        nc.vector.tensor_copy(picked_rows[:].bitcast(U8), scale_rows[:].bitcast(U8).indirect(idx[:]))
        gather_words(0, 0, S, v_words[0, 0][:])
        moves = [(a, q) for a in range(PASSES) for q in range(4)]
        for a, q in moves[:5]:
            move_rows(a, q)
        load_table(1, 0, T)
        for a, q in moves[5:8]:
            move_rows(a, q)
        nc.sync.dma_start(wa_last[:], wa_rows[:, LAST, :])
        load_table(LAST, 0, T)
        for a, q in moves[8:]:
            move_rows(a, q)

        wb_raw, w0_codes = {}, {}

        def load_wb(n0, n1, at):
            raw = placed([P, PACK, P * (n1 - n0)], F32, "wb_raw%d" % n0, at)
            nc.sync.dma_start(raw[:], wb[:, P * n0 : P * n1].rearrange("(p j) c -> p j c", j=PACK))
            wb_raw[n0] = raw

        def load_w0(n0, n1, at):
            codes = placed([P, PASSES, P * (n1 - n0) // 2], I32, "w0_codes%d" % n0, at)
            words = w0_words.rearrange("a p b -> p a b").bitcast(I32)
            nc.sync.dma_start(codes[:], words[:, :, P * n0 // 2 : P * n1 // 2])
            for head in range(n0, n1):
                w0_codes[head] = (codes, P * (head - n0) // 2)

        load_wb(0, 1, TABLE0_AT)
        w0_planes = placed([P, PASSES, N // 4], I32, "w0_planes", TABLE0_AT + 21 * KB // 2)
        nc.vector.memset(w0_planes[:], 0)
        for r in range(4):
            rows = w0_scales[:, r:16:4, :].rearrange("a q n -> q a n").bitcast(I32)
            nc.sync.dma_start(w0_planes[r:P:32, :, :], rows)
        load_w0(0, 2, TABLE0_AT + 9 * KB)
        load_wb(1, 2, TABLE0_AT + 4 * KB)

        turned = bank([P, P], 0)
        nc.tensor.transpose(turned[:], vector_rows[:], ident[:])
        nc.scalar.activation(vector_cols[:], turned[:, 0 : HEADS + S // P], COPY)
        nc.scalar.activation(first_bias[:, 0:1], turned[:, 0:1], COPY)
        spread = bank([P, QUARTER], 1)
        for c in range(2):
            column = vector_cols[:, HEADS + c : HEADS + c + 1]
            nc.tensor.transpose(spread[:, c * P : (c + 1) * P], column.to_broadcast([P, P]), ident[:])
        for c in range(2):
            nc.vector.tensor_tensor(
                gain[c][:],
                spread[:, c * P : (c + 1) * P].unsqueeze(2).broadcast_to([P, P, PACK]),
                lam_sb[:].unsqueeze(1).broadcast_to([P, P, PACK]),
                MULT,
            )
        for b in range(3):
            nc.vector.memset(cache[b][:], 0.0)

        wa_slot = {}

        def round_wa(a):
            nc.scalar.copy(
                wa_bf[a][:].rearrange("p t m j -> p m j t"),
                wa_raw[a].rearrange("p (j m t) -> p m j t", j=PACK, t=PACK),
            )

        def quantize_wa(a, t0, t1, codes, plane):
            nc.vector.quantize_mx(
                out=codes.bitcast(FP8X4),
                scales=plane,
                in_=wa_bf[a][:, t0:t1, :, :].rearrange("p t m j -> p (t m j)"),
            )
            for t in range(t0, t1):
                cols = slice((t - t0) * P, (t - t0 + 1) * P)
                wa_slot[a, t] = (codes[:, cols], plane[:, cols])

        round_wa(0)
        quantize_wa(0, 0, PACK, wa_codes[0][:], wa_planes[0][:])
        round_wa(1)
        quantize_wa(1, 0, PACK // 2, wa_codes[1][:], wa_planes[1][:])
        v_planes[LAST, HALF] = placed([P, HALF // 4], I32, "v_plane_late", WA01_AT + 11 * KB // 2)
        nc.vector.memset(v_planes[LAST, HALF][:], 0)
        wgo_sb = placed([P, S], F32, "wgo_sb", WA01_AT)
        nc.sync.dma_start(wgo_sb[:, 0:QUARTER], wgo[:, 0:QUARTER])
        load_wb(2, 3, WA01_AT + 10 * KB)
        load_w0(2, 4, WA01_AT + 4 * KB)
        load_wb(3, 4, WA01_AT + 6 * KB)
        nc.sync.dma_start(wgo_sb[:, QUARTER:S], wgo[:, QUARTER:S])
        load_wb(4, 5, WA01_AT + 8 * KB)
        for q in range(4):
            move_rows(LAST, q, HALF)
        gather_words(1, 0, S, v_words[1, 0][:])
        load_w0(4, HEADS, TABLE1_AT)
        round_wa(LAST)
        held_codes = placed([P, R // 2], U32, "held_codes", WA2_AT + 2 * KB)
        held_plane = placed([P, R // 2], U8, "held_plane", WA2_AT + 3 * KB)
        quantize_wa(1, PACK // 2, PACK, held_codes[:], held_plane[:])
        quantize_wa(LAST, 0, PACK, wa_codes[LAST][:], wa_planes[LAST][:])

        def picked(a, j0, j1):
            lo = HALF if a == LAST and j0 >= HALF else 0
            words = v_words[a, lo][:, j0 - lo : j1 - lo].bitcast(FP8X4)
            return words, v_planes[a, lo][:, (j0 - lo) // 4 : (j1 - lo) // 4].bitcast(U8)

        def low_product(dst, a, t, j0, j1, start, stop):
            words, plane = picked(a, j0, j1)
            nc.tensor.matmul_mx(
                out=dst,
                lhsT=wa_slot[a, t][0].bitcast(FP8X4),
                lhsT_scale=wa_slot[a, t][1],
                rhs=words,
                rhs_scale=plane,
                start=start,
                stop=stop,
            )

        low_chunk = [bank([P, PACK, P], c) for c in range(2)]
        low_second = [bank([P, 2, QUARTER], 2 + u) for u in range(2)]
        low_half = [bank([P, HALF], 4 + t) for t in range(PACK)]

        def first_half_pass(a):
            for c in range(2):
                for t in range(PACK):
                    low_product(low_chunk[c][:, t, :], a, t, c * P, (c + 1) * P, a == 0 and t == 0, a == LAST and t == PACK - 1)
            for t in range(PACK):
                low_product(low_second[t // 2][:, t % 2, :], a, t, QUARTER, HALF, a == 0 and t % 2 == 0, a == LAST and t % 2 == 1)

        def second_half_pass(a):
            for t in range(PACK):
                low_product(low_half[t][:], a, t, HALF, S, a == 0, a == LAST)

        for a in range(LAST):
            first_half_pass(a)
            second_half_pass(a)
        load_wb(5, HEADS, WA2_AT + 2 * KB)

        def round_wb(n0, n1, wb_bf):
            nc.scalar.copy(
                wb_bf[:].rearrange("p (c i) j -> p c j i", i=4),
                wb_raw[n0][:].rearrange("p j (c i) -> p c j i", i=4),
            )

        def quantize_wb(n0, n1, wb_bf):
            nc.vector.quantize_mx(
                out=wb_codes[:, n0 * P : n1 * P].bitcast(FP8X4),
                scales=wb_plane[:, n0 * P : n1 * P],
                in_=wb_bf[:].rearrange("p c j -> p (c j)"),
            )

        def quantize_h(j0, j1, rounded):
            nc.vector.quantize_mx(
                out=h_codes[:, j0:j1].bitcast(FP8X4),
                scales=h_plane[:, j0:j1],
                in_=rounded[:].rearrange("p j t -> p (j t)"),
            )

        def scale_by_strength(c, slots, pairs, b):
            by_entry = bank([P, PACK, P], b)
            for t in reversed(range(PACK)):
                nc.tensor.transpose(by_entry[:, t, :], slots[t], ident[:])
            col = HEADS + c
            nc.scalar.activation(
                pairs, by_entry[:].rearrange("p (u e) m -> p u m e", u=2), COPY, scale=vector_cols[:, col : col + 1]
            )

        def turn_back(pairs, dst, b):
            back = bank([P, len(pairs), 2, P], b)
            for i in range(len(pairs)):
                words = pairs[i].rearrange("p u m e -> p (u m e)").bitcast(F32)
                for u in range(2):
                    nc.tensor.transpose(back[:, i, u, :], words[:, u * P : (u + 1) * P], ident[:])
            words = dst.rearrange("p j t -> p (j t)").bitcast(F32)
            nc.scalar.copy(words.rearrange("p (i j u) -> p i j u", i=len(pairs), u=2), back[:].rearrange("p i u j -> p i j u"))

        def keys(head, j0, j1, dst, b, bias=None):
            codes, c0 = w0_codes[head]
            n0, n1 = head * P, (head + 1) * P
            y = bank([P, j1 - j0], b)
            for a in range(PASSES):
                words, plane = picked(a, j0, j1)
                nc.tensor.matmul_mx(
                    out=y[:],
                    lhsT=codes[:, a, c0 : c0 + P // 2].bitcast(U8).bitcast(FP4X4),
                    lhsT_scale=w0_planes[:, a, n0 // 4 : n1 // 4].bitcast(U8),
                    rhs=words,
                    rhs_scale=plane,
                    start=(a == 0),
                    stop=False,
                )
            nc.tensor.matmul_mx(
                out=y[:],
                lhsT=wb_codes[:, n0:n1].bitcast(FP8X4),
                lhsT_scale=wb_plane[:, n0:n1],
                rhs=h_codes[:, j0:j1].bitcast(FP8X4),
                rhs_scale=h_plane[:, j0:j1],
                start=False,
                stop=True,
            )
            nc.scalar.activation(dst, y[:], IDENTITY, bias=vector_cols[:, head : head + 1] if bias is None else bias)

        def scatter(head, values, j0, j1):
            window = cache[head % CACHES][:].indirect(idx2[:, j0 // 16 : j1 // 16])
            nc.vector.tensor_tensor(window, values, wgo_sb[:, j0:j1], MULT)

        def store(head):
            nc.sync.dma_start(out[head * P : (head + 1) * P, :], cache[head % CACHES][:])

        def values_at(width, name, at):
            return placed([P, width], F32, name, at)

        v_words[LAST, 0] = placed([P, HALF], I32, "v_first", WA2_BF_AT)
        wb_plane = placed([P, N], U8, "wb_plane", GAIN0_AT)
        gather_words(LAST, 0, QUARTER, v_words[LAST, 0][:, 0:QUARTER])
        gather_words(LAST, QUARTER, HALF, v_words[LAST, 0][:, QUARTER:HALF])
        first_half_pass(LAST)
        wb_bf = {head: placed([P, P, PACK], BF16, "wb_bf%d" % head, WA2_AT + head * KB) for head in range(2)}
        round_wb(0, 1, wb_bf[0])
        h_first = kept([P, QUARTER, PACK], BF16, "h_first")
        for c in range(2):
            nc.vector.tensor_tensor(
                h_first[:, c * P : (c + 1) * P, :], low_chunk[c][:].rearrange("p t j -> p j t"), gain[c][:], MULT
            )
        quantize_wb(0, 1, wb_bf[0])
        quantize_h(0, QUARTER, h_first)
        v_words[LAST, HALF] = placed([P, HALF], I32, "v_late", GAIN1_AT)
        gather_words(LAST, HALF, S, v_words[LAST, HALF][:])
        scaled_second = placed([P, PACK, QUARTER], F32, "scaled_second", TABLE0_AT)

        def scale_second(t, c0, c1, dst):
            nc.scalar.activation(dst, low_second[t // 2][:, t % 2, c0:c1], COPY, scale=lam_sb[:, t : t + 1])

        for t in range(PACK - 1):
            scale_second(t, 0, QUARTER, scaled_second[:, t, :])
        scale_second(PACK - 1, 0, P, scaled_second[:, PACK - 1, 0:P])
        round_wb(1, 2, wb_bf[1])
        quantize_wb(1, 2, wb_bf[1])
        values = values_at(QUARTER, "values00", TABLE0_AT + 4 * KB)
        keys(0, 0, QUARTER, values[:], 0, first_bias[:, 0:1])
        scatter(0, values[:], 0, QUARTER)
        scaled_last = placed([P, P], F32, "scaled_last", BIAS0_AT - 448)
        scale_second(PACK - 1, P, QUARTER, scaled_last[:])

        pairs = {c: kept([P, 2, P, 2], BF16, "pairs%d" % c)[:] for c in (2, 4, 5, 6)}
        pairs[3] = placed([P, 2, P, 2], BF16, "pairs3", PAIRS3_AT)[:]
        pairs[7] = placed([P, 2, P, 2], BF16, "pairs7", PAIRS7_AT)[:]
        wb_bf[2] = placed([P, P, PACK], BF16, "wb_bf2", BIAS0_AT + 64)
        round_wb(2, 3, wb_bf[2])
        quantize_wb(2, 3, wb_bf[2])
        scale_by_strength(2, [scaled_second[:, t, 0:P] for t in range(PACK)], pairs[2], 0)
        values = values_at(QUARTER, "values10", WA01_AT + 10 * KB)
        keys(1, 0, QUARTER, values[:], 1)
        scatter(1, values[:], 0, QUARTER)
        scale_by_strength(3, [scaled_second[:, t, P:QUARTER] for t in range(PACK - 1)] + [scaled_last[:]], pairs[3], 2)
        h_second = kept([P, QUARTER, PACK], BF16, "h_second")
        turn_back([pairs[2]], h_second[:, 0:P, :], 0)
        turn_back([pairs[3]], h_second[:, P:QUARTER, :], 2)
        quantize_h(QUARTER, HALF, h_second)
        values = values_at(QUARTER, "values20", PAIRS3_AT + KB // 2)
        keys(2, 0, QUARTER, values[:], 1)
        scatter(2, values[:], 0, QUARTER)
        wb_bf[3] = placed([P, P, PACK], BF16, "wb_bf3", TABLE0_AT)
        round_wb(3, 4, wb_bf[3])
        quantize_wb(3, 4, wb_bf[3])
        second_half_pass(LAST)

        scaled_half = placed([P, PACK, HALF], F32, "scaled_half", PAIRS3_AT - 15 * KB // 2)

        def scale_by_lam(t):
            nc.scalar.activation(scaled_half[:, t, :], low_half[t][:], COPY, scale=lam_sb[:, t : t + 1])

        def late_slots(c):
            return [scaled_half[:, t, (c - 4) * P : (c - 3) * P] for t in range(PACK)]

        def second_quarter(head, b):
            values = values_at(QUARTER, "values%d1" % head, TABLE1_AT + (4 + head) * KB)
            keys(head, QUARTER, HALF, values[:], b)
            scatter(head, values[:], QUARTER, HALF)

        scale_by_lam(0)
        scale_by_lam(1)
        second_quarter(0, 3)
        scale_by_lam(2)
        scale_by_lam(3)
        second_quarter(1, 0)
        wb_bf[4] = placed([P, P, PACK], BF16, "wb_bf4", TABLE0_AT + 256)
        round_wb(4, 5, wb_bf[4])
        quantize_wb(4, 5, wb_bf[4])
        for b, at in ((3, CACHE3_AT), (4, CACHE4_AT)):
            cache.append(placed([P, T2], F32, "cache%d" % b, at))
            nc.gpsimd.memset(cache[b][:], 0.0)
        scale_by_strength(4, late_slots(4), pairs[4], 4)
        second_quarter(2, 1)
        scale_by_strength(5, late_slots(5), pairs[5], 5)
        values = values_at(HALF, "values3", WA01_AT + 8 * KB)
        keys(3, 0, HALF, values[:], 2)
        scatter(3, values[:], 0, HALF)
        for c in (6, 7):
            scale_by_strength(c, late_slots(c), pairs[c], c)
        h_late = kept([P, HALF, PACK], BF16, "h_late")
        turn_back([pairs[4], pairs[5]], h_late[:, 0:QUARTER, :], 3)
        turn_back([pairs[6], pairs[7]], h_late[:, QUARTER:HALF, :], 0)
        quantize_h(HALF, S, h_late)
        values = values_at(HALF, "values4", PAIRS7_AT - 3 * KB // 2)
        keys(4, 0, HALF, values[:], 1)
        scatter(4, values[:], 0, HALF)
        late_bf = placed([P, 3 * P, PACK], BF16, "wb_bf_late", PAIRS7_AT + KB // 2)
        round_wb(5, HEADS, late_bf)
        quantize_wb(5, HEADS, late_bf)
        late_at = [TABLE1_AT + (7 + 2 * head) * KB for head in range(4)] + [TABLE0_AT + 27 * KB // 2]
        for head, b in enumerate((4, 5, 6, 7, 3)):
            values = values_at(HALF, "values%d2" % head, late_at[head])
            keys(head, HALF, S, values[:], b)
            scatter(head, values[:], HALF, S)
            store(head)
        banks = (2, 0, 1, 4, 5, 6)
        for head in range(CACHES, HEADS):
            values = values_at(S, "values%d" % head, (0, 4 * KB, TABLE2_AT)[head - CACHES])
            keys(head, 0, HALF, values[:, 0:HALF], banks[2 * (head - CACHES)])
            keys(head, HALF, S, values[:, HALF:S], banks[2 * (head - CACHES) + 1])
            scatter(head, values[:], 0, S)
            store(head)
